import numpy as np
import ml_dtypes


def mxq(x, axis, fmt="e4m3"):
    dtype, down = {"e4m3": (ml_dtypes.float8_e4m3fn, 7), "e5m2": (ml_dtypes.float8_e5m2, 14)}[fmt]
    v = np.moveaxis(np.asarray(x, np.float32).astype(ml_dtypes.bfloat16).astype(np.float64), axis, -1)
    blocks = v.reshape(v.shape[:-1] + (-1, 32))
    amax = np.abs(blocks).max(-1, keepdims=True)
    byte = np.maximum(np.where(amax > 0, np.frexp(amax)[1] - 1 + 127, 0) - down, 1)
    scale = np.exp2(byte - 127.0)
    codes = (blocks / scale).astype(np.float32).astype(dtype).astype(np.float64)
    return np.moveaxis((codes * scale).reshape(v.shape), -1, axis)


WIDE = False


def mx_kscale(k):
    if not WIDE:
        return np.ones(k)
    levels = np.array([10, -10, 5, -5, 0])
    if k % 512:
        return np.exp2(np.random.permutation(np.resize(levels, k // 32))).repeat(32)
    a = np.empty((k // 512, 16))
    for p in range(k // 512):
        a[p, :8] = np.random.permutation(np.resize(levels, 8))
        for g in range(8):
            far = levels[np.abs(levels - a[p, g]) >= 10]
            a[p, g + 8] = far[np.random.randint(len(far))]
    return np.exp2(a.ravel()).repeat(32)


def f64(x):
    return np.asarray(x).astype(np.float64)


def striped(idx):
    return np.tile(idx.reshape(-1, 16).T, (8, 1)).astype(np.uint16)


def unstriped(offs):
    return offs[:16].T.reshape(-1).astype(np.int64)


E2M1 = np.array([0.0, 0.5, 1.0, 1.5, 2.0, 3.0, 4.0, 6.0, -0.0, -0.5, -1.0, -1.5, -2.0, -3.0, -4.0, -6.0])


def pack_weight(w, fmt):
    k, n = w.shape
    w = f64(np.asarray(w, np.float32).astype(ml_dtypes.bfloat16)).reshape(k // 32, 32, n)
    amax = np.abs(w).max(1)
    if fmt == "e4m3":
        byte = np.frexp(amax)[1] - 1 + 127 - 7
    else:
        mant, ex = np.frexp(amax / 6.0)
        byte = np.where(mant > 0.5, ex, ex - 1) + 127
    byte = np.clip(np.where(amax > 0, byte, 1), 1, 254)
    scaled = (w * np.exp2(127.0 - byte)[:, None, :]).reshape(k, n).astype(np.float32)
    by_word = np.ascontiguousarray(scaled.reshape(k // 512, 128, 4, n).transpose(0, 1, 3, 2))
    if fmt == "e4m3":
        words = by_word.astype(ml_dtypes.float8_e4m3fn).view(np.uint8)
    else:
        c = by_word.astype(ml_dtypes.float4_e2m1fn).view(np.uint8) & 0xF
        words = (c[..., 0::2] | (c[..., 1::2] << 4)).reshape(k // 512, 128, 2 * n)
    return np.ascontiguousarray(words), np.ascontiguousarray(byte.astype(np.uint8).reshape(k // 512, 16, n))


def unpack_weight(words, scales, fmt):
    g, _, n = scales.shape
    words = np.ascontiguousarray(words).reshape(g, 128, n, -1)
    if fmt == "e4m3":
        vals = words.view(ml_dtypes.float8_e4m3fn).astype(np.float64)
    else:
        nib = np.empty((g, 128, n, 4), np.uint8)
        nib[..., 0::2] = words & 0xF
        nib[..., 1::2] = words >> 4
        vals = E2M1[nib]
    vals = vals * np.repeat(np.exp2(scales.astype(np.float64) - 127.0), 8, axis=1)[..., None]
    return vals.transpose(0, 1, 3, 2).reshape(g * 512, n)


def gelu(v):
    return 0.5 * v * (1.0 + np.tanh(np.sqrt(2.0 / np.pi) * (v + 0.044715 * v**3)))


def bf(x):
    return np.asarray(x, np.float32).astype(ml_dtypes.bfloat16)


def planes(Y):
    n, m = Y.shape
    b = f64(bf(Y)).reshape(n // 32, 32, m)
    amax = np.abs(b).max(1)
    byte = np.clip(np.where(amax > 0, np.frexp(amax)[1] - 1 + 127 - 7, 1), 1, 254)
    codes = (b * np.exp2(127.0 - byte)[:, None, :]).reshape(n, m).astype(np.float32).astype(ml_dtypes.float8_e4m3fn).view(np.uint8)
    words = codes.reshape(n // 512, 128, 4, m).transpose(0, 1, 3, 2)
    return np.ascontiguousarray(words), np.ascontiguousarray(byte.astype(np.uint8).reshape(n // 512, 16, m))


K, H, N, T, S, T2, PR = 1024, 512, 768, 4096, 1024, 2048, 128

def setup_inputs():
    n = np.random.standard_normal
    s = mx_kscale(K)[:, None]
    u = mx_kscale(H)[:, None]
    tab_words, tab_scales = pack_weight(n((K, T)) * s, "e4m3")
    w4_words, w4_scales = pack_weight(n((K, H)) / np.sqrt(K) / s, "e2m1")
    w8_words, w8_scales = pack_weight(n((H, N)) / np.sqrt(H) / u, "e4m3")
    return {
        "tab_words": tab_words, "tab_scales": tab_scales,
        "offs": striped(np.random.permutation(T)[:S]),
        "offs2": striped(np.random.permutation(T2)[:S]),
        "w1": (n((K, H)) / np.sqrt(K) / s * u.T).astype(np.float32),
        "w4_words": w4_words, "w4_scales": w4_scales,
        "bg": n(H).astype(np.float32),
        "page0": (n((H, T2)) * u).astype(np.float32),
        "wgs": np.exp(0.3 * n((PR, S))).astype(np.float32),
        "w8_words": w8_words, "w8_scales": w8_scales,
        "gain": np.exp(0.3 * n(N)).astype(np.float32),
    }

def reference(tab_words, tab_scales, offs, offs2, w1, w4_words, w4_scales, bg,
              page0, wgs, w8_words, w8_scales, gain):
    v = unpack_weight(tab_words, tab_scales, "e4m3")[:, unstriped(offs)]
    w4 = unpack_weight(w4_words, w4_scales, "e2m1")
    w8 = unpack_weight(w8_words, w8_scales, "e4m3")
    a = mxq(f64(w1), 0, "e4m3").T @ v
    b = (w4.T @ v) + f64(bg)[:, None]
    h = a / (1.0 + np.exp(-b))
    page = f64(page0).copy()
    page[:, unstriped(offs2)] = np.tile(f64(wgs), (H // PR, 1)) * h
    y = (w8.T @ mxq(page, 0, "e4m3")) * f64(gain)[:, None]
    words, scales = planes(page)
    return y, page, words, scales

@@ -1,0 +1,264 @@
+from contextlib import ExitStack
+
+import concourse.mybir as mybir
+
+K, H, N, T, S, T2 = 1024, 512, 768, 4096, 1024, 2048
+FLOPS = 2 * (2 * K * H * S + H * N * T2)
+
+F32 = mybir.dt.float32
+BF16 = mybir.dt.bfloat16
+I32 = mybir.dt.int32
+U32 = mybir.dt.uint32
+U16 = mybir.dt.uint16
+U8 = mybir.dt.uint8
+FP8X4 = mybir.dt.float8_e4m3fn_x4
+FP4X4 = mybir.dt.float4_e2m1fn_x4
+ACT = mybir.ActivationFunctionType
+MULT = mybir.AluOpType.mult
+
+P = 128
+PACK = 4
+PASSES = K // (P * PACK)
+BANK = 512
+HALVES = S // BANK
+QUADS = 4
+N_TILES = N // P
+CHUNKS = [(0, 256), (256, 256), (512, 512), (1024, 512), (1536, 512)]
+
+
+def tile_list_forked_prefix_page_kernel(
+    tc, tab_words, tab_scales, offs, offs2, w1, w4_words, w4_scales, bg,
+    page0, wgs, w8_words, w8_scales, gain, out_0, out_1, out_2, out_3,
+):
+    nc = tc.nc
+    with ExitStack() as ctx:
+        keep = ctx.enter_context(tc.tile_pool(name="keep", bufs=1))
+        ring = ctx.enter_context(tc.tile_pool(name="ring", bufs=3))
+        psum = ctx.enter_context(tc.psum_pool(name="psum", bufs=8))
+
+        def held(shape, dtype, name):
+            return keep.tile(shape, dtype, name=name, align_bytes=64)
+
+        pick = keep.tile([P, S // 16], U16, name="pick")
+        slot = keep.tile([P, S // 16], U16, name="slot")
+        tab_z = held([P, T], U8, "tab_z")
+        w4_z_raw = held([P, PASSES, H], U8, "w4_z_raw")
+        v_z = [held([P, S], U8, f"v_z{a}") for a in range(PASSES)]
+        w8_z = held([P, N], U8, "w8_z")
+        nc.vector.memset(w4_z_raw[:].bitcast(I32), 0)
+        nc.vector.memset(tab_z[32:64, :].bitcast(I32), 0)
+        nc.vector.memset(tab_z[64:P, :].bitcast(I32), 0)
+        for a in range(PASSES):
+            nc.vector.memset(v_z[a][:].bitcast(I32), 0)
+        nc.vector.memset(w8_z[:].bitcast(I32), 0)
+
+        def w1_rows(a):
+            return w1[512 * a : 512 * (a + 1), :].rearrange("(p j) c -> p j c", j=PACK)
+
+        nc.sync.dma_start(pick[:], offs)
+        nc.sync.dma_start(tab_z[0:32, :].bitcast(I32), tab_scales.rearrange("a q t -> (a q) t").bitcast(I32))
+        w1_raw0 = held([P, PACK, H], F32, "w1_raw0")
+        nc.sync.dma_start(w1_raw0[:], w1_rows(0))
+        tab_w = [held([P, T], U32, f"tab_w{a}") for a in range(PASSES)]
+
+        def load_table(a):
+            nc.sync.dma_start(tab_w[a][:].bitcast(I32), tab_words[a].rearrange("p t i -> p (t i)").bitcast(I32))
+
+        load_table(0)
+        w4_raw = held([P, PASSES, 2 * H], U8, "w4_raw")
+        nc.sync.dma_start(w4_raw[:].bitcast(I32), w4_words.rearrange("a p c -> p a c").bitcast(I32))
+        for q in range(QUADS):
+            nc.scalar.dma_start(
+                w4_z_raw[32 * q : 32 * q + 4].bitcast(I32),
+                w4_scales[:, 4 * q : 4 * q + 4, :].rearrange("a r c -> r a c").bitcast(I32),
+            )
+        bias = held([P, PACK], F32, "bias")
+        nc.gpsimd.dma_start(bias[:], bg.rearrange("(p t) -> p t", t=PACK))
+        load_table(1)
+        nc.sync.dma_start(slot[:], offs2)
+        w1_raw1 = [held([P, PACK, H // 2], F32, f"w1_raw1_{h}") for h in range(2)]
+        nc.sync.dma_start(w1_raw1[0][:], w1_rows(1)[:, :, 0 : H // 2])
+
+        v_z_rows = held([P, S], U8, "v_z_rows")
+        nc.vector.tensor_copy(v_z_rows[:], tab_z[:].indirect(pick[:]))
+        for a in range(PASSES):
+            for q in range(QUADS):
+                row = 16 * a + 4 * q
+                nc.gpsimd.dma_start(
+                    v_z[a][32 * q : 32 * q + 4, :].bitcast(I32), v_z_rows[row : row + 4, :].bitcast(I32)
+                )
+
+        nc.sync.dma_start(w1_raw1[1][:], w1_rows(1)[:, :, H // 2 : H])
+        page = [held([P, T2], F32, f"page{t}") for t in range(PACK)]
+        page_rows = page0.rearrange("(p t) c -> p t c", t=PACK)
+        wgs_rows = wgs.rearrange("(q t) j -> q t j", t=PACK)
+        wg_first = held([P, S], F32, "wg_first")
+        wg_rest = held([P, PACK - 1, S], F32, "wg_rest")
+        nc.sync.dma_start(page[0][:], page_rows[:, 0, :])
+        for q in range(QUADS):
+            nc.sync.dma_start(wg_first[32 * q : 32 * (q + 1), :], wgs_rows[:, 0, :])
+        nc.sync.dma_start(page[1][:], page_rows[:, 1, :])
+        for q in range(QUADS):
+            nc.sync.dma_start(wg_rest[32 * q : 32 * (q + 1)], wgs_rows[:, 1:PACK, :])
+        for t in range(2, PACK):
+            nc.sync.dma_start(page[t][:], page_rows[:, t, :])
+        w8_w = held([P, N], U32, "w8_w")
+        nc.sync.dma_start(w8_w[:].bitcast(I32), w8_words[0].rearrange("p c i -> p (c i)").bitcast(I32))
+        for q in range(QUADS):
+            nc.sync.dma_start(
+                w8_z[32 * q : 32 * q + 4, :].bitcast(I32), w8_scales[0, 4 * q : 4 * q + 4, :].bitcast(I32)
+            )
+        gains = held([P, N_TILES], F32, "gains")
+        with nc.allow_non_contiguous_dma(reason="one gain value a partition and output tile"):
+            nc.sync.dma_start(gains[:], gain.rearrange("(i p) -> p i", p=P))
+
+        w4_w = held([P, PASSES, 2 * H], U8, "w4_w")
+        w4_z = held([P, PASSES, H], U8, "w4_z")
+        nc.vector.tensor_copy(
+            w4_w[:].bitcast(U16).rearrange("p a (t m) -> p a t m", t=PACK),
+            w4_raw[:].bitcast(U16).rearrange("p a (m t) -> p a t m", t=PACK),
+        )
+        nc.vector.tensor_copy(
+            w4_z[:].rearrange("p a (t m) -> p a t m", t=PACK),
+            w4_z_raw[:].rearrange("p a (m t) -> p a t m", t=PACK),
+        )
+
+        w1_g = [held([P, PACK * H], BF16, f"w1_g{a}") for a in range(PASSES)]
+        w1_w = [held([P, H], U32, f"w1_w{a}") for a in range(PASSES)]
+        w1_z = [held([P, H], U8, f"w1_z{a}") for a in range(PASSES)]
+
+        def grouped(a):
+            return w1_g[a][:].rearrange("p (t m j) -> p m j t", t=PACK, j=PACK)
+
+        def columns(raw):
+            return raw[:].rearrange("p j (m t) -> p m j t", t=PACK)
+
+        def quantise_w1(a, c0, c1):
+            nc.vector.quantize_mx(
+                out=w1_w[a][:, c0:c1].bitcast(FP8X4), scales=w1_z[a][:, c0:c1],
+                in_=w1_g[a][:, PACK * c0 : PACK * c1],
+            )
+
+        nc.scalar.copy(grouped(0), columns(w1_raw0))
+        quantise_w1(0, 0, H)
+
+        v_w = [[held([P, BANK], U32, f"v_w{a}_{h}") for h in range(HALVES)] for a in range(PASSES)]
+
+        def list_half(lst, h):
+            return lst[:, 32 * h : 32 * (h + 1)]
+
+        for a in range(PASSES):
+            for h in range(HALVES):
+                nc.vector.tensor_copy(v_w[a][h][:], tab_w[a][:].indirect(list_half(pick, h)))
+
+        nc.scalar.copy(grouped(1)[:, 0:64], columns(w1_raw1[0]))
+        nc.vector.tensor_copy(grouped(1)[:, 64:128], columns(w1_raw1[1]))
+        quantise_w1(1, 0, 128)
+        quantise_w1(1, 128, 256)
+        quantise_w1(1, 256, 512)
+
+        def product(t, h, words, dtype, width, scales):
+            acc = psum.tile([P, BANK], F32, name="acc")
+            for a in range(PASSES):
+                nc.tensor.matmul_mx(
+                    out=acc[:],
+                    lhsT=words(a)[:, width * t : width * (t + 1)].bitcast(dtype),
+                    lhsT_scale=scales(a)[:, P * t : P * (t + 1)],
+                    rhs=v_w[a][h][:].bitcast(FP8X4),
+                    rhs_scale=v_z[a][:, BANK * h : BANK * (h + 1)],
+                    start=(a == 0), stop=(a == PASSES - 1),
+                )
+            return acc
+
+        def gate_of(t, h):
+            logit = product(t, h, lambda a: w4_w[:, a, :], FP4X4, 2 * P, lambda a: w4_z[:, a, :])
+            gate = held([P, BANK], F32, f"gate{t}_{h}")
+            nc.scalar.activation(gate[:], logit[:], ACT.Sigmoid, bias=bias[:, t : t + 1])
+            return gate
+
+        def value_of(t, h):
+            return product(t, h, lambda a: w1_w[a][:], FP8X4, P, lambda a: w1_z[a][:])
+
+        def gated(value, gate):
+            hid = ring.tile([P, BANK], F32, name="hid")
+            nc.vector.tensor_tensor(hid[:], value[:], gate[:], MULT)
+            return hid
+
+        def scatter(t, h, hid):
+            cols = slice(BANK * h, BANK * (h + 1))
+            weight = wg_first[:, cols] if t == 0 else wg_rest[:, t - 1, cols]
+            nc.vector.tensor_tensor(page[t][:].indirect(list_half(slot, h)), hid[:], weight, MULT)
+
+        page_g = [held([P, PACK * w], BF16, f"page_g{c0}") for c0, w in CHUNKS]
+        page_out = out_1.rearrange("(p t) c -> p t c", t=PACK)
+
+        def round_chunk(t, i):
+            c0, w = CHUNKS[i]
+            nc.scalar.copy(page_g[i][:].rearrange("p (m t) -> p t m", t=PACK)[:, t, :], page[t][:, c0 : c0 + w])
+
+        steps = [(t, h) for t in range(PACK) for h in range(HALVES)]
+        gates = [gate_of(*step) for step in steps[:2]]
+        values = [value_of(*step) for step in steps[:2]]
+        gates.extend(gate_of(*step) for step in steps[2:])
+        hid = gated(values[0], gates[0])
+        for s, (t, h) in enumerate(steps):
+            if s + 2 < len(steps):
+                values.append(value_of(*steps[s + 2]))
+            following = gated(values[s + 1], gates[s + 1]) if s + 1 < len(steps) else None
+            scatter(t, h, hid)
+            hid = following
+            if h == HALVES - 1:
+                nc.sync.dma_start(page_out[:, t, :], page[t][:])
+                if t < PACK - 1:
+                    for i in range(len(CHUNKS)):
+                        round_chunk(t, i)
+
+        page_w = held([P, T2], U32, "page_w")
+        page_z = held([P, T2], U8, "page_z")
+        y_rows = out_0.rearrange("(i p) c -> p i c", p=P)
+        codes_out = out_2[0].rearrange("p m t -> p (m t)").bitcast(I32)
+
+        def quantise_chunk(i):
+            c0, w = CHUNKS[i]
+            nc.vector.quantize_mx(
+                out=page_w[:, c0 : c0 + w].bitcast(FP8X4), scales=page_z[:, c0 : c0 + w], in_=page_g[i][:]
+            )
+
+        def multiply_chunk(i, on_scalar):
+            c0, w = CHUNKS[i]
+            for g in range(2):
+                y = ring.tile([P, 3, w], F32, name="y", bufs=6)
+                for e in range(3):
+                    n = 3 * g + e
+                    acc = psum.tile([P, BANK], F32, name="acc")
+                    nc.tensor.matmul_mx(
+                        out=acc[:, 0:w],
+                        lhsT=w8_w[:, P * n : P * (n + 1)].bitcast(FP8X4),
+                        lhsT_scale=w8_z[:, P * n : P * (n + 1)],
+                        rhs=page_w[:, c0 : c0 + w].bitcast(FP8X4),
+                        rhs_scale=page_z[:, c0 : c0 + w],
+                        start=True, stop=True,
+                    )
+                    if on_scalar(n):
+                        nc.scalar.activation(y[:, e, :], acc[:, 0:w], ACT.Copy, scale=gains[:, n : n + 1])
+                    else:
+                        nc.vector.tensor_scalar(y[:, e, :], acc[:, 0:w], gains[:, n : n + 1], None, MULT)
+                nc.sync.dma_start(y_rows[:, 3 * g : 3 * g + 3, c0 : c0 + w], y[:])
+
+        last = len(CHUNKS) - 1
+        round_chunk(PACK - 1, 0)
+        quantise_chunk(0)
+        for i in range(len(CHUNKS)):
+            if i < last:
+                round_chunk(PACK - 1, i + 1)
+            multiply_chunk(i, lambda n: i >= 3 and n % 3 != 2)
+            if i < last:
+                quantise_chunk(i + 1)
+            if i == 1:
+                nc.sync.dma_start(codes_out[:, 0:1024], page_w[:, 0:1024].bitcast(I32))
+            if i == last - 1:
+                nc.sync.dma_start(codes_out[:, 1024:T2], page_w[:, 1024:T2].bitcast(I32))
+                for q in range(QUADS):
+                    nc.sync.dma_start(
+                        out_3[0, 4 * q : 4 * q + 4, :].bitcast(I32), page_z[32 * q : 32 * q + 4, :].bitcast(I32)
+                    )

@@ -23,6 +23,7 @@ BANK = 512
 HALVES = S // BANK
 QUADS = 4
 N_TILES = N // P
+BANKS = 8
 CHUNKS = [(0, 256), (256, 256), (512, 512), (1024, 512), (1536, 512)]
 
 
@@ -34,14 +35,21 @@ def tile_list_forked_prefix_page_kernel(
     with ExitStack() as ctx:
         keep = ctx.enter_context(tc.tile_pool(name="keep", bufs=1))
         ring = ctx.enter_context(tc.tile_pool(name="ring", bufs=3))
-        psum = ctx.enter_context(tc.psum_pool(name="psum", bufs=8))
+        arena = ctx.enter_context(tc.tile_pool(name="arena", bufs=1))
+        psum = ctx.enter_context(tc.psum_pool(name="psum", bufs=1))
 
-        def held(shape, dtype, name):
-            return keep.tile(shape, dtype, name=name, align_bytes=64)
+        def held(shape, dtype, name, tag=None):
+            return keep.tile(shape, dtype, name=name, tag=tag or name, align_bytes=64)
+
+        def placed(shape, dtype, name, kib):
+            return arena.tile(shape, dtype, name=name, align_bytes=64, offset=int(1024 * kib))
+
+        def bank(b):
+            return psum.tile([P, BANK], F32, name=f"bank{b}")
 
         pick = keep.tile([P, S // 16], U16, name="pick")
         slot = keep.tile([P, S // 16], U16, name="slot")
-        tab_z = held([P, T], U8, "tab_z")
+        tab_z = placed([P, T], U8, "tab_z", 46)
         w4_z_raw = held([P, PASSES, H], U8, "w4_z_raw")
         v_z = [held([P, S], U8, f"v_z{a}") for a in range(PASSES)]
         w8_z = held([P, N], U8, "w8_z")
@@ -52,68 +60,81 @@ def tile_list_forked_prefix_page_kernel(
             nc.vector.memset(v_z[a][:].bitcast(I32), 0)
         nc.vector.memset(w8_z[:].bitcast(I32), 0)
 
+        warm = held([P, 2], F32, "warm")
+        nc.gpsimd.memset(warm[:, 0:1], 0.0)
+        nc.scalar.activation(warm[:, 1:2], warm[:, 0:1], ACT.Sigmoid)
+
         def w1_rows(a):
             return w1[512 * a : 512 * (a + 1), :].rearrange("(p j) c -> p j c", j=PACK)
 
+        def load_table(a, kib):
+            words = placed([P, T], U32, f"tab_w{a}", kib)
+            nc.sync.dma_start(words[:].bitcast(I32), tab_words[a].rearrange("p t i -> p (t i)").bitcast(I32))
+            return words
+
         nc.sync.dma_start(pick[:], offs)
         nc.sync.dma_start(tab_z[0:32, :].bitcast(I32), tab_scales.rearrange("a q t -> (a q) t").bitcast(I32))
+        tab_w = [load_table(0, 15)]
         w1_raw0 = held([P, PACK, H], F32, "w1_raw0")
         nc.sync.dma_start(w1_raw0[:], w1_rows(0))
-        tab_w = [held([P, T], U32, f"tab_w{a}") for a in range(PASSES)]
-
-        def load_table(a):
-            nc.sync.dma_start(tab_w[a][:].bitcast(I32), tab_words[a].rearrange("p t i -> p (t i)").bitcast(I32))
-
-        load_table(0)
         w4_raw = held([P, PASSES, 2 * H], U8, "w4_raw")
         nc.sync.dma_start(w4_raw[:].bitcast(I32), w4_words.rearrange("a p c -> p a c").bitcast(I32))
+        nc.sync.dma_start(slot[:], offs2)
         for q in range(QUADS):
-            nc.scalar.dma_start(
+            nc.gpsimd.dma_start(
                 w4_z_raw[32 * q : 32 * q + 4].bitcast(I32),
                 w4_scales[:, 4 * q : 4 * q + 4, :].rearrange("a r c -> r a c").bitcast(I32),
             )
-        bias = held([P, PACK], F32, "bias")
-        nc.gpsimd.dma_start(bias[:], bg.rearrange("(p t) -> p t", t=PACK))
-        load_table(1)
-        nc.sync.dma_start(slot[:], offs2)
-        w1_raw1 = [held([P, PACK, H // 2], F32, f"w1_raw1_{h}") for h in range(2)]
-        nc.sync.dma_start(w1_raw1[0][:], w1_rows(1)[:, :, 0 : H // 2])
+        for q in range(QUADS):
+            nc.gpsimd.dma_start(
+                w8_z[32 * q : 32 * q + 4, :].bitcast(I32), w8_scales[0, 4 * q : 4 * q + 4, :].bitcast(I32)
+            )
 
         v_z_rows = held([P, S], U8, "v_z_rows")
         nc.vector.tensor_copy(v_z_rows[:], tab_z[:].indirect(pick[:]))
-        for a in range(PASSES):
+
+        def place_scales(a):
             for q in range(QUADS):
                 row = 16 * a + 4 * q
-                nc.gpsimd.dma_start(
+                nc.sync.dma_start(
                     v_z[a][32 * q : 32 * q + 4, :].bitcast(I32), v_z_rows[row : row + 4, :].bitcast(I32)
                 )
 
-        nc.sync.dma_start(w1_raw1[1][:], w1_rows(1)[:, :, H // 2 : H])
-        page = [held([P, T2], F32, f"page{t}") for t in range(PACK)]
+        place_scales(0)
+        tab_w.append(load_table(1, 42))
+        place_scales(1)
+
+        v_w = [[held([P, BANK], U32, f"v_w{a}_{h}") for h in range(HALVES)] for a in range(PASSES)]
+
+        def list_half(lst, h):
+            return lst[:, 32 * h : 32 * (h + 1)]
+
+        def gather_words(a):
+            for h in range(HALVES):
+                nc.vector.tensor_copy(v_w[a][h][:], tab_w[a][:].indirect(list_half(pick, h)))
+
+        gather_words(0)
+
         page_rows = page0.rearrange("(p t) c -> p t c", t=PACK)
         wgs_rows = wgs.rearrange("(q t) j -> q t j", t=PACK)
-        wg_first = held([P, S], F32, "wg_first")
-        wg_rest = held([P, PACK - 1, S], F32, "wg_rest")
-        nc.sync.dma_start(page[0][:], page_rows[:, 0, :])
+
+        def load_page(t, kib):
+            rows = placed([P, T2], F32, f"page{t}", kib)
+            nc.sync.dma_start(rows[:], page_rows[:, t, :])
+            return rows
+
+        bias = placed([P, PACK], F32, "bias", 23)
+        nc.sync.dma_start(bias[:], bg.rearrange("(p t) -> p t", t=PACK))
+        w1_raw1 = [placed([P, PACK, H // 2], F32, f"w1_raw1_{h}", 12 + 4 * h) for h in range(2)]
+        for h in range(2):
+            nc.sync.dma_start(w1_raw1[h][:], w1_rows(1)[:, :, 256 * h : 256 * (h + 1)])
+        page = [load_page(0, 28)]
+        wg_first = placed([P, S], F32, "wg_first", 23.5)
         for q in range(QUADS):
             nc.sync.dma_start(wg_first[32 * q : 32 * (q + 1), :], wgs_rows[:, 0, :])
-        nc.sync.dma_start(page[1][:], page_rows[:, 1, :])
-        for q in range(QUADS):
-            nc.sync.dma_start(wg_rest[32 * q : 32 * (q + 1)], wgs_rows[:, 1:PACK, :])
-        for t in range(2, PACK):
-            nc.sync.dma_start(page[t][:], page_rows[:, t, :])
-        w8_w = held([P, N], U32, "w8_w")
-        nc.sync.dma_start(w8_w[:].bitcast(I32), w8_words[0].rearrange("p c i -> p (c i)").bitcast(I32))
-        for q in range(QUADS):
-            nc.sync.dma_start(
-                w8_z[32 * q : 32 * q + 4, :].bitcast(I32), w8_scales[0, 4 * q : 4 * q + 4, :].bitcast(I32)
-            )
-        gains = held([P, N_TILES], F32, "gains")
-        with nc.allow_non_contiguous_dma(reason="one gain value a partition and output tile"):
-            nc.sync.dma_start(gains[:], gain.rearrange("(i p) -> p i", p=P))
 
-        w4_w = held([P, PASSES, 2 * H], U8, "w4_w")
-        w4_z = held([P, PASSES, H], U8, "w4_z")
+        w4_w = placed([P, PASSES, 2 * H], U8, "w4_w", 20)
+        w4_z = placed([P, PASSES, H], U8, "w4_z", 22)
         nc.vector.tensor_copy(
             w4_w[:].bitcast(U16).rearrange("p a (t m) -> p a t m", t=PACK),
             w4_raw[:].bitcast(U16).rearrange("p a (m t) -> p a t m", t=PACK),
@@ -123,7 +144,7 @@ def tile_list_forked_prefix_page_kernel(
             w4_z_raw[:].rearrange("p a (m t) -> p a t m", t=PACK),
         )
 
-        w1_g = [held([P, PACK * H], BF16, f"w1_g{a}") for a in range(PASSES)]
+        w1_g = [placed([P, PACK * H], BF16, f"w1_g{a}", 72 - 4 * a) for a in range(PASSES)]
         w1_w = [held([P, H], U32, f"w1_w{a}") for a in range(PASSES)]
         w1_z = [held([P, H], U8, f"w1_z{a}") for a in range(PASSES)]
 
@@ -142,23 +163,22 @@ def tile_list_forked_prefix_page_kernel(
         nc.scalar.copy(grouped(0), columns(w1_raw0))
         quantise_w1(0, 0, H)
 
-        v_w = [[held([P, BANK], U32, f"v_w{a}_{h}") for h in range(HALVES)] for a in range(PASSES)]
-
-        def list_half(lst, h):
-            return lst[:, 32 * h : 32 * (h + 1)]
-
-        for a in range(PASSES):
-            for h in range(HALVES):
-                nc.vector.tensor_copy(v_w[a][h][:], tab_w[a][:].indirect(list_half(pick, h)))
+        gather_words(1)
+        page.append(load_page(1, 36))
+        wg_rest = placed([P, PACK - 1, S], F32, "wg_rest", 44)
+        for q in range(QUADS):
+            nc.sync.dma_start(wg_rest[32 * q : 32 * (q + 1)], wgs_rows[:, 1:PACK, :])
+        page.append(load_page(2, 56))
 
         nc.scalar.copy(grouped(1)[:, 0:64], columns(w1_raw1[0]))
         nc.vector.tensor_copy(grouped(1)[:, 64:128], columns(w1_raw1[1]))
         quantise_w1(1, 0, 128)
         quantise_w1(1, 128, 256)
         quantise_w1(1, 256, 512)
+        page.append(load_page(3, 64))
 
-        def product(t, h, words, dtype, width, scales):
-            acc = psum.tile([P, BANK], F32, name="acc")
+        def product(b, t, h, words, dtype, width, scales):
+            acc = bank(b)
             for a in range(PASSES):
                 nc.tensor.matmul_mx(
                     out=acc[:],
@@ -170,53 +190,84 @@ def tile_list_forked_prefix_page_kernel(
                 )
             return acc
 
-        def gate_of(t, h):
-            logit = product(t, h, lambda a: w4_w[:, a, :], FP4X4, 2 * P, lambda a: w4_z[:, a, :])
-            gate = held([P, BANK], F32, f"gate{t}_{h}")
-            nc.scalar.activation(gate[:], logit[:], ACT.Sigmoid, bias=bias[:, t : t + 1])
+        gate_rows = placed([P, PACK * S], F32, "gate_rows", 0)
+
+        def gate_of(b, t, h):
+            logit = product(b, t, h, lambda a: w4_w[:, a, :], FP4X4, 2 * P, lambda a: w4_z[:, a, :])
+            gate = gate_rows[:, S * t + BANK * h : S * t + BANK * (h + 1)]
+            nc.scalar.activation(gate, logit[:], ACT.Sigmoid, bias=bias[:, t : t + 1])
             return gate
 
-        def value_of(t, h):
-            return product(t, h, lambda a: w1_w[a][:], FP8X4, P, lambda a: w1_z[a][:])
+        def value_of(b, t, h):
+            return product(b, t, h, lambda a: w1_w[a][:], FP8X4, P, lambda a: w1_z[a][:])
 
-        def gated(value, gate):
-            hid = ring.tile([P, BANK], F32, name="hid")
-            nc.vector.tensor_tensor(hid[:], value[:], gate[:], MULT)
-            return hid
+        hid = [held([P, S], F32, f"hid{t}") for t in range(PACK)]
 
-        def scatter(t, h, hid):
-            cols = slice(BANK * h, BANK * (h + 1))
-            weight = wg_first[:, cols] if t == 0 else wg_rest[:, t - 1, cols]
-            nc.vector.tensor_tensor(page[t][:].indirect(list_half(slot, h)), hid[:], weight, MULT)
+        def gated(s):
+            t, h = steps[s]
+            nc.vector.tensor_tensor(hid[t][:, BANK * h : BANK * (h + 1)], values[s][:], gates[s], MULT)
+
+        def scatter(t, j0, j1):
+            weight = wg_first[:, j0:j1] if t == 0 else wg_rest[:, t - 1, j0:j1]
+            nc.vector.tensor_tensor(page[t][:].indirect(slot[:, j0 // 16 : j1 // 16]), hid[t][:, j0:j1], weight, MULT)
 
         page_g = [held([P, PACK * w], BF16, f"page_g{c0}") for c0, w in CHUNKS]
         page_out = out_1.rearrange("(p t) c -> p t c", t=PACK)
 
-        def round_chunk(t, i):
-            c0, w = CHUNKS[i]
-            nc.scalar.copy(page_g[i][:].rearrange("p (m t) -> p t m", t=PACK)[:, t, :], page[t][:, c0 : c0 + w])
+        def slots(i):
+            return page_g[i][:].rearrange("p (m t) -> p m t", t=PACK)
+
+        def round_early(t):
+            for i, (c0, w) in enumerate(CHUNKS):
+                rows = page[t][:, c0 : c0 + w]
+                if t == PACK - 2:
+                    nc.scalar.copy(slots(i)[:, :, t:PACK], rows.unsqueeze(2).to_broadcast([P, w, 2]))
+                else:
+                    nc.scalar.copy(slots(i)[:, :, t], rows)
 
         steps = [(t, h) for t in range(PACK) for h in range(HALVES)]
-        gates = [gate_of(*step) for step in steps[:2]]
-        values = [value_of(*step) for step in steps[:2]]
-        gates.extend(gate_of(*step) for step in steps[2:])
-        hid = gated(values[0], gates[0])
-        for s, (t, h) in enumerate(steps):
-            if s + 2 < len(steps):
-                values.append(value_of(*steps[s + 2]))
-            following = gated(values[s + 1], gates[s + 1]) if s + 1 < len(steps) else None
-            scatter(t, h, hid)
-            hid = following
-            if h == HALVES - 1:
-                nc.sync.dma_start(page_out[:, t, :], page[t][:])
-                if t < PACK - 1:
-                    for i in range(len(CHUNKS)):
-                        round_chunk(t, i)
+        gates = [gate_of(s, *steps[s]) for s in range(6)]
+        values = [value_of(6 + s, *steps[s]) for s in range(2)]
+        values.extend(value_of(s - 2, *steps[s]) for s in range(2, 6))
+        gates.extend(gate_of(s - 2, *steps[s]) for s in range(6, 8))
+
+        def finish(t):
+            nc.sync.dma_start(page_out[:, t, :], page[t][:])
+            if t < PACK - 1:
+                round_early(t)
+
+        gated(0)
+        gated(1)
+        values.extend(value_of(s, *steps[s]) for s in range(6, 8))
+        scatter(0, 0, BANK)
+        gated(2)
+        scatter(0, BANK, S)
+        finish(0)
+        gated(3)
+        gated(4)
+        w8_w = held([P, N], U32, "w8_w", "v_w0_0")
+        nc.sync.dma_start(w8_w[:].bitcast(I32), w8_words[0].rearrange("p c i -> p (c i)").bitcast(I32))
+        gains = held([P, N_TILES], F32, "gains", "v_w0_1")
+        with nc.allow_non_contiguous_dma(reason="one gain value a partition and output tile"):
+            nc.sync.dma_start(gains[:], gain.rearrange("(i p) -> p i", p=P))
+        scatter(1, 0, S)
+        finish(1)
+        gated(5)
+        gated(6)
+        gated(7)
+        scatter(2, 0, S)
+        finish(2)
+        scatter(3, 0, S)
+        finish(3)
 
         page_w = held([P, T2], U32, "page_w")
         page_z = held([P, T2], U8, "page_z")
         y_rows = out_0.rearrange("(i p) c -> p i c", p=P)
         codes_out = out_2[0].rearrange("p m t -> p (m t)").bitcast(I32)
+
+        def round_last(i):
+            c0, w = CHUNKS[i]
+            nc.vector.tensor_copy(slots(i)[:, :, PACK - 1], page[PACK - 1][:, c0 : c0 + w])
 
         def quantise_chunk(i):
             c0, w = CHUNKS[i]
@@ -224,13 +275,16 @@ def tile_list_forked_prefix_page_kernel(
                 out=page_w[:, c0 : c0 + w].bitcast(FP8X4), scales=page_z[:, c0 : c0 + w], in_=page_g[i][:]
             )
 
-        def multiply_chunk(i, on_scalar):
+        def store_codes(c0, c1):
+            nc.sync.dma_start(codes_out[:, c0:c1], page_w[:, c0:c1].bitcast(I32))
+
+        def multiply_chunk(i):
             c0, w = CHUNKS[i]
-            for g in range(2):
-                y = ring.tile([P, 3, w], F32, name="y", bufs=6)
-                for e in range(3):
-                    n = 3 * g + e
-                    acc = psum.tile([P, BANK], F32, name="acc")
+            group = 2 if w < BANK else 3
+            for n0 in range(0, N_TILES, group):
+                y = ring.tile([P, group, w], F32, name="y", bufs=6)
+                for n in range(n0, n0 + group):
+                    acc = bank((N_TILES * i + n) % BANKS)
                     nc.tensor.matmul_mx(
                         out=acc[:, 0:w],
                         lhsT=w8_w[:, P * n : P * (n + 1)].bitcast(FP8X4),
@@ -239,26 +293,24 @@ def tile_list_forked_prefix_page_kernel(
                         rhs_scale=page_z[:, c0 : c0 + w],
                         start=True, stop=True,
                     )
-                    if on_scalar(n):
-                        nc.scalar.activation(y[:, e, :], acc[:, 0:w], ACT.Copy, scale=gains[:, n : n + 1])
+                    if w < BANK or n % 2 == 0:
+                        nc.scalar.activation(y[:, n - n0, :], acc[:, 0:w], ACT.Copy, scale=gains[:, n : n + 1])
                     else:
-                        nc.vector.tensor_scalar(y[:, e, :], acc[:, 0:w], gains[:, n : n + 1], None, MULT)
-                nc.sync.dma_start(y_rows[:, 3 * g : 3 * g + 3, c0 : c0 + w], y[:])
+                        nc.vector.tensor_scalar(y[:, n - n0, :], acc[:, 0:w], gains[:, n : n + 1], None, MULT)
+                nc.sync.dma_start(y_rows[:, n0 : n0 + group, c0 : c0 + w], y[:])
 
-        last = len(CHUNKS) - 1
-        round_chunk(PACK - 1, 0)
-        quantise_chunk(0)
+        round_last(0)
         for i in range(len(CHUNKS)):
-            if i < last:
-                round_chunk(PACK - 1, i + 1)
-            multiply_chunk(i, lambda n: i >= 3 and n % 3 != 2)
-            if i < last:
-                quantise_chunk(i + 1)
-            if i == 1:
-                nc.sync.dma_start(codes_out[:, 0:1024], page_w[:, 0:1024].bitcast(I32))
-            if i == last - 1:
-                nc.sync.dma_start(codes_out[:, 1024:T2], page_w[:, 1024:T2].bitcast(I32))
-                for q in range(QUADS):
-                    nc.sync.dma_start(
-                        out_3[0, 4 * q : 4 * q + 4, :].bitcast(I32), page_z[32 * q : 32 * q + 4, :].bitcast(I32)
-                    )
+            if i + 1 < len(CHUNKS):
+                round_last(i + 1)
+            quantise_chunk(i)
+        multiply_chunk(0)
+        store_codes(0, 1024)
+        multiply_chunk(1)
+        store_codes(1024, T2)
+        for q in range(QUADS):
+            nc.sync.dma_start(
+                out_3[0, 4 * q : 4 * q + 4, :].bitcast(I32), page_z[32 * q : 32 * q + 4, :].bitcast(I32)
+            )
+        for i in range(2, len(CHUNKS)):
+            multiply_chunk(i)

@@ -130,7 +130,7 @@ def tile_list_forked_prefix_page_kernel(
             nc.sync.dma_start(w1_raw1[h][:], w1_rows(1)[:, :, 256 * h : 256 * (h + 1)])
         page = [load_page(0, 28)]
         wg_first = placed([P, S], F32, "wg_first", 23.5)
-        for q in range(QUADS):
+        for q in (0, 2, 1, 3):
             nc.sync.dma_start(wg_first[32 * q : 32 * (q + 1), :], wgs_rows[:, 0, :])
 
         w4_w = placed([P, PASSES, 2 * H], U8, "w4_w", 20)
@@ -149,10 +149,10 @@ def tile_list_forked_prefix_page_kernel(
         w1_z = [held([P, H], U8, f"w1_z{a}") for a in range(PASSES)]
 
         def grouped(a):
-            return w1_g[a][:].rearrange("p (t m j) -> p m j t", t=PACK, j=PACK)
+            return w1_g[a][:].rearrange("p (t m j) -> p t m j", t=PACK, j=PACK)
 
         def columns(raw):
-            return raw[:].rearrange("p j (m t) -> p m j t", t=PACK)
+            return raw[:].rearrange("p j (m t) -> p t m j", t=PACK)
 
         def quantise_w1(a, c0, c1):
             nc.vector.quantize_mx(
@@ -166,12 +166,12 @@ def tile_list_forked_prefix_page_kernel(
         gather_words(1)
         page.append(load_page(1, 36))
         wg_rest = placed([P, PACK - 1, S], F32, "wg_rest", 44)
-        for q in range(QUADS):
+        for q in (0, 2, 1, 3):
             nc.sync.dma_start(wg_rest[32 * q : 32 * (q + 1)], wgs_rows[:, 1:PACK, :])
         page.append(load_page(2, 56))
 
-        nc.scalar.copy(grouped(1)[:, 0:64], columns(w1_raw1[0]))
-        nc.vector.tensor_copy(grouped(1)[:, 64:128], columns(w1_raw1[1]))
+        nc.scalar.copy(grouped(1)[:, :, 0:64], columns(w1_raw1[0]))
+        nc.vector.tensor_copy(grouped(1)[:, :, 64:128], columns(w1_raw1[1]))
         quantise_w1(1, 0, 128)
         quantise_w1(1, 128, 256)
         quantise_w1(1, 256, 512)
@@ -278,39 +278,50 @@ def tile_list_forked_prefix_page_kernel(
         def store_codes(c0, c1):
             nc.sync.dma_start(codes_out[:, c0:c1], page_w[:, c0:c1].bitcast(I32))
 
-        def multiply_chunk(i):
+        def multiply(step, i, n, y, on_scalar):
             c0, w = CHUNKS[i]
-            group = 2 if w < BANK else 3
-            for n0 in range(0, N_TILES, group):
-                y = ring.tile([P, group, w], F32, name="y", bufs=6)
-                for n in range(n0, n0 + group):
-                    acc = bank((N_TILES * i + n) % BANKS)
-                    nc.tensor.matmul_mx(
-                        out=acc[:, 0:w],
-                        lhsT=w8_w[:, P * n : P * (n + 1)].bitcast(FP8X4),
-                        lhsT_scale=w8_z[:, P * n : P * (n + 1)],
-                        rhs=page_w[:, c0 : c0 + w].bitcast(FP8X4),
-                        rhs_scale=page_z[:, c0 : c0 + w],
-                        start=True, stop=True,
-                    )
-                    if w < BANK or n % 2 == 0:
-                        nc.scalar.activation(y[:, n - n0, :], acc[:, 0:w], ACT.Copy, scale=gains[:, n : n + 1])
-                    else:
-                        nc.vector.tensor_scalar(y[:, n - n0, :], acc[:, 0:w], gains[:, n : n + 1], None, MULT)
-                nc.sync.dma_start(y_rows[:, n0 : n0 + group, c0 : c0 + w], y[:])
+            acc = bank(step % BANKS)
+            nc.tensor.matmul_mx(
+                out=acc[:, 0:w],
+                lhsT=w8_w[:, P * n : P * (n + 1)].bitcast(FP8X4),
+                lhsT_scale=w8_z[:, P * n : P * (n + 1)],
+                rhs=page_w[:, c0 : c0 + w].bitcast(FP8X4),
+                rhs_scale=page_z[:, c0 : c0 + w],
+                start=True, stop=True,
+            )
+            if on_scalar:
+                nc.scalar.activation(y, acc[:, 0:w], ACT.Copy, scale=gains[:, n : n + 1])
+            else:
+                nc.vector.tensor_scalar(y, acc[:, 0:w], gains[:, n : n + 1], None, MULT)
+
+        def narrow_chunk(i):
+            c0, w = CHUNKS[i]
+            for n0 in range(0, N_TILES, 2):
+                y = ring.tile([P, 2, w], F32, name="y_narrow", bufs=6)
+                for n in range(n0, n0 + 2):
+                    multiply(N_TILES * i + n, i, n, y[:, n - n0, :], True)
+                nc.sync.dma_start(y_rows[:, n0 : n0 + 2, c0 : c0 + w], y[:])
+
+        def wide_rows(n):
+            y = ring.tile([P, T2 - BANK], F32, name="y_wide", bufs=6)
+            for i in range(2, len(CHUNKS)):
+                c0, w = CHUNKS[i]
+                step = 2 * N_TILES + 3 * n + i - 2
+                multiply(step, i, n, y[:, c0 - BANK : c0 - BANK + w], step % 2 == 0)
+            nc.sync.dma_start(y_rows[:, n, BANK:T2], y[:])
 
         round_last(0)
         for i in range(len(CHUNKS)):
             if i + 1 < len(CHUNKS):
                 round_last(i + 1)
             quantise_chunk(i)
-        multiply_chunk(0)
+        narrow_chunk(0)
         store_codes(0, 1024)
-        multiply_chunk(1)
+        narrow_chunk(1)
         store_codes(1024, T2)
         for q in range(QUADS):
             nc.sync.dma_start(
                 out_3[0, 4 * q : 4 * q + 4, :].bitcast(I32), page_z[32 * q : 32 * q + 4, :].bitcast(I32)
             )
-        for i in range(2, len(CHUNKS)):
-            multiply_chunk(i)
+        for n in range(N_TILES):
+            wide_rows(n)

@@ -214,16 +214,11 @@ def tile_list_forked_prefix_page_kernel(
         page_g = [held([P, PACK * w], BF16, f"page_g{c0}") for c0, w in CHUNKS]
         page_out = out_1.rearrange("(p t) c -> p t c", t=PACK)
 
-        def slots(i):
-            return page_g[i][:].rearrange("p (m t) -> p m t", t=PACK)
+        page_b = [held([P, PACK, w], BF16, f"page_b{c0}") for c0, w in CHUNKS]
 
-        def round_early(t):
+        def round_slice(t):
             for i, (c0, w) in enumerate(CHUNKS):
-                rows = page[t][:, c0 : c0 + w]
-                if t == PACK - 2:
-                    nc.scalar.copy(slots(i)[:, :, t:PACK], rows.unsqueeze(2).to_broadcast([P, w, 2]))
-                else:
-                    nc.scalar.copy(slots(i)[:, :, t], rows)
+                nc.scalar.copy(page_b[i][:, t, :], page[t][:, c0 : c0 + w])
 
         steps = [(t, h) for t in range(PACK) for h in range(HALVES)]
         gates = [gate_of(s, *steps[s]) for s in range(6)]
@@ -233,8 +228,7 @@ def tile_list_forked_prefix_page_kernel(
 
         def finish(t):
             nc.sync.dma_start(page_out[:, t, :], page[t][:])
-            if t < PACK - 1:
-                round_early(t)
+            round_slice(t)
 
         gated(0)
         gated(1)
@@ -265,9 +259,10 @@ def tile_list_forked_prefix_page_kernel(
         y_rows = out_0.rearrange("(i p) c -> p i c", p=P)
         codes_out = out_2[0].rearrange("p m t -> p (m t)").bitcast(I32)
 
-        def round_last(i):
-            c0, w = CHUNKS[i]
-            nc.vector.tensor_copy(slots(i)[:, :, PACK - 1], page[PACK - 1][:, c0 : c0 + w])
+        def weave(i):
+            nc.vector.tensor_copy(
+                page_g[i][:].rearrange("p (m t) -> p m t", t=PACK), page_b[i][:].rearrange("p t m -> p m t")
+            )
 
         def quantise_chunk(i):
             c0, w = CHUNKS[i]
@@ -294,31 +289,29 @@ def tile_list_forked_prefix_page_kernel(
             else:
                 nc.vector.tensor_scalar(y, acc[:, 0:w], gains[:, n : n + 1], None, MULT)
 
-        def narrow_chunk(i):
+        def chunk_rows(i, group):
             c0, w = CHUNKS[i]
-            for n0 in range(0, N_TILES, 2):
-                y = ring.tile([P, 2, w], F32, name="y_narrow", bufs=6)
-                for n in range(n0, n0 + 2):
+            for n0 in range(0, N_TILES, group):
+                y = ring.tile([P, group, w], F32, name=f"y{w}", bufs=6 if w < BANK else 3)
+                for n in range(n0, n0 + group):
                     multiply(N_TILES * i + n, i, n, y[:, n - n0, :], True)
-                nc.sync.dma_start(y_rows[:, n0 : n0 + 2, c0 : c0 + w], y[:])
+                nc.sync.dma_start(y_rows[:, n0 : n0 + group, c0 : c0 + w], y[:])
 
         def wide_rows(n):
-            y = ring.tile([P, T2 - BANK], F32, name="y_wide", bufs=6)
-            for i in range(2, len(CHUNKS)):
-                c0, w = CHUNKS[i]
-                step = 2 * N_TILES + 3 * n + i - 2
-                multiply(step, i, n, y[:, c0 - BANK : c0 - BANK + w], step % 2 == 0)
-            nc.sync.dma_start(y_rows[:, n, BANK:T2], y[:])
+            y = ring.tile([P, T2 // 2], F32, name="y_wide", bufs=6)
+            for e in range(2):
+                multiply(3 * N_TILES + 2 * n + e, 3 + e, n, y[:, BANK * e : BANK * (e + 1)], (n + e) % 3 == 0)
+            nc.sync.dma_start(y_rows[:, n, T2 // 2 : T2], y[:])
 
-        round_last(0)
         for i in range(len(CHUNKS)):
-            if i + 1 < len(CHUNKS):
-                round_last(i + 1)
+            weave(i)
             quantise_chunk(i)
-        narrow_chunk(0)
-        store_codes(0, 1024)
-        narrow_chunk(1)
-        store_codes(1024, T2)
+        store_codes(0, BANK)
+        chunk_rows(0, 2)
+        chunk_rows(1, 2)
+        store_codes(BANK, 3 * BANK)
+        chunk_rows(2, 2)
+        store_codes(3 * BANK, T2)
         for q in range(QUADS):
             nc.sync.dma_start(
                 out_3[0, 4 * q : 4 * q + 4, :].bitcast(I32), page_z[32 * q : 32 * q + 4, :].bitcast(I32)

@@ -18,13 +18,36 @@ MULT = mybir.AluOpType.mult
 
 P = 128
 PACK = 4
-PASSES = K // (P * PACK)
+K_PASS = P * PACK
+PASSES = K // K_PASS
 BANK = 512
-HALVES = S // BANK
-QUADS = 4
-N_TILES = N // P
 BANKS = 8
+HALVES = S // BANK
+QUAD = 32
+QUADS = P // QUAD
+Z_ROWS = 4
+LIST_ROWS = 16
+N_TILES = N // P
+
+QUAD_ORDER = (0, 2, 1, 3)
+
 CHUNKS = [(0, 256), (256, 256), (512, 512), (1024, 512), (1536, 512)]
+SOLO_CHUNKS = 3
+PAIR = 2
+VECTOR_TILES = 4
+
+KIB = 1024
+AT_GATES = 0
+AT_W1_HALVES = (12 * KIB, 16 * KIB)
+AT_TABLE = (15 * KIB, 42 * KIB)
+AT_W4_W = 20 * KIB
+AT_W4_Z = 22 * KIB
+AT_BIAS = 23 * KIB
+AT_WG_FIRST = 23 * KIB + 512
+AT_PAGE = (28 * KIB, 36 * KIB, 56 * KIB, 64 * KIB)
+AT_WG_REST = 44 * KIB
+AT_TAB_Z = 46 * KIB
+AT_W1_BF16 = (72 * KIB, 68 * KIB)
 
 
 def tile_list_forked_prefix_page_kernel(
@@ -34,47 +57,57 @@ def tile_list_forked_prefix_page_kernel(
     nc = tc.nc
     with ExitStack() as ctx:
         keep = ctx.enter_context(tc.tile_pool(name="keep", bufs=1))
-        ring = ctx.enter_context(tc.tile_pool(name="ring", bufs=3))
+        ring = ctx.enter_context(tc.tile_pool(name="ring", bufs=1))
         arena = ctx.enter_context(tc.tile_pool(name="arena", bufs=1))
         psum = ctx.enter_context(tc.psum_pool(name="psum", bufs=1))
 
         def held(shape, dtype, name, tag=None):
             return keep.tile(shape, dtype, name=name, tag=tag or name, align_bytes=64)
 
-        def placed(shape, dtype, name, kib):
-            return arena.tile(shape, dtype, name=name, align_bytes=64, offset=int(1024 * kib))
+        def placed(shape, dtype, name, at):
+            return arena.tile(shape, dtype, name=name, align_bytes=64, offset=at)
 
         def bank(b):
             return psum.tile([P, BANK], F32, name=f"bank{b}")
 
-        pick = keep.tile([P, S // 16], U16, name="pick")
-        slot = keep.tile([P, S // 16], U16, name="slot")
-        tab_z = placed([P, T], U8, "tab_z", 46)
+        def quadrant(q):
+            return slice(QUAD * q, QUAD * (q + 1))
+
+        def z_partitions(q):
+            return slice(QUAD * q, QUAD * q + Z_ROWS)
+
+        def z_rows(q):
+            return slice(Z_ROWS * q, Z_ROWS * (q + 1))
+
+        def half(h):
+            return slice(BANK * h, BANK * (h + 1))
+
+        pick = keep.tile([P, S // LIST_ROWS], U16, name="pick")
+        slot = keep.tile([P, S // LIST_ROWS], U16, name="slot")
+        tab_z = placed([P, T], U8, "tab_z", AT_TAB_Z)
         w4_z_raw = held([P, PASSES, H], U8, "w4_z_raw")
         v_z = [held([P, S], U8, f"v_z{a}") for a in range(PASSES)]
-        w8_z = held([P, N], U8, "w8_z")
-        nc.vector.memset(w4_z_raw[:].bitcast(I32), 0)
-        nc.vector.memset(tab_z[32:64, :].bitcast(I32), 0)
-        nc.vector.memset(tab_z[64:P, :].bitcast(I32), 0)
+
+        nc.gpsimd.memset(w4_z_raw[:].bitcast(I32), 0)
+        warm = held([P, 2], F32, "warm")
+        nc.vector.memset(warm[:, 0:1], 0.0)
+        nc.scalar.activation(warm[:, 1:2], warm[:, 0:1], ACT.Sigmoid)
+        nc.vector.memset(tab_z[QUAD : 2 * QUAD, :].bitcast(I32), 0)
+        nc.vector.memset(tab_z[2 * QUAD : P, :].bitcast(I32), 0)
         for a in range(PASSES):
             nc.vector.memset(v_z[a][:].bitcast(I32), 0)
-        nc.vector.memset(w8_z[:].bitcast(I32), 0)
-
-        warm = held([P, 2], F32, "warm")
-        nc.gpsimd.memset(warm[:, 0:1], 0.0)
-        nc.scalar.activation(warm[:, 1:2], warm[:, 0:1], ACT.Sigmoid)
 
         def w1_rows(a):
-            return w1[512 * a : 512 * (a + 1), :].rearrange("(p j) c -> p j c", j=PACK)
+            return w1[K_PASS * a : K_PASS * (a + 1), :].rearrange("(p j) c -> p j c", j=PACK)
 
-        def load_table(a, kib):
-            words = placed([P, T], U32, f"tab_w{a}", kib)
+        def load_table(a):
+            words = placed([P, T], U32, f"tab_w{a}", AT_TABLE[a])
             nc.sync.dma_start(words[:].bitcast(I32), tab_words[a].rearrange("p t i -> p (t i)").bitcast(I32))
             return words
 
         nc.sync.dma_start(pick[:], offs)
-        nc.sync.dma_start(tab_z[0:32, :].bitcast(I32), tab_scales.rearrange("a q t -> (a q) t").bitcast(I32))
-        tab_w = [load_table(0, 15)]
+        nc.sync.dma_start(tab_z[0:QUAD, :].bitcast(I32), tab_scales.rearrange("a q t -> (a q) t").bitcast(I32))
+        tab_w = [load_table(0)]
         w1_raw0 = held([P, PACK, H], F32, "w1_raw0")
         nc.sync.dma_start(w1_raw0[:], w1_rows(0))
         w4_raw = held([P, PASSES, 2 * H], U8, "w4_raw")
@@ -82,12 +115,8 @@ def tile_list_forked_prefix_page_kernel(
         nc.sync.dma_start(slot[:], offs2)
         for q in range(QUADS):
             nc.gpsimd.dma_start(
-                w4_z_raw[32 * q : 32 * q + 4].bitcast(I32),
-                w4_scales[:, 4 * q : 4 * q + 4, :].rearrange("a r c -> r a c").bitcast(I32),
-            )
-        for q in range(QUADS):
-            nc.gpsimd.dma_start(
-                w8_z[32 * q : 32 * q + 4, :].bitcast(I32), w8_scales[0, 4 * q : 4 * q + 4, :].bitcast(I32)
+                w4_z_raw[z_partitions(q)].bitcast(I32),
+                w4_scales[:, z_rows(q), :].rearrange("a r c -> r a c").bitcast(I32),
             )
 
         v_z_rows = held([P, S], U8, "v_z_rows")
@@ -95,46 +124,48 @@ def tile_list_forked_prefix_page_kernel(
 
         def place_scales(a):
             for q in range(QUADS):
-                row = 16 * a + 4 * q
+                row = Z_ROWS * (QUADS * a + q)
                 nc.sync.dma_start(
-                    v_z[a][32 * q : 32 * q + 4, :].bitcast(I32), v_z_rows[row : row + 4, :].bitcast(I32)
+                    v_z[a][z_partitions(q), :].bitcast(I32), v_z_rows[row : row + Z_ROWS, :].bitcast(I32)
                 )
 
         place_scales(0)
-        tab_w.append(load_table(1, 42))
+        tab_w.append(load_table(1))
         place_scales(1)
 
         v_w = [[held([P, BANK], U32, f"v_w{a}_{h}") for h in range(HALVES)] for a in range(PASSES)]
 
-        def list_half(lst, h):
-            return lst[:, 32 * h : 32 * (h + 1)]
+        def entries(lst, j0, j1):
+            return lst[:, j0 // LIST_ROWS : j1 // LIST_ROWS]
 
         def gather_words(a):
             for h in range(HALVES):
-                nc.vector.tensor_copy(v_w[a][h][:], tab_w[a][:].indirect(list_half(pick, h)))
+                picked = tab_w[a][:].indirect(entries(pick, BANK * h, BANK * (h + 1)))
+                nc.vector.tensor_copy(v_w[a][h][:], picked)
 
         gather_words(0)
 
         page_rows = page0.rearrange("(p t) c -> p t c", t=PACK)
         wgs_rows = wgs.rearrange("(q t) j -> q t j", t=PACK)
 
-        def load_page(t, kib):
-            rows = placed([P, T2], F32, f"page{t}", kib)
+        def load_page(t):
+            rows = placed([P, T2], F32, f"page{t}", AT_PAGE[t])
             nc.sync.dma_start(rows[:], page_rows[:, t, :])
             return rows
 
-        bias = placed([P, PACK], F32, "bias", 23)
+        bias = placed([P, PACK], F32, "bias", AT_BIAS)
         nc.sync.dma_start(bias[:], bg.rearrange("(p t) -> p t", t=PACK))
-        w1_raw1 = [placed([P, PACK, H // 2], F32, f"w1_raw1_{h}", 12 + 4 * h) for h in range(2)]
-        for h in range(2):
-            nc.sync.dma_start(w1_raw1[h][:], w1_rows(1)[:, :, 256 * h : 256 * (h + 1)])
-        page = [load_page(0, 28)]
-        wg_first = placed([P, S], F32, "wg_first", 23.5)
-        for q in (0, 2, 1, 3):
-            nc.sync.dma_start(wg_first[32 * q : 32 * (q + 1), :], wgs_rows[:, 0, :])
+        w1_raw1 = [placed([P, PACK, H // 2], F32, f"w1_raw1_{u}", AT_W1_HALVES[u]) for u in range(2)]
+        for u in range(2):
+            nc.sync.dma_start(w1_raw1[u][:], w1_rows(1)[:, :, H // 2 * u : H // 2 * (u + 1)])
+        page = [load_page(0)]
+        wg_first = placed([P, S], F32, "wg_first", AT_WG_FIRST)
+        for h in range(HALVES):
+            for q in QUAD_ORDER:
+                nc.sync.dma_start(wg_first[quadrant(q), half(h)], wgs_rows[:, 0, half(h)])
 
-        w4_w = placed([P, PASSES, 2 * H], U8, "w4_w", 20)
-        w4_z = placed([P, PASSES, H], U8, "w4_z", 22)
+        w4_w = placed([P, PASSES, 2 * H], U8, "w4_w", AT_W4_W)
+        w4_z = placed([P, PASSES, H], U8, "w4_z", AT_W4_Z)
         nc.vector.tensor_copy(
             w4_w[:].bitcast(U16).rearrange("p a (t m) -> p a t m", t=PACK),
             w4_raw[:].bitcast(U16).rearrange("p a (m t) -> p a t m", t=PACK),
@@ -144,40 +175,49 @@ def tile_list_forked_prefix_page_kernel(
             w4_z_raw[:].rearrange("p a (m t) -> p a t m", t=PACK),
         )
 
-        w1_g = [placed([P, PACK * H], BF16, f"w1_g{a}", 72 - 4 * a) for a in range(PASSES)]
+        w1_b = [placed([P, PACK * H], BF16, f"w1_b{a}", AT_W1_BF16[a]) for a in range(PASSES)]
         w1_w = [held([P, H], U32, f"w1_w{a}") for a in range(PASSES)]
         w1_z = [held([P, H], U8, f"w1_z{a}") for a in range(PASSES)]
 
-        def grouped(a):
-            return w1_g[a][:].rearrange("p (t m j) -> p t m j", t=PACK, j=PACK)
+        def rounded(a):
+            return w1_b[a][:].rearrange("p (t m j) -> p t m j", t=PACK, j=PACK)
 
         def columns(raw):
             return raw[:].rearrange("p j (m t) -> p t m j", t=PACK)
 
-        def quantise_w1(a, c0, c1):
+        def quantise_w1(a, t0, t1):
             nc.vector.quantize_mx(
-                out=w1_w[a][:, c0:c1].bitcast(FP8X4), scales=w1_z[a][:, c0:c1],
-                in_=w1_g[a][:, PACK * c0 : PACK * c1],
+                out=w1_w[a][:, P * t0 : P * t1].bitcast(FP8X4),
+                scales=w1_z[a][:, P * t0 : P * t1],
+                in_=w1_b[a][:, K_PASS * t0 : K_PASS * t1],
             )
 
-        nc.scalar.copy(grouped(0), columns(w1_raw0))
-        quantise_w1(0, 0, H)
+        nc.scalar.copy(rounded(0), columns(w1_raw0))
+        quantise_w1(0, 0, PACK)
 
         gather_words(1)
-        page.append(load_page(1, 36))
-        wg_rest = placed([P, PACK - 1, S], F32, "wg_rest", 44)
-        for q in (0, 2, 1, 3):
-            nc.sync.dma_start(wg_rest[32 * q : 32 * (q + 1)], wgs_rows[:, 1:PACK, :])
-        page.append(load_page(2, 56))
+        page.append(load_page(1))
+        wg_rest = placed([P, PACK - 1, S], F32, "wg_rest", AT_WG_REST)
+        for q in QUAD_ORDER:
+            nc.sync.dma_start(wg_rest[quadrant(q), 0, :], wgs_rows[:, 1, :])
+        page.append(load_page(2))
+        for q in QUAD_ORDER:
+            nc.sync.dma_start(wg_rest[quadrant(q), 1 : PACK - 1, :], wgs_rows[:, 2:PACK, :])
 
-        nc.scalar.copy(grouped(1)[:, :, 0:64], columns(w1_raw1[0]))
-        nc.vector.tensor_copy(grouped(1)[:, :, 64:128], columns(w1_raw1[1]))
-        quantise_w1(1, 0, 128)
-        quantise_w1(1, 128, 256)
-        quantise_w1(1, 256, 512)
-        page.append(load_page(3, 64))
+        low, high = slice(0, P // 2), slice(P // 2, P)
+        nc.scalar.copy(rounded(1)[:, 0, low], columns(w1_raw1[0])[:, 0])
+        nc.scalar.copy(rounded(1)[:, 1:PACK, low], columns(w1_raw1[0])[:, 1:PACK])
+        nc.vector.tensor_copy(rounded(1)[:, 0, high], columns(w1_raw1[1])[:, 0])
+        quantise_w1(1, 0, 1)
+        nc.vector.tensor_copy(rounded(1)[:, 1:PACK, high], columns(w1_raw1[1])[:, 1:PACK])
+        quantise_w1(1, 1, 2)
+        quantise_w1(1, 2, PACK)
+        page.append(load_page(3))
 
-        def product(b, t, h, words, dtype, width, scales):
+        steps = [(t, h) for t in range(PACK) for h in range(HALVES)]
+
+        def product(b, s, words, dtype, width, scales):
+            t, h = steps[s]
             acc = bank(b)
             for a in range(PASSES):
                 nc.tensor.matmul_mx(
@@ -185,65 +225,68 @@ def tile_list_forked_prefix_page_kernel(
                     lhsT=words(a)[:, width * t : width * (t + 1)].bitcast(dtype),
                     lhsT_scale=scales(a)[:, P * t : P * (t + 1)],
                     rhs=v_w[a][h][:].bitcast(FP8X4),
-                    rhs_scale=v_z[a][:, BANK * h : BANK * (h + 1)],
+                    rhs_scale=v_z[a][:, half(h)],
                     start=(a == 0), stop=(a == PASSES - 1),
                 )
             return acc
 
-        gate_rows = placed([P, PACK * S], F32, "gate_rows", 0)
+        gate_rows = placed([P, PACK * S], F32, "gate_rows", AT_GATES)
 
-        def gate_of(b, t, h):
-            logit = product(b, t, h, lambda a: w4_w[:, a, :], FP4X4, 2 * P, lambda a: w4_z[:, a, :])
-            gate = gate_rows[:, S * t + BANK * h : S * t + BANK * (h + 1)]
+        def gate_of(b, s):
+            logit = product(b, s, lambda a: w4_w[:, a, :], FP4X4, 2 * P, lambda a: w4_z[:, a, :])
+            t = steps[s][0]
+            gate = gate_rows[:, BANK * s : BANK * (s + 1)]
             nc.scalar.activation(gate, logit[:], ACT.Sigmoid, bias=bias[:, t : t + 1])
             return gate
 
-        def value_of(b, t, h):
-            return product(b, t, h, lambda a: w1_w[a][:], FP8X4, P, lambda a: w1_z[a][:])
+        def value_of(b, s):
+            return product(b, s, lambda a: w1_w[a][:], FP8X4, P, lambda a: w1_z[a][:])
 
         hid = [held([P, S], F32, f"hid{t}") for t in range(PACK)]
 
         def gated(s):
             t, h = steps[s]
-            nc.vector.tensor_tensor(hid[t][:, BANK * h : BANK * (h + 1)], values[s][:], gates[s], MULT)
+            nc.vector.tensor_tensor(hid[t][:, half(h)], values[s][:], gates[s], MULT)
 
         def scatter(t, j0, j1):
             weight = wg_first[:, j0:j1] if t == 0 else wg_rest[:, t - 1, j0:j1]
-            nc.vector.tensor_tensor(page[t][:].indirect(slot[:, j0 // 16 : j1 // 16]), hid[t][:, j0:j1], weight, MULT)
+            nc.vector.tensor_tensor(page[t][:].indirect(entries(slot, j0, j1)), hid[t][:, j0:j1], weight, MULT)
 
         page_g = [held([P, PACK * w], BF16, f"page_g{c0}") for c0, w in CHUNKS]
         page_out = out_1.rearrange("(p t) c -> p t c", t=PACK)
-
         page_b = [held([P, PACK, w], BF16, f"page_b{c0}") for c0, w in CHUNKS]
-
-        def round_slice(t):
-            for i, (c0, w) in enumerate(CHUNKS):
-                nc.scalar.copy(page_b[i][:, t, :], page[t][:, c0 : c0 + w])
-
-        steps = [(t, h) for t in range(PACK) for h in range(HALVES)]
-        gates = [gate_of(s, *steps[s]) for s in range(6)]
-        values = [value_of(6 + s, *steps[s]) for s in range(2)]
-        values.extend(value_of(s - 2, *steps[s]) for s in range(2, 6))
-        gates.extend(gate_of(s - 2, *steps[s]) for s in range(6, 8))
 
         def finish(t):
             nc.sync.dma_start(page_out[:, t, :], page[t][:])
-            round_slice(t)
+            for i, (c0, w) in enumerate(CHUNKS):
+                nc.scalar.copy(page_b[i][:, t, :], page[t][:, c0 : c0 + w])
+
+        early = BANKS - HALVES
+        gates = [gate_of(s, s) for s in range(early)]
+        values = [value_of(early + s, s) for s in range(HALVES)]
+        values.extend(value_of(s - HALVES, s) for s in range(HALVES, early))
+        gates.extend(gate_of(s - HALVES, s) for s in range(early, BANKS))
 
         gated(0)
-        gated(1)
-        values.extend(value_of(s, *steps[s]) for s in range(6, 8))
         scatter(0, 0, BANK)
+        gated(1)
+        values.extend(value_of(s, s) for s in range(early, BANKS))
         gated(2)
         scatter(0, BANK, S)
         finish(0)
         gated(3)
         gated(4)
+
         w8_w = held([P, N], U32, "w8_w", "v_w0_0")
         nc.sync.dma_start(w8_w[:].bitcast(I32), w8_words[0].rearrange("p c i -> p (c i)").bitcast(I32))
         gains = held([P, N_TILES], F32, "gains", "v_w0_1")
         with nc.allow_non_contiguous_dma(reason="one gain value a partition and output tile"):
             nc.sync.dma_start(gains[:], gain.rearrange("(i p) -> p i", p=P))
+        w8_z = held([P, N], U8, "w8_z", "v_w1_0")
+        nc.gpsimd.memset(w8_z[:].bitcast(I32), 0)
+        for q in range(QUADS):
+            nc.sync.dma_start(w8_z[z_partitions(q), :].bitcast(I32), w8_scales[0, z_rows(q), :].bitcast(I32))
+
         scatter(1, 0, S)
         finish(1)
         gated(5)
@@ -259,13 +302,11 @@ def tile_list_forked_prefix_page_kernel(
         y_rows = out_0.rearrange("(i p) c -> p i c", p=P)
         codes_out = out_2[0].rearrange("p m t -> p (m t)").bitcast(I32)
 
-        def weave(i):
+        def quantise_chunk(i):
+            c0, w = CHUNKS[i]
             nc.vector.tensor_copy(
                 page_g[i][:].rearrange("p (m t) -> p m t", t=PACK), page_b[i][:].rearrange("p t m -> p m t")
             )
-
-        def quantise_chunk(i):
-            c0, w = CHUNKS[i]
             nc.vector.quantize_mx(
                 out=page_w[:, c0 : c0 + w].bitcast(FP8X4), scales=page_z[:, c0 : c0 + w], in_=page_g[i][:]
             )
@@ -273,9 +314,9 @@ def tile_list_forked_prefix_page_kernel(
         def store_codes(c0, c1):
             nc.sync.dma_start(codes_out[:, c0:c1], page_w[:, c0:c1].bitcast(I32))
 
-        def multiply(step, i, n, y, on_scalar):
+        def multiply(turn, i, n, y, on_scalar):
             c0, w = CHUNKS[i]
-            acc = bank(step % BANKS)
+            acc = bank(turn % BANKS)
             nc.tensor.matmul_mx(
                 out=acc[:, 0:w],
                 lhsT=w8_w[:, P * n : P * (n + 1)].bitcast(FP8X4),
@@ -289,32 +330,31 @@ def tile_list_forked_prefix_page_kernel(
             else:
                 nc.vector.tensor_scalar(y, acc[:, 0:w], gains[:, n : n + 1], None, MULT)
 
-        def chunk_rows(i, group):
+        def solo_chunk(i):
             c0, w = CHUNKS[i]
-            for n0 in range(0, N_TILES, group):
-                y = ring.tile([P, group, w], F32, name=f"y{w}", bufs=6 if w < BANK else 3)
-                for n in range(n0, n0 + group):
+            alike = len([1 for chunk in CHUNKS[:SOLO_CHUNKS] if chunk[1] == w])
+            for n0 in range(0, N_TILES, PAIR):
+                y = ring.tile([P, PAIR, w], F32, name=f"y{w}", bufs=alike * N_TILES // PAIR)
+                for n in range(n0, n0 + PAIR):
                     multiply(N_TILES * i + n, i, n, y[:, n - n0, :], True)
-                nc.sync.dma_start(y_rows[:, n0 : n0 + group, c0 : c0 + w], y[:])
+                nc.sync.dma_start(y_rows[:, n0 : n0 + PAIR, c0 : c0 + w], y[:])
 
-        def wide_rows(n):
-            y = ring.tile([P, T2 // 2], F32, name="y_wide", bufs=6)
+        def last_chunks(n):
+            y = ring.tile([P, T2 // 2], F32, name="y_wide", bufs=N_TILES)
             for e in range(2):
-                multiply(3 * N_TILES + 2 * n + e, 3 + e, n, y[:, BANK * e : BANK * (e + 1)], (n + e) % 3 == 0)
+                turn = SOLO_CHUNKS * N_TILES + 2 * n + e
+                multiply(turn, SOLO_CHUNKS + e, n, y[:, half(e)], n >= VECTOR_TILES)
             nc.sync.dma_start(y_rows[:, n, T2 // 2 : T2], y[:])
 
         for i in range(len(CHUNKS)):
-            weave(i)
             quantise_chunk(i)
         store_codes(0, BANK)
-        chunk_rows(0, 2)
-        chunk_rows(1, 2)
-        store_codes(BANK, 3 * BANK)
-        chunk_rows(2, 2)
-        store_codes(3 * BANK, T2)
+        solo_chunk(0)
+        solo_chunk(1)
+        store_codes(BANK, T2 - BANK)
+        solo_chunk(2)
+        store_codes(T2 - BANK, T2)
         for q in range(QUADS):
-            nc.sync.dma_start(
-                out_3[0, 4 * q : 4 * q + 4, :].bitcast(I32), page_z[32 * q : 32 * q + 4, :].bitcast(I32)
-            )
+            nc.sync.dma_start(out_3[0, z_rows(q), :].bitcast(I32), page_z[z_partitions(q), :].bitcast(I32))
         for n in range(N_TILES):
-            wide_rows(n)
+            last_chunks(n)

@@ -158,11 +158,15 @@ def tile_list_forked_prefix_page_kernel(
         w1_raw1 = [placed([P, PACK, H // 2], F32, f"w1_raw1_{u}", AT_W1_HALVES[u]) for u in range(2)]
         for u in range(2):
             nc.sync.dma_start(w1_raw1[u][:], w1_rows(1)[:, :, H // 2 * u : H // 2 * (u + 1)])
-        page = [load_page(0)]
         wg_first = placed([P, S], F32, "wg_first", AT_WG_FIRST)
-        for h in range(HALVES):
+
+        def load_wg_first(h):
             for q in QUAD_ORDER:
                 nc.sync.dma_start(wg_first[quadrant(q), half(h)], wgs_rows[:, 0, half(h)])
+
+        load_wg_first(0)
+        page = [load_page(0)]
+        load_wg_first(1)
 
         w4_w = placed([P, PASSES, 2 * H], U8, "w4_w", AT_W4_W)
         w4_z = placed([P, PASSES, H], U8, "w4_z", AT_W4_Z)
@@ -196,13 +200,12 @@ def tile_list_forked_prefix_page_kernel(
         quantise_w1(0, 0, PACK)
 
         gather_words(1)
-        page.append(load_page(1))
         wg_rest = placed([P, PACK - 1, S], F32, "wg_rest", AT_WG_REST)
-        for q in QUAD_ORDER:
-            nc.sync.dma_start(wg_rest[quadrant(q), 0, :], wgs_rows[:, 1, :])
-        page.append(load_page(2))
-        for q in QUAD_ORDER:
-            nc.sync.dma_start(wg_rest[quadrant(q), 1 : PACK - 1, :], wgs_rows[:, 2:PACK, :])
+        for t in range(1, PACK):
+            for q in QUAD_ORDER:
+                nc.sync.dma_start(wg_rest[quadrant(q), t - 1, :], wgs_rows[:, t, :])
+            if t < PACK - 1:
+                page.append(load_page(t))
 
         low, high = slice(0, P // 2), slice(P // 2, P)
         nc.scalar.copy(rounded(1)[:, 0, low], columns(w1_raw1[0])[:, 0])
@@ -244,13 +247,22 @@ def tile_list_forked_prefix_page_kernel(
 
         hid = [held([P, S], F32, f"hid{t}") for t in range(PACK)]
 
+        def weighted(s, engine):
+            t, h = steps[s]
+            weight = wg_first[:, half(h)] if t == 0 else wg_rest[:, t - 1, half(h)]
+            engine.tensor_tensor(gates[s], gates[s], weight, MULT)
+
         def gated(s):
             t, h = steps[s]
-            nc.vector.tensor_tensor(hid[t][:, half(h)], values[s][:], gates[s], MULT)
+            if s < HALVES:
+                nc.vector.tensor_tensor(hid[t][:, half(h)], values[s][:], gates[s], MULT)
+            else:
+                weighted(s, nc.gpsimd)
+                nc.scalar.copy(hid[t][:, half(h)], values[s][:])
+                nc.gpsimd.tensor_tensor(hid[t][:, half(h)], hid[t][:, half(h)], gates[s], MULT)
 
         def scatter(t, j0, j1):
-            weight = wg_first[:, j0:j1] if t == 0 else wg_rest[:, t - 1, j0:j1]
-            nc.vector.tensor_tensor(page[t][:].indirect(entries(slot, j0, j1)), hid[t][:, j0:j1], weight, MULT)
+            nc.vector.tensor_copy(page[t][:].indirect(entries(slot, j0, j1)), hid[t][:, j0:j1])
 
         page_g = [held([P, PACK * w], BF16, f"page_g{c0}") for c0, w in CHUNKS]
         page_out = out_1.rearrange("(p t) c -> p t c", t=PACK)
@@ -267,8 +279,10 @@ def tile_list_forked_prefix_page_kernel(
         values.extend(value_of(s - HALVES, s) for s in range(HALVES, early))
         gates.extend(gate_of(s - HALVES, s) for s in range(early, BANKS))
 
+        weighted(0, nc.vector)
         gated(0)
         scatter(0, 0, BANK)
+        weighted(1, nc.gpsimd)
         gated(1)
         values.extend(value_of(s, s) for s in range(early, BANKS))
         gated(2)
@@ -282,8 +296,8 @@ def tile_list_forked_prefix_page_kernel(
         gains = held([P, N_TILES], F32, "gains", "v_w0_1")
         with nc.allow_non_contiguous_dma(reason="one gain value a partition and output tile"):
             nc.sync.dma_start(gains[:], gain.rearrange("(i p) -> p i", p=P))
-        w8_z = held([P, N], U8, "w8_z", "v_w1_0")
-        nc.gpsimd.memset(w8_z[:].bitcast(I32), 0)
+        w8_z = held([P, N], U8, "w8_z", "hid0")
+        nc.vector.memset(w8_z[:].bitcast(I32), 0)
         for q in range(QUADS):
             nc.sync.dma_start(w8_z[z_partitions(q), :].bitcast(I32), w8_scales[0, z_rows(q), :].bitcast(I32))
 

@@ -31,23 +31,25 @@ N_TILES = N // P
 
 QUAD_ORDER = (0, 2, 1, 3)
 
-CHUNKS = [(0, 256), (256, 256), (512, 512), (1024, 512), (1536, 512)]
-SOLO_CHUNKS = 3
+CHUNKS = [(0, 256), (256, 512), (768, 512), (1280, 512), (1792, 256)]
+SOLO_CHUNKS = 2
+WIDE = CHUNKS[SOLO_CHUNKS][0]
+ORDER = (0, 2, 3, 1)
+STEPPED = 2
 PAIR = 2
 VECTOR_TILES = 4
 
 KIB = 1024
-AT_GATES = 0
-AT_W1_HALVES = (12 * KIB, 16 * KIB)
-AT_TABLE = (15 * KIB, 42 * KIB)
-AT_W4_W = 20 * KIB
-AT_W4_Z = 22 * KIB
-AT_BIAS = 23 * KIB
-AT_WG_FIRST = 23 * KIB + 512
-AT_PAGE = (28 * KIB, 36 * KIB, 56 * KIB, 64 * KIB)
-AT_WG_REST = 44 * KIB
-AT_TAB_Z = 46 * KIB
-AT_W1_BF16 = (72 * KIB, 68 * KIB)
+AT_TAB_Z = 0
+AT_W4_W = 1 * KIB
+AT_TABLE = (33 * KIB, 3 * KIB)
+AT_WG_REST = 3 * KIB
+AT_GATES = 27 * KIB
+AT_W1_LATE = 33 * KIB
+AT_BIAS = 41 * KIB
+AT_WG_FIRST = 41 * KIB + 512
+AT_PAGE = (48 * KIB + 512, 18 * KIB + 512, 57 * KIB, 68 * KIB)
+AT_W1_BF16 = (76 * KIB, 64 * KIB + 512)
 
 
 def tile_list_forked_prefix_page_kernel(
@@ -85,17 +87,19 @@ def tile_list_forked_prefix_page_kernel(
         pick = keep.tile([P, S // LIST_ROWS], U16, name="pick")
         slot = keep.tile([P, S // LIST_ROWS], U16, name="slot")
         tab_z = placed([P, T], U8, "tab_z", AT_TAB_Z)
-        w4_z_raw = held([P, PASSES, H], U8, "w4_z_raw")
-        v_z = [held([P, S], U8, f"v_z{a}") for a in range(PASSES)]
+        w4_z_raw = held([P, H], U8, "w4_z_raw")
+        z_rows_all = held([P, S + H + N], U8, "z_rows_all")
+        z_width = (S + H + N, S + H)
+        z_all = [held([P, z_width[a]], U8, f"z_all{a}") for a in range(PASSES)]
+        v_z = [z_all[a][:, 0:S] for a in range(PASSES)]
+        w8_z = z_all[0][:, S + H : S + H + N]
 
-        nc.gpsimd.memset(w4_z_raw[:].bitcast(I32), 0)
-        warm = held([P, 2], F32, "warm")
-        nc.vector.memset(warm[:, 0:1], 0.0)
-        nc.scalar.activation(warm[:, 1:2], warm[:, 0:1], ACT.Sigmoid)
         nc.vector.memset(tab_z[QUAD : 2 * QUAD, :].bitcast(I32), 0)
         nc.vector.memset(tab_z[2 * QUAD : P, :].bitcast(I32), 0)
+        nc.vector.memset(w4_z_raw[QUAD : 2 * QUAD, :].bitcast(I32), 0)
+        nc.vector.memset(w4_z_raw[2 * QUAD : P, :].bitcast(I32), 0)
         for a in range(PASSES):
-            nc.vector.memset(v_z[a][:].bitcast(I32), 0)
+            nc.gpsimd.memset(z_all[a][:].bitcast(I32), 0)
 
         def w1_rows(a):
             return w1[K_PASS * a : K_PASS * (a + 1), :].rearrange("(p j) c -> p j c", j=PACK)
@@ -107,31 +111,40 @@ def tile_list_forked_prefix_page_kernel(
 
         nc.sync.dma_start(pick[:], offs)
         nc.sync.dma_start(tab_z[0:QUAD, :].bitcast(I32), tab_scales.rearrange("a q t -> (a q) t").bitcast(I32))
+        nc.sync.dma_start(w4_z_raw[0:QUAD, :].bitcast(I32), w4_scales.rearrange("a q c -> (a q) c").bitcast(I32))
+        nc.sync.dma_start(z_rows_all[0 : QUADS * Z_ROWS, S + H :].bitcast(I32), w8_scales[0].bitcast(I32))
+        nc.sync.dma_start(slot[:], offs2)
+        w4_raw = held([P, PASSES, 2 * H], U8, "w4_raw")
+        nc.sync.dma_start(w4_raw[:].bitcast(I32), w4_words.rearrange("a p c -> p a c").bitcast(I32))
         tab_w = [load_table(0)]
         w1_raw0 = held([P, PACK, H], F32, "w1_raw0")
         nc.sync.dma_start(w1_raw0[:], w1_rows(0))
-        w4_raw = held([P, PASSES, 2 * H], U8, "w4_raw")
-        nc.sync.dma_start(w4_raw[:].bitcast(I32), w4_words.rearrange("a p c -> p a c").bitcast(I32))
-        nc.sync.dma_start(slot[:], offs2)
-        for q in range(QUADS):
-            nc.gpsimd.dma_start(
-                w4_z_raw[z_partitions(q)].bitcast(I32),
-                w4_scales[:, z_rows(q), :].rearrange("a r c -> r a c").bitcast(I32),
-            )
 
         v_z_rows = held([P, S], U8, "v_z_rows")
+        nc.vector.tensor_copy(
+            z_rows_all[:, S : S + H].rearrange("p (t m) -> p t m", t=PACK),
+            w4_z_raw[:].rearrange("p (m t) -> p t m", t=PACK),
+        )
         nc.vector.tensor_copy(v_z_rows[:], tab_z[:].indirect(pick[:]))
+        nc.vector.tensor_copy(z_rows_all[:, 0:S].bitcast(I32), v_z_rows[:].bitcast(I32))
 
         def place_scales(a):
             for q in range(QUADS):
                 row = Z_ROWS * (QUADS * a + q)
                 nc.sync.dma_start(
-                    v_z[a][z_partitions(q), :].bitcast(I32), v_z_rows[row : row + Z_ROWS, :].bitcast(I32)
+                    z_all[a][z_partitions(q), :].bitcast(I32),
+                    z_rows_all[row : row + Z_ROWS, 0 : z_width[a]].bitcast(I32),
                 )
 
         place_scales(0)
         tab_w.append(load_table(1))
         place_scales(1)
+
+        w4_w = placed([P, PASSES, 2 * H], U8, "w4_w", AT_W4_W)
+        nc.vector.tensor_copy(
+            w4_w[:].bitcast(U16).rearrange("p a (t m) -> p a t m", t=PACK),
+            w4_raw[:].bitcast(U16).rearrange("p a (m t) -> p a t m", t=PACK),
+        )
 
         v_w = [[held([P, BANK], U32, f"v_w{a}_{h}") for h in range(HALVES)] for a in range(PASSES)]
 
@@ -150,14 +163,13 @@ def tile_list_forked_prefix_page_kernel(
 
         def load_page(t):
             rows = placed([P, T2], F32, f"page{t}", AT_PAGE[t])
-            nc.sync.dma_start(rows[:], page_rows[:, t, :])
+            nc.sync.dma_start(rows[:], page_rows[:, ORDER[t], :])
             return rows
 
         bias = placed([P, PACK], F32, "bias", AT_BIAS)
         nc.sync.dma_start(bias[:], bg.rearrange("(p t) -> p t", t=PACK))
-        w1_raw1 = [placed([P, PACK, H // 2], F32, f"w1_raw1_{u}", AT_W1_HALVES[u]) for u in range(2)]
-        for u in range(2):
-            nc.sync.dma_start(w1_raw1[u][:], w1_rows(1)[:, :, H // 2 * u : H // 2 * (u + 1)])
+        w1_raw1 = placed([P, PACK, H], F32, "w1_raw1", AT_W1_LATE)
+        nc.sync.dma_start(w1_raw1[:], w1_rows(1))
         wg_first = placed([P, S], F32, "wg_first", AT_WG_FIRST)
 
         def load_wg_first(h):
@@ -167,17 +179,6 @@ def tile_list_forked_prefix_page_kernel(
         load_wg_first(0)
         page = [load_page(0)]
         load_wg_first(1)
-
-        w4_w = placed([P, PASSES, 2 * H], U8, "w4_w", AT_W4_W)
-        w4_z = placed([P, PASSES, H], U8, "w4_z", AT_W4_Z)
-        nc.vector.tensor_copy(
-            w4_w[:].bitcast(U16).rearrange("p a (t m) -> p a t m", t=PACK),
-            w4_raw[:].bitcast(U16).rearrange("p a (m t) -> p a t m", t=PACK),
-        )
-        nc.vector.tensor_copy(
-            w4_z[:].rearrange("p a (t m) -> p a t m", t=PACK),
-            w4_z_raw[:].rearrange("p a (m t) -> p a t m", t=PACK),
-        )
 
         w1_b = [placed([P, PACK * H], BF16, f"w1_b{a}", AT_W1_BF16[a]) for a in range(PASSES)]
         w1_w = [held([P, H], U32, f"w1_w{a}") for a in range(PASSES)]
@@ -196,31 +197,28 @@ def tile_list_forked_prefix_page_kernel(
                 in_=w1_b[a][:, K_PASS * t0 : K_PASS * t1],
             )
 
-        nc.scalar.copy(rounded(0), columns(w1_raw0))
+        nc.vector.tensor_copy(rounded(0), columns(w1_raw0))
         quantise_w1(0, 0, PACK)
 
         gather_words(1)
         wg_rest = placed([P, PACK - 1, S], F32, "wg_rest", AT_WG_REST)
         for t in range(1, PACK):
             for q in QUAD_ORDER:
-                nc.sync.dma_start(wg_rest[quadrant(q), t - 1, :], wgs_rows[:, t, :])
-            if t < PACK - 1:
+                nc.sync.dma_start(wg_rest[quadrant(q), t - 1, :], wgs_rows[:, ORDER[t], :])
+            if t == 1:
                 page.append(load_page(t))
 
-        low, high = slice(0, P // 2), slice(P // 2, P)
-        nc.scalar.copy(rounded(1)[:, 0, low], columns(w1_raw1[0])[:, 0])
-        nc.scalar.copy(rounded(1)[:, 1:PACK, low], columns(w1_raw1[0])[:, 1:PACK])
-        nc.vector.tensor_copy(rounded(1)[:, 0, high], columns(w1_raw1[1])[:, 0])
+        nc.vector.tensor_copy(rounded(1)[:, 0], columns(w1_raw1)[:, 0])
         quantise_w1(1, 0, 1)
-        nc.vector.tensor_copy(rounded(1)[:, 1:PACK, high], columns(w1_raw1[1])[:, 1:PACK])
-        quantise_w1(1, 1, 2)
-        quantise_w1(1, 2, PACK)
-        page.append(load_page(3))
+        nc.scalar.copy(rounded(1)[:, 1], columns(w1_raw1)[:, 1])
+        nc.vector.tensor_copy(rounded(1)[:, 2:PACK], columns(w1_raw1)[:, 2:PACK])
+        quantise_w1(1, 1, PACK)
+        page.extend(load_page(t) for t in range(2, PACK))
 
         steps = [(t, h) for t in range(PACK) for h in range(HALVES)]
 
         def product(b, s, words, dtype, width, scales):
-            t, h = steps[s]
+            t, h = ORDER[steps[s][0]], steps[s][1]
             acc = bank(b)
             for a in range(PASSES):
                 nc.tensor.matmul_mx(
@@ -233,19 +231,20 @@ def tile_list_forked_prefix_page_kernel(
                 )
             return acc
 
-        gate_rows = placed([P, PACK * S], F32, "gate_rows", AT_GATES)
+        gate_first = held([P, BANK], F32, "gate_first")
+        gate_rows = placed([P, PACK * S - BANK], F32, "gate_rows", AT_GATES)
 
         def gate_of(b, s):
-            logit = product(b, s, lambda a: w4_w[:, a, :], FP4X4, 2 * P, lambda a: w4_z[:, a, :])
-            t = steps[s][0]
-            gate = gate_rows[:, BANK * s : BANK * (s + 1)]
+            logit = product(b, s, lambda a: w4_w[:, a, :], FP4X4, 2 * P, lambda a: z_all[a][:, S : S + H])
+            t = ORDER[steps[s][0]]
+            gate = gate_rows[:, half(s - 1)] if s else gate_first[:]
             nc.scalar.activation(gate, logit[:], ACT.Sigmoid, bias=bias[:, t : t + 1])
             return gate
 
         def value_of(b, s):
             return product(b, s, lambda a: w1_w[a][:], FP8X4, P, lambda a: w1_z[a][:])
 
-        hid = [held([P, S], F32, f"hid{t}") for t in range(PACK)]
+        hid = [held([P, S], F32, f"hid{t}") for t in range(PACK - 1)]
 
         def weighted(s, engine):
             t, h = steps[s]
@@ -258,7 +257,8 @@ def tile_list_forked_prefix_page_kernel(
                 nc.vector.tensor_tensor(hid[t][:, half(h)], values[s][:], gates[s], MULT)
             else:
                 weighted(s, nc.gpsimd)
-                nc.scalar.copy(hid[t][:, half(h)], values[s][:])
+                if t < PACK - 1:
+                    nc.scalar.copy(hid[t][:, half(h)], values[s][:])
                 nc.gpsimd.tensor_tensor(hid[t][:, half(h)], hid[t][:, half(h)], gates[s], MULT)
 
         def scatter(t, j0, j1):
@@ -266,44 +266,48 @@ def tile_list_forked_prefix_page_kernel(
 
         page_g = [held([P, PACK * w], BF16, f"page_g{c0}") for c0, w in CHUNKS]
         page_out = out_1.rearrange("(p t) c -> p t c", t=PACK)
-        page_b = [held([P, PACK, w], BF16, f"page_b{c0}") for c0, w in CHUNKS]
+        page_b = {i: held([P, PACK, CHUNKS[i][1]], BF16, f"page_b{i}") for i in range(STEPPED, len(CHUNKS))}
+
+        def woven(i, t):
+            return page_g[i][:].rearrange("p (m t) -> p m t", t=PACK)[:, :, ORDER[t]]
 
         def finish(t):
-            nc.sync.dma_start(page_out[:, t, :], page[t][:])
+            nc.sync.dma_start(page_out[:, ORDER[t], :], page[t][:])
             for i, (c0, w) in enumerate(CHUNKS):
-                nc.scalar.copy(page_b[i][:, t, :], page[t][:, c0 : c0 + w])
+                if i >= STEPPED:
+                    nc.scalar.copy(page_b[i][:, ORDER[t], :], page[t][:, c0 : c0 + w])
+                elif t < PACK - 1:
+                    nc.scalar.copy(woven(i, t), page[t][:, c0 : c0 + w])
 
         early = BANKS - HALVES
-        gates = [gate_of(s, s) for s in range(early)]
-        values = [value_of(early + s, s) for s in range(HALVES)]
-        values.extend(value_of(s - HALVES, s) for s in range(HALVES, early))
-        gates.extend(gate_of(s - HALVES, s) for s in range(early, BANKS))
+        gates = [gate_of(s, s) for s in range(HALVES)]
+        values = [value_of(HALVES + s, s) for s in range(early)]
+        gates.extend(gate_of(s % HALVES, s) for s in range(HALVES, BANKS))
 
-        weighted(0, nc.vector)
+        weighted(0, nc.gpsimd)
         gated(0)
         scatter(0, 0, BANK)
         weighted(1, nc.gpsimd)
         gated(1)
-        values.extend(value_of(s, s) for s in range(early, BANKS))
+        values.extend(value_of(HALVES + s - early, s) for s in range(early, BANKS))
         gated(2)
         scatter(0, BANK, S)
         finish(0)
         gated(3)
         gated(4)
+        gated(5)
+        hid.append(held([P, S], F32, "hid_last", "hid0"))
+        for h in range(HALVES):
+            nc.scalar.copy(hid[PACK - 1][:, half(h)], values[BANKS - HALVES + h][:])
 
         w8_w = held([P, N], U32, "w8_w", "v_w0_0")
         nc.sync.dma_start(w8_w[:].bitcast(I32), w8_words[0].rearrange("p c i -> p (c i)").bitcast(I32))
         gains = held([P, N_TILES], F32, "gains", "v_w0_1")
         with nc.allow_non_contiguous_dma(reason="one gain value a partition and output tile"):
             nc.sync.dma_start(gains[:], gain.rearrange("(i p) -> p i", p=P))
-        w8_z = held([P, N], U8, "w8_z", "hid0")
-        nc.vector.memset(w8_z[:].bitcast(I32), 0)
-        for q in range(QUADS):
-            nc.sync.dma_start(w8_z[z_partitions(q), :].bitcast(I32), w8_scales[0, z_rows(q), :].bitcast(I32))
 
         scatter(1, 0, S)
         finish(1)
-        gated(5)
         gated(6)
         gated(7)
         scatter(2, 0, S)
@@ -318,9 +322,13 @@ def tile_list_forked_prefix_page_kernel(
 
         def quantise_chunk(i):
             c0, w = CHUNKS[i]
-            nc.vector.tensor_copy(
-                page_g[i][:].rearrange("p (m t) -> p m t", t=PACK), page_b[i][:].rearrange("p t m -> p m t")
-            )
+            if i < STEPPED:
+                nc.vector.tensor_copy(woven(i, PACK - 1), page[PACK - 1][:, c0 : c0 + w])
+            else:
+                nc.vector.tensor_copy(
+                    page_g[i][:].rearrange("p (c m t) -> p c t m", m=PACK, t=PACK),
+                    page_b[i][:].rearrange("p t (c m) -> p c t m", m=PACK),
+                )
             nc.vector.quantize_mx(
                 out=page_w[:, c0 : c0 + w].bitcast(FP8X4), scales=page_z[:, c0 : c0 + w], in_=page_g[i][:]
             )
@@ -344,30 +352,34 @@ def tile_list_forked_prefix_page_kernel(
             else:
                 nc.vector.tensor_scalar(y, acc[:, 0:w], gains[:, n : n + 1], None, MULT)
 
-        def solo_chunk(i):
+        def solo_chunk(i, n0):
             c0, w = CHUNKS[i]
             alike = len([1 for chunk in CHUNKS[:SOLO_CHUNKS] if chunk[1] == w])
-            for n0 in range(0, N_TILES, PAIR):
-                y = ring.tile([P, PAIR, w], F32, name=f"y{w}", bufs=alike * N_TILES // PAIR)
-                for n in range(n0, n0 + PAIR):
-                    multiply(N_TILES * i + n, i, n, y[:, n - n0, :], True)
-                nc.sync.dma_start(y_rows[:, n0 : n0 + PAIR, c0 : c0 + w], y[:])
+            y = ring.tile([P, PAIR, w], F32, name=f"y{w}", bufs=alike * N_TILES // PAIR)
+            for n in range(n0, n0 + PAIR):
+                multiply(N_TILES * i + n, i, n, y[:, n - n0, :], True)
+            nc.sync.dma_start(y_rows[:, n0 : n0 + PAIR, c0 : c0 + w], y[:])
 
         def last_chunks(n):
-            y = ring.tile([P, T2 // 2], F32, name="y_wide", bufs=N_TILES)
-            for e in range(2):
-                turn = SOLO_CHUNKS * N_TILES + 2 * n + e
-                multiply(turn, SOLO_CHUNKS + e, n, y[:, half(e)], n >= VECTOR_TILES)
-            nc.sync.dma_start(y_rows[:, n, T2 // 2 : T2], y[:])
+            y = ring.tile([P, T2 - WIDE], F32, name="y_wide", bufs=N_TILES)
+            for i in range(SOLO_CHUNKS, len(CHUNKS)):
+                c0, w = CHUNKS[i]
+                turn = SOLO_CHUNKS * N_TILES + (len(CHUNKS) - SOLO_CHUNKS) * n + i - SOLO_CHUNKS
+                multiply(turn, i, n, y[:, c0 - WIDE : c0 - WIDE + w], n % 2 == 1)
+            nc.sync.dma_start(y_rows[:, n, WIDE:T2], y[:])
 
         for i in range(len(CHUNKS)):
             quantise_chunk(i)
-        store_codes(0, BANK)
-        solo_chunk(0)
-        solo_chunk(1)
-        store_codes(BANK, T2 - BANK)
-        solo_chunk(2)
-        store_codes(T2 - BANK, T2)
+        store_codes(0, 256)
+        solo_chunk(0, 0)
+        store_codes(256, 768)
+        solo_chunk(0, 2)
+        solo_chunk(0, 4)
+        store_codes(768, 1280)
+        solo_chunk(1, 0)
+        solo_chunk(1, 2)
+        store_codes(1280, T2)
+        solo_chunk(1, 4)
         for q in range(QUADS):
             nc.sync.dma_start(out_3[0, z_rows(q), :].bitcast(I32), page_z[z_partitions(q), :].bitcast(I32))
         for n in range(N_TILES):

@@ -46,7 +46,6 @@ AT_TABLE = (33 * KIB, 3 * KIB)
 AT_WG_REST = 3 * KIB
 AT_GATES = 27 * KIB
 AT_W1_LATE = 33 * KIB
-AT_BIAS = 41 * KIB
 AT_WG_FIRST = 41 * KIB + 512
 AT_PAGE = (48 * KIB + 512, 18 * KIB + 512, 57 * KIB, 68 * KIB)
 AT_W1_BF16 = (76 * KIB, 64 * KIB + 512)
@@ -88,11 +87,10 @@ def tile_list_forked_prefix_page_kernel(
         slot = keep.tile([P, S // LIST_ROWS], U16, name="slot")
         tab_z = placed([P, T], U8, "tab_z", AT_TAB_Z)
         w4_z_raw = held([P, H], U8, "w4_z_raw")
-        z_rows_all = held([P, S + H + N], U8, "z_rows_all")
-        z_width = (S + H + N, S + H)
-        z_all = [held([P, z_width[a]], U8, f"z_all{a}") for a in range(PASSES)]
+        z_rows_all = held([P, S + H], U8, "z_rows_all")
+        z_all = [held([P, S + H], U8, f"z_all{a}") for a in range(PASSES)]
         v_z = [z_all[a][:, 0:S] for a in range(PASSES)]
-        w8_z = z_all[0][:, S + H : S + H + N]
+        w8_z = z_all[1][:, 0:N]
 
         nc.vector.memset(tab_z[QUAD : 2 * QUAD, :].bitcast(I32), 0)
         nc.vector.memset(tab_z[2 * QUAD : P, :].bitcast(I32), 0)
@@ -112,8 +110,9 @@ def tile_list_forked_prefix_page_kernel(
         nc.sync.dma_start(pick[:], offs)
         nc.sync.dma_start(tab_z[0:QUAD, :].bitcast(I32), tab_scales.rearrange("a q t -> (a q) t").bitcast(I32))
         nc.sync.dma_start(w4_z_raw[0:QUAD, :].bitcast(I32), w4_scales.rearrange("a q c -> (a q) c").bitcast(I32))
-        nc.sync.dma_start(z_rows_all[0 : QUADS * Z_ROWS, S + H :].bitcast(I32), w8_scales[0].bitcast(I32))
         nc.sync.dma_start(slot[:], offs2)
+        bias = held([P, PACK], F32, "bias")
+        nc.sync.dma_start(bias[:], bg.rearrange("(p t) -> p t", t=PACK))
         w4_raw = held([P, PASSES, 2 * H], U8, "w4_raw")
         nc.sync.dma_start(w4_raw[:].bitcast(I32), w4_words.rearrange("a p c -> p a c").bitcast(I32))
         tab_w = [load_table(0)]
@@ -133,7 +132,7 @@ def tile_list_forked_prefix_page_kernel(
                 row = Z_ROWS * (QUADS * a + q)
                 nc.sync.dma_start(
                     z_all[a][z_partitions(q), :].bitcast(I32),
-                    z_rows_all[row : row + Z_ROWS, 0 : z_width[a]].bitcast(I32),
+                    z_rows_all[row : row + Z_ROWS, :].bitcast(I32),
                 )
 
         place_scales(0)
@@ -166,8 +165,6 @@ def tile_list_forked_prefix_page_kernel(
             nc.sync.dma_start(rows[:], page_rows[:, ORDER[t], :])
             return rows
 
-        bias = placed([P, PACK], F32, "bias", AT_BIAS)
-        nc.sync.dma_start(bias[:], bg.rearrange("(p t) -> p t", t=PACK))
         w1_raw1 = placed([P, PACK, H], F32, "w1_raw1", AT_W1_LATE)
         nc.sync.dma_start(w1_raw1[:], w1_rows(1))
         wg_first = placed([P, S], F32, "wg_first", AT_WG_FIRST)
@@ -284,7 +281,7 @@ def tile_list_forked_prefix_page_kernel(
         values = [value_of(HALVES + s, s) for s in range(early)]
         gates.extend(gate_of(s % HALVES, s) for s in range(HALVES, BANKS))
 
-        weighted(0, nc.gpsimd)
+        weighted(0, nc.vector)
         gated(0)
         scatter(0, 0, BANK)
         weighted(1, nc.gpsimd)
@@ -302,6 +299,8 @@ def tile_list_forked_prefix_page_kernel(
 
         w8_w = held([P, N], U32, "w8_w", "v_w0_0")
         nc.sync.dma_start(w8_w[:].bitcast(I32), w8_words[0].rearrange("p c i -> p (c i)").bitcast(I32))
+        for q in range(QUADS):
+            nc.sync.dma_start(z_all[1][z_partitions(q), 0:N].bitcast(I32), w8_scales[0, z_rows(q), :].bitcast(I32))
         gains = held([P, N_TILES], F32, "gains", "v_w0_1")
         with nc.allow_non_contiguous_dma(reason="one gain value a partition and output tile"):
             nc.sync.dma_start(gains[:], gain.rearrange("(i p) -> p i", p=P))

@@ -109,13 +109,13 @@ def tile_list_forked_prefix_page_kernel(
 
         nc.sync.dma_start(pick[:], offs)
         nc.sync.dma_start(tab_z[0:QUAD, :].bitcast(I32), tab_scales.rearrange("a q t -> (a q) t").bitcast(I32))
-        nc.sync.dma_start(w4_z_raw[0:QUAD, :].bitcast(I32), w4_scales.rearrange("a q c -> (a q) c").bitcast(I32))
-        nc.sync.dma_start(slot[:], offs2)
+        nc.scalar.dma_start(w4_z_raw[0:QUAD, :].bitcast(I32), w4_scales.rearrange("a q c -> (a q) c").bitcast(I32))
         bias = held([P, PACK], F32, "bias")
-        nc.sync.dma_start(bias[:], bg.rearrange("(p t) -> p t", t=PACK))
+        nc.scalar.dma_start(bias[:], bg.rearrange("(p t) -> p t", t=PACK))
         w4_raw = held([P, PASSES, 2 * H], U8, "w4_raw")
-        nc.sync.dma_start(w4_raw[:].bitcast(I32), w4_words.rearrange("a p c -> p a c").bitcast(I32))
+        nc.scalar.dma_start(w4_raw[:].bitcast(I32), w4_words.rearrange("a p c -> p a c").bitcast(I32))
         tab_w = [load_table(0)]
+        nc.sync.dma_start(slot[:], offs2)
         w1_raw0 = held([P, PACK, H], F32, "w1_raw0")
         nc.sync.dma_start(w1_raw0[:], w1_rows(0))
 

@@ -114,8 +114,8 @@ def tile_list_forked_prefix_page_kernel(
         nc.scalar.dma_start(bias[:], bg.rearrange("(p t) -> p t", t=PACK))
         w4_raw = held([P, PASSES, 2 * H], U8, "w4_raw")
         nc.scalar.dma_start(w4_raw[:].bitcast(I32), w4_words.rearrange("a p c -> p a c").bitcast(I32))
-        tab_w = [load_table(0)]
         nc.sync.dma_start(slot[:], offs2)
+        tab_w = [load_table(0)]
         w1_raw0 = held([P, PACK, H], F32, "w1_raw0")
         nc.sync.dma_start(w1_raw0[:], w1_rows(0))
 

@@ -1,6 +1,7 @@
 from contextlib import ExitStack
 
 import concourse.mybir as mybir
+from concourse.masks import make_identity
 
 K, H, N, T, S, T2 = 1024, 512, 768, 4096, 1024, 2048
 FLOPS = 2 * (2 * K * H * S + H * N * T2)
@@ -23,32 +24,36 @@ PASSES = K // K_PASS
 BANK = 512
 BANKS = 8
 HALVES = S // BANK
+QUARTER = BANK // 2
 QUAD = 32
 QUADS = P // QUAD
 Z_ROWS = 4
 LIST_ROWS = 16
 N_TILES = N // P
 
-QUAD_ORDER = (0, 2, 1, 3)
+ORDER = (0, 2, 3, 1)
+STEPS = [(i, j) for i in range(PACK) for j in range(0, S, BANK)]
 
 CHUNKS = [(0, 256), (256, 512), (768, 512), (1280, 512), (1792, 256)]
 SOLO_CHUNKS = 2
 WIDE = CHUNKS[SOLO_CHUNKS][0]
-ORDER = (0, 2, 3, 1)
 STEPPED = 2
 PAIR = 2
-VECTOR_TILES = 4
 
 KIB = 1024
-AT_TAB_Z = 0
-AT_W4_W = 1 * KIB
-AT_TABLE = (33 * KIB, 3 * KIB)
-AT_WG_REST = 3 * KIB
-AT_GATES = 27 * KIB
-AT_W1_LATE = 33 * KIB
-AT_WG_FIRST = 41 * KIB + 512
-AT_PAGE = (48 * KIB + 512, 18 * KIB + 512, 57 * KIB, 68 * KIB)
-AT_W1_BF16 = (76 * KIB, 64 * KIB + 512)
+LAP = 64
+AT_W1_RAW = (0, 8 * KIB)
+AT_GATES = (8 * KIB, 10 * KIB)
+AT_TABLE0 = 8 * KIB - LAP
+AT_PAGE = (16 * KIB, 24 * KIB, 32 * KIB, 40 * KIB)
+AT_TABLE1 = 32 * KIB - LAP
+AT_V_Z_ROWS = 40 * KIB
+AT_WGS_TURNED = (48 * KIB, 56 * KIB)
+AT_W1_BF16 = (64 * KIB, 68 * KIB)
+AT_FACTOR = 68 * KIB
+AT_TAB_Z = 72 * KIB
+AT_W4_W = 72 * KIB
+AT_Y = 48 * KIB
 
 
 def tile_list_forked_prefix_page_kernel(
@@ -58,7 +63,6 @@ def tile_list_forked_prefix_page_kernel(
     nc = tc.nc
     with ExitStack() as ctx:
         keep = ctx.enter_context(tc.tile_pool(name="keep", bufs=1))
-        ring = ctx.enter_context(tc.tile_pool(name="ring", bufs=1))
         arena = ctx.enter_context(tc.tile_pool(name="arena", bufs=1))
         psum = ctx.enter_context(tc.psum_pool(name="psum", bufs=1))
 
@@ -71,9 +75,6 @@ def tile_list_forked_prefix_page_kernel(
         def bank(b):
             return psum.tile([P, BANK], F32, name=f"bank{b}")
 
-        def quadrant(q):
-            return slice(QUAD * q, QUAD * (q + 1))
-
         def z_partitions(q):
             return slice(QUAD * q, QUAD * q + Z_ROWS)
 
@@ -83,29 +84,34 @@ def tile_list_forked_prefix_page_kernel(
         def half(h):
             return slice(BANK * h, BANK * (h + 1))
 
+        def block(b):
+            return slice(P * b, P * (b + 1))
+
         pick = keep.tile([P, S // LIST_ROWS], U16, name="pick")
         slot = keep.tile([P, S // LIST_ROWS], U16, name="slot")
         tab_z = placed([P, T], U8, "tab_z", AT_TAB_Z)
         w4_z_raw = held([P, H], U8, "w4_z_raw")
         z_rows_all = held([P, S + H], U8, "z_rows_all")
         z_all = [held([P, S + H], U8, f"z_all{a}") for a in range(PASSES)]
-        v_z = [z_all[a][:, 0:S] for a in range(PASSES)]
         w8_z = z_all[1][:, 0:N]
 
         nc.vector.memset(tab_z[QUAD : 2 * QUAD, :].bitcast(I32), 0)
         nc.vector.memset(tab_z[2 * QUAD : P, :].bitcast(I32), 0)
         nc.vector.memset(w4_z_raw[QUAD : 2 * QUAD, :].bitcast(I32), 0)
         nc.vector.memset(w4_z_raw[2 * QUAD : P, :].bitcast(I32), 0)
+        identity = held([P, P], F32, "identity")
+        make_identity(nc, identity[:])
         for a in range(PASSES):
             nc.gpsimd.memset(z_all[a][:].bitcast(I32), 0)
 
-        def w1_rows(a):
-            return w1[K_PASS * a : K_PASS * (a + 1), :].rearrange("(p j) c -> p j c", j=PACK)
+        def load_w1(a):
+            raw = placed([P, PACK, H], F32, f"w1_raw{a}", AT_W1_RAW[a])
+            nc.sync.dma_start(raw[:], w1[K_PASS * a : K_PASS * (a + 1), :].rearrange("(p j) c -> p j c", j=PACK))
+            return raw
 
-        def load_table(a):
-            words = placed([P, T], U32, f"tab_w{a}", AT_TABLE[a])
-            nc.sync.dma_start(words[:].bitcast(I32), tab_words[a].rearrange("p t i -> p (t i)").bitcast(I32))
-            return words
+        def load_table(a, c0, c1):
+            words = tab_words[a].rearrange("p t i -> p (t i)").bitcast(I32)
+            nc.sync.dma_start(tab_w[a][:, c0:c1].bitcast(I32), words[:, c0:c1])
 
         nc.sync.dma_start(pick[:], offs)
         nc.sync.dma_start(tab_z[0:QUAD, :].bitcast(I32), tab_scales.rearrange("a q t -> (a q) t").bitcast(I32))
@@ -115,11 +121,28 @@ def tile_list_forked_prefix_page_kernel(
         w4_raw = held([P, PASSES, 2 * H], U8, "w4_raw")
         nc.scalar.dma_start(w4_raw[:].bitcast(I32), w4_words.rearrange("a p c -> p a c").bitcast(I32))
         nc.sync.dma_start(slot[:], offs2)
-        tab_w = [load_table(0)]
-        w1_raw0 = held([P, PACK, H], F32, "w1_raw0")
-        nc.sync.dma_start(w1_raw0[:], w1_rows(0))
+        wgs_raw = held([P, S], F32, "wgs_raw")
+        nc.sync.dma_start(wgs_raw[:], wgs)
+        tab_w = [placed([P, T], U32, "tab_w0", AT_TABLE0)]
+        load_table(0, 0, T)
 
-        v_z_rows = held([P, S], U8, "v_z_rows")
+        weights = held([P, PACK, S], F32, "weights")
+        for h in range(HALVES):
+            turned = bank(h)
+            for b in range(PACK):
+                nc.tensor.transpose(turned[:, block(b)], wgs_raw[:, block(PACK * h + b)], identity[:])
+            spread = placed([P, PACK, PACK, QUADS, QUAD], F32, f"wgs_spread{h}", AT_WGS_TURNED[h])
+            rows = turned[:].rearrange("j (b m t) -> j b t m", b=PACK, t=PACK)
+            nc.scalar.copy(spread[:], rows.unsqueeze(3).broadcast_to([P, PACK, PACK, QUADS, QUAD]))
+            for i in range(PACK):
+                back = bank(HALVES + (PACK * h + i) % (BANKS - HALVES))
+                for b in range(PACK):
+                    nc.tensor.transpose(
+                        back[:, block(b)], spread[:, b, ORDER[i]].rearrange("j q m -> j (q m)"), identity[:]
+                    )
+                nc.scalar.copy(weights[:, i, half(h)], back[:])
+
+        v_z_rows = placed([P, S], U8, "v_z_rows", AT_V_Z_ROWS)
         nc.vector.tensor_copy(
             z_rows_all[:, S : S + H].rearrange("p (t m) -> p t m", t=PACK),
             w4_z_raw[:].rearrange("p (m t) -> p t m", t=PACK),
@@ -135,9 +158,10 @@ def tile_list_forked_prefix_page_kernel(
                     z_rows_all[row : row + Z_ROWS, :].bitcast(I32),
                 )
 
-        place_scales(0)
-        tab_w.append(load_table(1))
-        place_scales(1)
+        tab_w.append(placed([P, T], U32, "tab_w1", AT_TABLE1))
+        for a in range(PASSES):
+            place_scales(a)
+            load_table(1, a * T // PASSES, (a + 1) * T // PASSES)
 
         w4_w = placed([P, PASSES, 2 * H], U8, "w4_w", AT_W4_W)
         nc.vector.tensor_copy(
@@ -147,45 +171,40 @@ def tile_list_forked_prefix_page_kernel(
 
         v_w = [[held([P, BANK], U32, f"v_w{a}_{h}") for h in range(HALVES)] for a in range(PASSES)]
 
-        def entries(lst, j0, j1):
-            return lst[:, j0 // LIST_ROWS : j1 // LIST_ROWS]
+        def entries(lst, j0, n):
+            return lst[:, j0 // LIST_ROWS : (j0 + n) // LIST_ROWS]
 
-        def gather_words(a):
-            for h in range(HALVES):
-                picked = tab_w[a][:].indirect(entries(pick, BANK * h, BANK * (h + 1)))
-                nc.vector.tensor_copy(v_w[a][h][:], picked)
+        def picked_words(a, j0, n):
+            return v_w[a][j0 // BANK][:, j0 % BANK : j0 % BANK + n]
 
-        gather_words(0)
+        def gather_words(a, j0, n):
+            nc.vector.tensor_copy(picked_words(a, j0, n), tab_w[a][:].indirect(entries(pick, j0, n)))
+
+        for h in range(HALVES):
+            gather_words(0, BANK * h, BANK)
 
         page_rows = page0.rearrange("(p t) c -> p t c", t=PACK)
-        wgs_rows = wgs.rearrange("(q t) j -> q t j", t=PACK)
 
-        def load_page(t):
-            rows = placed([P, T2], F32, f"page{t}", AT_PAGE[t])
-            nc.sync.dma_start(rows[:], page_rows[:, ORDER[t], :])
+        def load_page(i):
+            rows = placed([P, T2], F32, f"page{i}", AT_PAGE[i])
+            nc.sync.dma_start(rows[:], page_rows[:, ORDER[i], :])
             return rows
 
-        w1_raw1 = placed([P, PACK, H], F32, "w1_raw1", AT_W1_LATE)
-        nc.sync.dma_start(w1_raw1[:], w1_rows(1))
-        wg_first = placed([P, S], F32, "wg_first", AT_WG_FIRST)
-
-        def load_wg_first(h):
-            for q in QUAD_ORDER:
-                nc.sync.dma_start(wg_first[quadrant(q), half(h)], wgs_rows[:, 0, half(h)])
-
-        load_wg_first(0)
+        w1_raw = [load_w1(a) for a in range(PASSES)]
         page = [load_page(0)]
-        load_wg_first(1)
+        for h in range(HALVES):
+            gather_words(1, BANK * h, BANK)
+        page.extend(load_page(i) for i in range(1, PACK))
 
-        w1_b = [placed([P, PACK * H], BF16, f"w1_b{a}", AT_W1_BF16[a]) for a in range(PASSES)]
         w1_w = [held([P, H], U32, f"w1_w{a}") for a in range(PASSES)]
         w1_z = [held([P, H], U8, f"w1_z{a}") for a in range(PASSES)]
+        w1_b = [placed([P, PACK * H], BF16, f"w1_b{a}", AT_W1_BF16[a]) for a in range(PASSES)]
 
-        def rounded(a):
-            return w1_b[a][:].rearrange("p (t m j) -> p t m j", t=PACK, j=PACK)
-
-        def columns(raw):
-            return raw[:].rearrange("p j (m t) -> p t m j", t=PACK)
+        def round_w1(copy, a, t0, t1):
+            copy(
+                w1_b[a][:].rearrange("p (t m j) -> p m j t", t=PACK, j=PACK)[:, :, :, t0:t1],
+                w1_raw[a][:].rearrange("p j (m t) -> p m j t", t=PACK)[:, :, :, t0:t1],
+            )
 
         def quantise_w1(a, t0, t1):
             nc.vector.quantize_mx(
@@ -194,108 +213,66 @@ def tile_list_forked_prefix_page_kernel(
                 in_=w1_b[a][:, K_PASS * t0 : K_PASS * t1],
             )
 
-        nc.vector.tensor_copy(rounded(0), columns(w1_raw0))
-        quantise_w1(0, 0, PACK)
+        hid = [held([P, S], F32, f"hid{i}") for i in range(PACK - 1)]
 
-        gather_words(1)
-        wg_rest = placed([P, PACK - 1, S], F32, "wg_rest", AT_WG_REST)
-        for t in range(1, PACK):
-            for q in QUAD_ORDER:
-                nc.sync.dma_start(wg_rest[quadrant(q), t - 1, :], wgs_rows[:, ORDER[t], :])
-            if t == 1:
-                page.append(load_page(t))
-
-        nc.vector.tensor_copy(rounded(1)[:, 0], columns(w1_raw1)[:, 0])
-        quantise_w1(1, 0, 1)
-        nc.scalar.copy(rounded(1)[:, 1], columns(w1_raw1)[:, 1])
-        nc.vector.tensor_copy(rounded(1)[:, 2:PACK], columns(w1_raw1)[:, 2:PACK])
-        quantise_w1(1, 1, PACK)
-        page.extend(load_page(t) for t in range(2, PACK))
-
-        steps = [(t, h) for t in range(PACK) for h in range(HALVES)]
-
-        def product(b, s, words, dtype, width, scales):
-            t, h = ORDER[steps[s][0]], steps[s][1]
+        def product(b, i, j0, n, words, dtype, width, scales):
+            t = ORDER[i]
             acc = bank(b)
             for a in range(PASSES):
                 nc.tensor.matmul_mx(
-                    out=acc[:],
+                    out=acc[:, 0:n],
                     lhsT=words(a)[:, width * t : width * (t + 1)].bitcast(dtype),
-                    lhsT_scale=scales(a)[:, P * t : P * (t + 1)],
-                    rhs=v_w[a][h][:].bitcast(FP8X4),
-                    rhs_scale=v_z[a][:, half(h)],
+                    lhsT_scale=scales(a)[:, block(t)],
+                    rhs=picked_words(a, j0, n).bitcast(FP8X4),
+                    rhs_scale=z_all[a][:, j0 : j0 + n],
                     start=(a == 0), stop=(a == PASSES - 1),
                 )
-            return acc
+            return acc[:, 0:n]
 
-        gate_first = held([P, BANK], F32, "gate_first")
-        gate_rows = placed([P, PACK * S - BANK], F32, "gate_rows", AT_GATES)
+        def gate_of(s, gate):
+            i, j0 = STEPS[s]
+            b = (2 * s + min(s, 1)) % BANKS
+            logit = product(b, i, j0, BANK, lambda a: w4_w[:, a, :], FP4X4, 2 * P, lambda a: z_all[a][:, S : S + H])
+            nc.scalar.activation(gate[:], logit, ACT.Sigmoid, bias=bias[:, ORDER[i] : ORDER[i] + 1])
 
-        def gate_of(b, s):
-            logit = product(b, s, lambda a: w4_w[:, a, :], FP4X4, 2 * P, lambda a: z_all[a][:, S : S + H])
-            t = ORDER[steps[s][0]]
-            gate = gate_rows[:, half(s - 1)] if s else gate_first[:]
-            nc.scalar.activation(gate, logit[:], ACT.Sigmoid, bias=bias[:, t : t + 1])
-            return gate
+        def value_of(b, i, j0, n):
+            return product(b, i, j0, n, lambda a: w1_w[a][:], FP8X4, P, lambda a: w1_z[a][:])
 
-        def value_of(b, s):
-            return product(b, s, lambda a: w1_w[a][:], FP8X4, P, lambda a: w1_z[a][:])
+        first = held([P, BANK], F32, "first")
+        gate_of(0, first)
+        round_w1(nc.vector.tensor_copy, 0, 0, 2)
+        round_w1(nc.scalar.copy, 0, 2, PACK)
+        quantise_w1(0, 0, 2)
+        nc.vector.tensor_tensor(first[:], first[:], weights[:, 0, 0:BANK], MULT)
+        quantise_w1(0, 2, PACK)
+        round_w1(nc.vector.tensor_copy, 1, 0, 2)
+        round_w1(nc.scalar.copy, 1, 2, PACK)
+        quantise_w1(1, 0, 1)
+        quantise_w1(1, 1, 2)
+        quantise_w1(1, 2, PACK)
 
-        hid = [held([P, S], F32, f"hid{t}") for t in range(PACK - 1)]
+        nc.vector.tensor_tensor(hid[0][:, 0:QUARTER], value_of(1, 0, 0, QUARTER), first[:, 0:QUARTER], MULT)
+        nc.scalar.copy(hid[0][:, QUARTER:BANK], value_of(2, 0, QUARTER, QUARTER))
+        nc.gpsimd.tensor_tensor(hid[0][:, QUARTER:BANK], hid[0][:, QUARTER:BANK], first[:, QUARTER:BANK], MULT)
 
-        def weighted(s, engine):
-            t, h = steps[s]
-            weight = wg_first[:, half(h)] if t == 0 else wg_rest[:, t - 1, half(h)]
-            engine.tensor_tensor(gates[s], gates[s], weight, MULT)
+        def gated(s, gate, sums):
+            i, j0 = STEPS[s]
+            value = hid[i][:, j0 : j0 + BANK]
+            factor = placed([P, BANK], F32, f"factor{s}", AT_FACTOR)
+            nc.gpsimd.tensor_tensor(factor[:], gate[:], weights[:, i, j0 : j0 + BANK], MULT)
+            nc.scalar.copy(value, sums)
+            nc.gpsimd.tensor_tensor(value, value, factor[:], MULT)
 
-        def gated(s):
-            t, h = steps[s]
-            if s < HALVES:
-                nc.vector.tensor_tensor(hid[t][:, half(h)], values[s][:], gates[s], MULT)
+        late = []
+        for s in range(1, len(STEPS)):
+            i, j0 = STEPS[s]
+            gate = placed([P, BANK], F32, f"gate{s}", AT_GATES[s % 2] + (4 * KIB if i == PACK - 1 else 0))
+            gate_of(s, gate)
+            sums = value_of((2 * s + 2) % BANKS, i, j0, BANK)
+            if i < PACK - 1:
+                gated(s, gate, sums)
             else:
-                weighted(s, nc.gpsimd)
-                if t < PACK - 1:
-                    nc.scalar.copy(hid[t][:, half(h)], values[s][:])
-                nc.gpsimd.tensor_tensor(hid[t][:, half(h)], hid[t][:, half(h)], gates[s], MULT)
-
-        def scatter(t, j0, j1):
-            nc.vector.tensor_copy(page[t][:].indirect(entries(slot, j0, j1)), hid[t][:, j0:j1])
-
-        page_g = [held([P, PACK * w], BF16, f"page_g{c0}") for c0, w in CHUNKS]
-        page_out = out_1.rearrange("(p t) c -> p t c", t=PACK)
-        page_b = {i: held([P, PACK, CHUNKS[i][1]], BF16, f"page_b{i}") for i in range(STEPPED, len(CHUNKS))}
-
-        def woven(i, t):
-            return page_g[i][:].rearrange("p (m t) -> p m t", t=PACK)[:, :, ORDER[t]]
-
-        def finish(t):
-            nc.sync.dma_start(page_out[:, ORDER[t], :], page[t][:])
-            for i, (c0, w) in enumerate(CHUNKS):
-                if i >= STEPPED:
-                    nc.scalar.copy(page_b[i][:, ORDER[t], :], page[t][:, c0 : c0 + w])
-                elif t < PACK - 1:
-                    nc.scalar.copy(woven(i, t), page[t][:, c0 : c0 + w])
-
-        early = BANKS - HALVES
-        gates = [gate_of(s, s) for s in range(HALVES)]
-        values = [value_of(HALVES + s, s) for s in range(early)]
-        gates.extend(gate_of(s % HALVES, s) for s in range(HALVES, BANKS))
-
-        weighted(0, nc.vector)
-        gated(0)
-        scatter(0, 0, BANK)
-        weighted(1, nc.gpsimd)
-        gated(1)
-        values.extend(value_of(HALVES + s - early, s) for s in range(early, BANKS))
-        gated(2)
-        scatter(0, BANK, S)
-        finish(0)
-        gated(3)
-        gated(4)
-        gated(5)
-        hid.append(held([P, S], F32, "hid_last", "hid0"))
-        for h in range(HALVES):
-            nc.scalar.copy(hid[PACK - 1][:, half(h)], values[BANKS - HALVES + h][:])
+                late.append((s, gate, sums))
 
         w8_w = held([P, N], U32, "w8_w", "v_w0_0")
         nc.sync.dma_start(w8_w[:].bitcast(I32), w8_words[0].rearrange("p c i -> p (c i)").bitcast(I32))
@@ -305,43 +282,66 @@ def tile_list_forked_prefix_page_kernel(
         with nc.allow_non_contiguous_dma(reason="one gain value a partition and output tile"):
             nc.sync.dma_start(gains[:], gain.rearrange("(i p) -> p i", p=P))
 
-        scatter(1, 0, S)
-        finish(1)
-        gated(6)
-        gated(7)
-        scatter(2, 0, S)
-        finish(2)
-        scatter(3, 0, S)
-        finish(3)
+        def scatter(i, j0, n):
+            nc.vector.tensor_copy(page[i][:].indirect(entries(slot, j0, n)), hid[i][:, j0 : j0 + n])
+
+        page_g = [held([P, PACK * w], BF16, f"page_g{c0}") for c0, w in CHUNKS]
+        page_out = out_1.rearrange("(p t) c -> p t c", t=PACK)
+        page_b = {c: held([P, PACK, CHUNKS[c][1]], BF16, f"page_b{c}") for c in range(STEPPED, len(CHUNKS))}
+
+        def woven(c, i):
+            return page_g[c][:].rearrange("p (m t) -> p m t", t=PACK)[:, :, ORDER[i]]
+
+        def rounded(c, i):
+            return woven(c, i) if c < STEPPED else page_b[c][:, ORDER[i], :]
+
+        for i in range(PACK):
+            for j0 in range(0, S, BANK):
+                if i == 0 and j0 == 0:
+                    scatter(i, 0, QUARTER)
+                    scatter(i, QUARTER, QUARTER)
+                else:
+                    scatter(i, j0, BANK)
+            nc.sync.dma_start(page_out[:, ORDER[i], :], page[i][:])
+            if i < PACK - 1:
+                for c, (c0, w) in enumerate(CHUNKS):
+                    nc.scalar.copy(rounded(c, i), page[i][:, c0 : c0 + w])
+            if i == 0:
+                hid.append(held([P, S], F32, "hid_last", "hid0"))
+                for s, gate, sums in late:
+                    gated(s, gate, sums)
 
         page_w = held([P, T2], U32, "page_w")
         page_z = held([P, T2], U8, "page_z")
         y_rows = out_0.rearrange("(i p) c -> p i c", p=P)
         codes_out = out_2[0].rearrange("p m t -> p (m t)").bitcast(I32)
 
-        def quantise_chunk(i):
-            c0, w = CHUNKS[i]
-            if i < STEPPED:
-                nc.vector.tensor_copy(woven(i, PACK - 1), page[PACK - 1][:, c0 : c0 + w])
-            else:
-                nc.vector.tensor_copy(
-                    page_g[i][:].rearrange("p (c m t) -> p c t m", m=PACK, t=PACK),
-                    page_b[i][:].rearrange("p t (c m) -> p c t m", m=PACK),
-                )
+        def round_last(c):
+            c0, w = CHUNKS[c]
+            nc.vector.tensor_copy(rounded(c, PACK - 1), page[PACK - 1][:, c0 : c0 + w])
+
+        def weave(c):
+            nc.vector.tensor_copy(
+                page_g[c][:].rearrange("p (c m t) -> p c t m", m=PACK, t=PACK),
+                page_b[c][:].rearrange("p t (c m) -> p c t m", m=PACK),
+            )
+
+        def quantise(c):
+            c0, w = CHUNKS[c]
             nc.vector.quantize_mx(
-                out=page_w[:, c0 : c0 + w].bitcast(FP8X4), scales=page_z[:, c0 : c0 + w], in_=page_g[i][:]
+                out=page_w[:, c0 : c0 + w].bitcast(FP8X4), scales=page_z[:, c0 : c0 + w], in_=page_g[c][:]
             )
 
         def store_codes(c0, c1):
             nc.sync.dma_start(codes_out[:, c0:c1], page_w[:, c0:c1].bitcast(I32))
 
-        def multiply(turn, i, n, y, on_scalar):
-            c0, w = CHUNKS[i]
+        def multiply(turn, c, n, y, on_scalar):
+            c0, w = CHUNKS[c]
             acc = bank(turn % BANKS)
             nc.tensor.matmul_mx(
                 out=acc[:, 0:w],
-                lhsT=w8_w[:, P * n : P * (n + 1)].bitcast(FP8X4),
-                lhsT_scale=w8_z[:, P * n : P * (n + 1)],
+                lhsT=w8_w[:, block(n)].bitcast(FP8X4),
+                lhsT_scale=w8_z[:, block(n)],
                 rhs=page_w[:, c0 : c0 + w].bitcast(FP8X4),
                 rhs_scale=page_z[:, c0 : c0 + w],
                 start=True, stop=True,
@@ -351,24 +351,26 @@ def tile_list_forked_prefix_page_kernel(
             else:
                 nc.vector.tensor_scalar(y, acc[:, 0:w], gains[:, n : n + 1], None, MULT)
 
-        def solo_chunk(i, n0):
-            c0, w = CHUNKS[i]
-            alike = len([1 for chunk in CHUNKS[:SOLO_CHUNKS] if chunk[1] == w])
-            y = ring.tile([P, PAIR, w], F32, name=f"y{w}", bufs=alike * N_TILES // PAIR)
+        def solo_chunk(c, n0):
+            c0, w = CHUNKS[c]
+            y = placed([P, PAIR, w], F32, f"y{c}_{n0}", AT_Y + 4 * (N_TILES * c0 + n0 * w))
             for n in range(n0, n0 + PAIR):
-                multiply(N_TILES * i + n, i, n, y[:, n - n0, :], True)
+                multiply(N_TILES * c + n, c, n, y[:, n - n0, :], True)
             nc.sync.dma_start(y_rows[:, n0 : n0 + PAIR, c0 : c0 + w], y[:])
 
         def last_chunks(n):
-            y = ring.tile([P, T2 - WIDE], F32, name="y_wide", bufs=N_TILES)
-            for i in range(SOLO_CHUNKS, len(CHUNKS)):
-                c0, w = CHUNKS[i]
-                turn = SOLO_CHUNKS * N_TILES + (len(CHUNKS) - SOLO_CHUNKS) * n + i - SOLO_CHUNKS
-                multiply(turn, i, n, y[:, c0 - WIDE : c0 - WIDE + w], n % 2 == 1)
+            y = placed([P, T2 - WIDE], F32, f"y_wide{n}", AT_Y + 4 * (N_TILES * WIDE + n * (T2 - WIDE)))
+            for c in range(SOLO_CHUNKS, len(CHUNKS)):
+                c0, w = CHUNKS[c]
+                turn = SOLO_CHUNKS * N_TILES + (len(CHUNKS) - SOLO_CHUNKS) * n + c - SOLO_CHUNKS
+                multiply(turn, c, n, y[:, c0 - WIDE : c0 - WIDE + w], n % 2 == 1)
             nc.sync.dma_start(y_rows[:, n, WIDE:T2], y[:])
 
-        for i in range(len(CHUNKS)):
-            quantise_chunk(i)
+        for c in range(len(CHUNKS)):
+            round_last(c)
+            if c >= STEPPED:
+                weave(c)
+            quantise(c)
         store_codes(0, 256)
         solo_chunk(0, 0)
         store_codes(256, 768)

@@ -32,7 +32,10 @@ LIST_ROWS = 16
 N_TILES = N // P
 
 ORDER = (0, 2, 3, 1)
-STEPS = [(i, j) for i in range(PACK) for j in range(0, S, BANK)]
+STEPS = [(0, 0), (1, 0), (0, BANK), (2, 0), (1, BANK), (3, 0), (2, BANK), (3, BANK)]
+
+LOGIT_BANKS = (0, 3, 5, 6, 7, 0, 1, 2)
+VALUE_BANKS = (1, 3, 4, 5, 6, 7, 4, 0)
 
 CHUNKS = [(0, 256), (256, 512), (768, 512), (1280, 512), (1792, 256)]
 SOLO_CHUNKS = 2
@@ -42,12 +45,12 @@ PAIR = 2
 
 KIB = 1024
 LAP = 64
-AT_W1_RAW = (0, 8 * KIB)
-AT_GATES = (8 * KIB, 10 * KIB)
-AT_TABLE0 = 8 * KIB - LAP
-AT_PAGE = (16 * KIB, 24 * KIB, 32 * KIB, 40 * KIB)
-AT_TABLE1 = 32 * KIB - LAP
-AT_V_Z_ROWS = 40 * KIB
+AT_GATES = 0
+AT_TABLE0 = 8 * KIB
+AT_W1_RAW = (24 * KIB, 8 * KIB)
+AT_PAGE = (16 * KIB, 32 * KIB, 40 * KIB, 24 * KIB)
+AT_TABLE1 = 32 * KIB
+AT_V_Z_ROWS = 32 * KIB - LAP
 AT_WGS_TURNED = (48 * KIB, 56 * KIB)
 AT_W1_BF16 = (64 * KIB, 68 * KIB)
 AT_FACTOR = 68 * KIB
@@ -75,11 +78,11 @@ def tile_list_forked_prefix_page_kernel(
         def bank(b):
             return psum.tile([P, BANK], F32, name=f"bank{b}")
 
-        def z_partitions(q):
-            return slice(QUAD * q, QUAD * q + Z_ROWS)
+        def z_partitions(r):
+            return slice(r, P, QUAD)
 
-        def z_rows(q):
-            return slice(Z_ROWS * q, Z_ROWS * (q + 1))
+        def z_rows(r, a=0):
+            return slice(Z_ROWS * QUADS * a + r, Z_ROWS * QUADS * (a + 1), Z_ROWS)
 
         def half(h):
             return slice(BANK * h, BANK * (h + 1))
@@ -151,12 +154,8 @@ def tile_list_forked_prefix_page_kernel(
         nc.vector.tensor_copy(z_rows_all[:, 0:S].bitcast(I32), v_z_rows[:].bitcast(I32))
 
         def place_scales(a):
-            for q in range(QUADS):
-                row = Z_ROWS * (QUADS * a + q)
-                nc.sync.dma_start(
-                    z_all[a][z_partitions(q), :].bitcast(I32),
-                    z_rows_all[row : row + Z_ROWS, :].bitcast(I32),
-                )
+            for r in range(Z_ROWS):
+                nc.sync.dma_start(z_all[a][z_partitions(r), :].bitcast(I32), z_rows_all[z_rows(r, a), :].bitcast(I32))
 
         tab_w.append(placed([P, T], U32, "tab_w1", AT_TABLE1))
         for a in range(PASSES):
@@ -213,7 +212,7 @@ def tile_list_forked_prefix_page_kernel(
                 in_=w1_b[a][:, K_PASS * t0 : K_PASS * t1],
             )
 
-        hid = [held([P, S], F32, f"hid{i}") for i in range(PACK - 1)]
+        hid = [held([P, BANK], F32, f"hid{s}") for s in range(len(STEPS) - 1)]
 
         def product(b, i, j0, n, words, dtype, width, scales):
             t = ORDER[i]
@@ -231,22 +230,21 @@ def tile_list_forked_prefix_page_kernel(
 
         def gate_of(s, gate):
             i, j0 = STEPS[s]
-            b = (2 * s + min(s, 1)) % BANKS
-            logit = product(b, i, j0, BANK, lambda a: w4_w[:, a, :], FP4X4, 2 * P, lambda a: z_all[a][:, S : S + H])
-            nc.scalar.activation(gate[:], logit, ACT.Sigmoid, bias=bias[:, ORDER[i] : ORDER[i] + 1])
+            logit = product(LOGIT_BANKS[s], i, j0, BANK, lambda a: w4_w[:, a, :], FP4X4, 2 * P, lambda a: z_all[a][:, S : S + H])
+            nc.scalar.activation(gate, logit, ACT.Sigmoid, bias=bias[:, ORDER[i] : ORDER[i] + 1])
 
         def value_of(b, i, j0, n):
             return product(b, i, j0, n, lambda a: w1_w[a][:], FP8X4, P, lambda a: w1_z[a][:])
 
         first = held([P, BANK], F32, "first")
-        gate_of(0, first)
+        gate_of(0, first[:])
         round_w1(nc.vector.tensor_copy, 0, 0, 2)
         round_w1(nc.scalar.copy, 0, 2, PACK)
-        quantise_w1(0, 0, 2)
         nc.vector.tensor_tensor(first[:], first[:], weights[:, 0, 0:BANK], MULT)
-        quantise_w1(0, 2, PACK)
+        quantise_w1(0, 0, 2)
         round_w1(nc.vector.tensor_copy, 1, 0, 2)
         round_w1(nc.scalar.copy, 1, 2, PACK)
+        quantise_w1(0, 2, PACK)
         quantise_w1(1, 0, 1)
         quantise_w1(1, 1, 2)
         quantise_w1(1, 2, PACK)
@@ -257,33 +255,32 @@ def tile_list_forked_prefix_page_kernel(
 
         def gated(s, gate, sums):
             i, j0 = STEPS[s]
-            value = hid[i][:, j0 : j0 + BANK]
+            value = hid[s][:]
             factor = placed([P, BANK], F32, f"factor{s}", AT_FACTOR)
-            nc.gpsimd.tensor_tensor(factor[:], gate[:], weights[:, i, j0 : j0 + BANK], MULT)
+            nc.gpsimd.tensor_tensor(factor[:], gate, weights[:, i, j0 : j0 + BANK], MULT)
             nc.scalar.copy(value, sums)
             nc.gpsimd.tensor_tensor(value, value, factor[:], MULT)
 
-        late = []
+        gates = placed([P, len(STEPS) - 1, BANK], F32, "gates", AT_GATES)
         for s in range(1, len(STEPS)):
             i, j0 = STEPS[s]
-            gate = placed([P, BANK], F32, f"gate{s}", AT_GATES[s % 2] + (4 * KIB if i == PACK - 1 else 0))
+            gate = gates[:, s - 1, :]
             gate_of(s, gate)
-            sums = value_of((2 * s + 2) % BANKS, i, j0, BANK)
-            if i < PACK - 1:
+            sums = value_of(VALUE_BANKS[s], i, j0, BANK)
+            if s < len(STEPS) - 1:
                 gated(s, gate, sums)
-            else:
-                late.append((s, gate, sums))
 
         w8_w = held([P, N], U32, "w8_w", "v_w0_0")
         nc.sync.dma_start(w8_w[:].bitcast(I32), w8_words[0].rearrange("p c i -> p (c i)").bitcast(I32))
-        for q in range(QUADS):
-            nc.sync.dma_start(z_all[1][z_partitions(q), 0:N].bitcast(I32), w8_scales[0, z_rows(q), :].bitcast(I32))
+        for r in range(Z_ROWS):
+            nc.sync.dma_start(z_all[1][z_partitions(r), 0:N].bitcast(I32), w8_scales[0, z_rows(r), :].bitcast(I32))
         gains = held([P, N_TILES], F32, "gains", "v_w0_1")
         with nc.allow_non_contiguous_dma(reason="one gain value a partition and output tile"):
             nc.sync.dma_start(gains[:], gain.rearrange("(i p) -> p i", p=P))
 
-        def scatter(i, j0, n):
-            nc.vector.tensor_copy(page[i][:].indirect(entries(slot, j0, n)), hid[i][:, j0 : j0 + n])
+        def scatter(s, c0, n):
+            i, j0 = STEPS[s]
+            nc.vector.tensor_copy(page[i][:].indirect(entries(slot, j0 + c0, n)), hid[s][:, c0 : c0 + n])
 
         page_g = [held([P, PACK * w], BF16, f"page_g{c0}") for c0, w in CHUNKS]
         page_out = out_1.rearrange("(p t) c -> p t c", t=PACK)
@@ -295,21 +292,22 @@ def tile_list_forked_prefix_page_kernel(
         def rounded(c, i):
             return woven(c, i) if c < STEPPED else page_b[c][:, ORDER[i], :]
 
-        for i in range(PACK):
-            for j0 in range(0, S, BANK):
-                if i == 0 and j0 == 0:
-                    scatter(i, 0, QUARTER)
-                    scatter(i, QUARTER, QUARTER)
-                else:
-                    scatter(i, j0, BANK)
+        def finish(i):
             nc.sync.dma_start(page_out[:, ORDER[i], :], page[i][:])
             if i < PACK - 1:
                 for c, (c0, w) in enumerate(CHUNKS):
                     nc.scalar.copy(rounded(c, i), page[i][:, c0 : c0 + w])
-            if i == 0:
-                hid.append(held([P, S], F32, "hid_last", "hid0"))
-                for s, gate, sums in late:
-                    gated(s, gate, sums)
+
+        scatter(0, 0, QUARTER)
+        scatter(0, QUARTER, QUARTER)
+        for s in range(1, len(STEPS)):
+            i, j0 = STEPS[s]
+            scatter(s, 0, BANK)
+            if j0:
+                finish(i)
+            if j0 and i == 0:
+                hid.append(held([P, BANK], F32, "hid_last", f"hid{s}"))
+                gated(len(STEPS) - 1, gate, sums)
 
         page_w = held([P, T2], U32, "page_w")
         page_z = held([P, T2], U8, "page_z")
@@ -381,7 +379,7 @@ def tile_list_forked_prefix_page_kernel(
         solo_chunk(1, 2)
         store_codes(1280, T2)
         solo_chunk(1, 4)
-        for q in range(QUADS):
-            nc.sync.dma_start(out_3[0, z_rows(q), :].bitcast(I32), page_z[z_partitions(q), :].bitcast(I32))
+        for r in range(Z_ROWS):
+            nc.sync.dma_start(out_3[0, z_rows(r), :].bitcast(I32), page_z[z_partitions(r), :].bitcast(I32))
         for n in range(N_TILES):
             last_chunks(n)

@@ -294,8 +294,8 @@ def tile_list_forked_prefix_page_kernel(
 
         def finish(i):
             nc.sync.dma_start(page_out[:, ORDER[i], :], page[i][:])
-            if i < PACK - 1:
-                for c, (c0, w) in enumerate(CHUNKS):
+            for c, (c0, w) in enumerate(CHUNKS):
+                if i < PACK - 1 or c >= STEPPED:
                     nc.scalar.copy(rounded(c, i), page[i][:, c0 : c0 + w])
 
         scatter(0, 0, QUARTER)
@@ -361,12 +361,13 @@ def tile_list_forked_prefix_page_kernel(
             for c in range(SOLO_CHUNKS, len(CHUNKS)):
                 c0, w = CHUNKS[c]
                 turn = SOLO_CHUNKS * N_TILES + (len(CHUNKS) - SOLO_CHUNKS) * n + c - SOLO_CHUNKS
-                multiply(turn, c, n, y[:, c0 - WIDE : c0 - WIDE + w], n % 2 == 1)
+                multiply(turn, c, n, y[:, c0 - WIDE : c0 - WIDE + w], n % 2 == 0)
             nc.sync.dma_start(y_rows[:, n, WIDE:T2], y[:])
 
         for c in range(len(CHUNKS)):
-            round_last(c)
-            if c >= STEPPED:
+            if c < STEPPED:
+                round_last(c)
+            else:
                 weave(c)
             quantise(c)
         store_codes(0, 256)
@@ -377,8 +378,8 @@ def tile_list_forked_prefix_page_kernel(
         store_codes(768, 1280)
         solo_chunk(1, 0)
         solo_chunk(1, 2)
-        store_codes(1280, T2)
         solo_chunk(1, 4)
+        store_codes(1280, T2)
         for r in range(Z_ROWS):
             nc.sync.dma_start(out_3[0, z_rows(r), :].bitcast(I32), page_z[z_partitions(r), :].bitcast(I32))
         for n in range(N_TILES):

@@ -32,10 +32,11 @@ LIST_ROWS = 16
 N_TILES = N // P
 
 ORDER = (0, 2, 3, 1)
-STEPS = [(0, 0), (1, 0), (0, BANK), (2, 0), (1, BANK), (3, 0), (2, BANK), (3, BANK)]
+STEPS = [(0, 0), (1, 0), (2, 0), (0, BANK), (1, BANK), (3, 0), (2, BANK), (3, BANK)]
 
-LOGIT_BANKS = (0, 3, 5, 6, 7, 0, 1, 2)
-VALUE_BANKS = (1, 3, 4, 5, 6, 7, 4, 0)
+LOGIT_BANKS = (0, 3, 0, 0, 3, 2, 4, 6)
+VALUE_BANKS = (1, 3, 2, 0, 3, 5, 7, 1)
+SPREAD_BANKS = ((1, 2, 3, 4), (4, 5, 6, 7))
 
 CHUNKS = [(0, 256), (256, 512), (768, 512), (1280, 512), (1792, 256)]
 SOLO_CHUNKS = 2
@@ -45,14 +46,16 @@ PAIR = 2
 
 KIB = 1024
 LAP = 64
-AT_GATES = 0
-AT_TABLE0 = 8 * KIB
-AT_W1_RAW = (24 * KIB, 8 * KIB)
-AT_PAGE = (16 * KIB, 32 * KIB, 40 * KIB, 24 * KIB)
+AT_TABLE0 = 8 * KIB - LAP
+AT_WGS_LATE = 8 * KIB
+AT_GATES = 10 * KIB
+AT_W1_RAW = (24 * KIB, 10 * KIB)
+AT_PAGE = (0, 32 * KIB, 40 * KIB, 24 * KIB)
 AT_TABLE1 = 32 * KIB
 AT_V_Z_ROWS = 32 * KIB - LAP
 AT_WGS_TURNED = (48 * KIB, 56 * KIB)
-AT_W1_BF16 = (64 * KIB, 68 * KIB)
+AT_W1_BF16 = (46 * KIB, 64 * KIB)
+AT_W1_BF16_UPPER = 68 * KIB
 AT_FACTOR = 68 * KIB
 AT_TAB_Z = 72 * KIB
 AT_W4_W = 72 * KIB
@@ -122,28 +125,34 @@ def tile_list_forked_prefix_page_kernel(
         bias = held([P, PACK], F32, "bias")
         nc.scalar.dma_start(bias[:], bg.rearrange("(p t) -> p t", t=PACK))
         w4_raw = held([P, PASSES, 2 * H], U8, "w4_raw")
-        nc.scalar.dma_start(w4_raw[:].bitcast(I32), w4_words.rearrange("a p c -> p a c").bitcast(I32))
         nc.sync.dma_start(slot[:], offs2)
-        wgs_raw = held([P, S], F32, "wgs_raw")
-        nc.sync.dma_start(wgs_raw[:], wgs)
+        wgs_raw = [held([P, BANK], F32, "wgs_raw0")]
+        nc.sync.dma_start(wgs_raw[0][:], wgs[:, half(0)])
         tab_w = [placed([P, T], U32, "tab_w0", AT_TABLE0)]
         load_table(0, 0, T)
+        nc.sync.dma_start(w4_raw[:].bitcast(I32), w4_words.rearrange("a p c -> p a c").bitcast(I32))
 
         weights = held([P, PACK, S], F32, "weights")
-        for h in range(HALVES):
+
+        def spread_wgs(h):
             turned = bank(h)
             for b in range(PACK):
-                nc.tensor.transpose(turned[:, block(b)], wgs_raw[:, block(PACK * h + b)], identity[:])
+                nc.tensor.transpose(turned[:, block(b)], wgs_raw[h][:, block(b)], identity[:])
             spread = placed([P, PACK, PACK, QUADS, QUAD], F32, f"wgs_spread{h}", AT_WGS_TURNED[h])
-            rows = turned[:].rearrange("j (b m t) -> j b t m", b=PACK, t=PACK)
-            nc.scalar.copy(spread[:], rows.unsqueeze(3).broadcast_to([P, PACK, PACK, QUADS, QUAD]))
+            rows = turned[:].rearrange("j (b m t) -> j b m t", b=PACK, t=PACK)
+            nc.scalar.copy(
+                spread[:].rearrange("j b t q m -> j b q m t"),
+                rows.unsqueeze(2).broadcast_to([P, PACK, QUADS, QUAD, PACK]),
+            )
             for i in range(PACK):
-                back = bank(HALVES + (PACK * h + i) % (BANKS - HALVES))
+                back = bank(SPREAD_BANKS[h][i])
                 for b in range(PACK):
                     nc.tensor.transpose(
                         back[:, block(b)], spread[:, b, ORDER[i]].rearrange("j q m -> j (q m)"), identity[:]
                     )
                 nc.scalar.copy(weights[:, i, half(h)], back[:])
+
+        spread_wgs(0)
 
         v_z_rows = placed([P, S], U8, "v_z_rows", AT_V_Z_ROWS)
         nc.vector.tensor_copy(
@@ -159,8 +168,8 @@ def tile_list_forked_prefix_page_kernel(
 
         tab_w.append(placed([P, T], U32, "tab_w1", AT_TABLE1))
         for a in range(PASSES):
-            place_scales(a)
             load_table(1, a * T // PASSES, (a + 1) * T // PASSES)
+            place_scales(a)
 
         w4_w = placed([P, PASSES, 2 * H], U8, "w4_w", AT_W4_W)
         nc.vector.tensor_copy(
@@ -191,67 +200,76 @@ def tile_list_forked_prefix_page_kernel(
 
         w1_raw = [load_w1(a) for a in range(PASSES)]
         page = [load_page(0)]
-        for h in range(HALVES):
-            gather_words(1, BANK * h, BANK)
-        page.extend(load_page(i) for i in range(1, PACK))
+        wgs_raw.append(placed([P, BANK], F32, "wgs_raw1", AT_WGS_LATE))
+        nc.sync.dma_start(wgs_raw[1][:], wgs[:, half(1)])
+        gather_words(1, 0, QUARTER)
+        gather_words(1, QUARTER, QUARTER)
+        gather_words(1, BANK, BANK)
 
-        w1_w = [held([P, H], U32, f"w1_w{a}") for a in range(PASSES)]
-        w1_z = [held([P, H], U8, f"w1_z{a}") for a in range(PASSES)]
-        w1_b = [placed([P, PACK * H], BF16, f"w1_b{a}", AT_W1_BF16[a]) for a in range(PASSES)]
+        w1_w = held([P, PASSES * H], U32, "w1_w")
+        w1_z = held([P, PASSES * H], U8, "w1_z")
+        bias_first = placed([P, 1], F32, "bias_first", AT_W1_BF16_UPPER)
+        nc.vector.tensor_copy(bias_first[:], bias[:, ORDER[0] : ORDER[0] + 1])
 
-        def round_w1(copy, a, t0, t1):
+        def w1_block(a, t):
+            return block(PACK * (t // 2) + 2 * a + t % 2)
+
+        def round_w1(copy, rounded_pair, a, t0):
             copy(
-                w1_b[a][:].rearrange("p (t m j) -> p m j t", t=PACK, j=PACK)[:, :, :, t0:t1],
-                w1_raw[a][:].rearrange("p j (m t) -> p m j t", t=PACK)[:, :, :, t0:t1],
+                rounded_pair.rearrange("p (t m j) -> p m j t", t=2, j=PACK),
+                w1_raw[a][:].rearrange("p j (m t) -> p m j t", t=PACK)[:, :, :, t0 : t0 + 2],
             )
 
-        def quantise_w1(a, t0, t1):
-            nc.vector.quantize_mx(
-                out=w1_w[a][:, P * t0 : P * t1].bitcast(FP8X4),
-                scales=w1_z[a][:, P * t0 : P * t1],
-                in_=w1_b[a][:, K_PASS * t0 : K_PASS * t1],
-            )
+        def quantise_w1(rounded_rows, a, t0):
+            c0 = w1_block(a, t0).start
+            columns = slice(c0, c0 + rounded_rows.shape[1] // PACK)
+            nc.vector.quantize_mx(out=w1_w[:, columns].bitcast(FP8X4), scales=w1_z[:, columns], in_=rounded_rows)
 
         hid = [held([P, BANK], F32, f"hid{s}") for s in range(len(STEPS) - 1)]
 
-        def product(b, i, j0, n, words, dtype, width, scales):
-            t = ORDER[i]
+        def product(b, j0, n, words, dtype, scales):
             acc = bank(b)
             for a in range(PASSES):
                 nc.tensor.matmul_mx(
                     out=acc[:, 0:n],
-                    lhsT=words(a)[:, width * t : width * (t + 1)].bitcast(dtype),
-                    lhsT_scale=scales(a)[:, block(t)],
+                    lhsT=words(a).bitcast(dtype),
+                    lhsT_scale=scales(a),
                     rhs=picked_words(a, j0, n).bitcast(FP8X4),
                     rhs_scale=z_all[a][:, j0 : j0 + n],
                     start=(a == 0), stop=(a == PASSES - 1),
                 )
             return acc[:, 0:n]
 
-        def gate_of(s, gate):
-            i, j0 = STEPS[s]
-            logit = product(LOGIT_BANKS[s], i, j0, BANK, lambda a: w4_w[:, a, :], FP4X4, 2 * P, lambda a: z_all[a][:, S : S + H])
-            nc.scalar.activation(gate, logit, ACT.Sigmoid, bias=bias[:, ORDER[i] : ORDER[i] + 1])
+        def gate_of(b, i, j0, gate, row_bias):
+            t = ORDER[i]
+            logit = product(
+                b, j0, gate.shape[1], lambda a: w4_w[:, a, 2 * P * t : 2 * P * (t + 1)], FP4X4,
+                lambda a: z_all[a][:, S + P * t : S + P * (t + 1)],
+            )
+            nc.scalar.activation(gate, logit, ACT.Sigmoid, bias=row_bias)
 
         def value_of(b, i, j0, n):
-            return product(b, i, j0, n, lambda a: w1_w[a][:], FP8X4, P, lambda a: w1_z[a][:])
+            t = ORDER[i]
+            return product(b, j0, n, lambda a: w1_w[:, w1_block(a, t)], FP8X4, lambda a: w1_z[:, w1_block(a, t)])
 
         first = held([P, BANK], F32, "first")
-        gate_of(0, first[:])
-        round_w1(nc.vector.tensor_copy, 0, 0, 2)
-        round_w1(nc.scalar.copy, 0, 2, PACK)
+        gate_of(0, 0, 0, first[:, 0:QUARTER], bias_first[:])
+        gate_of(4, 0, QUARTER, first[:, QUARTER:BANK], bias[:, ORDER[0] : ORDER[0] + 1])
+        lower = [placed([P, 2 * K_PASS], BF16, f"w1_lower{a}", AT_W1_BF16[a]) for a in range(PASSES)]
+        upper = placed([P, PASSES, 2 * K_PASS], BF16, "w1_upper", AT_W1_BF16_UPPER)
+        round_w1(nc.vector.tensor_copy, lower[0][:], 0, 0)
+        round_w1(nc.scalar.copy, upper[:, 0, :], 0, 2)
         nc.vector.tensor_tensor(first[:], first[:], weights[:, 0, 0:BANK], MULT)
-        quantise_w1(0, 0, 2)
-        round_w1(nc.vector.tensor_copy, 1, 0, 2)
-        round_w1(nc.scalar.copy, 1, 2, PACK)
-        quantise_w1(0, 2, PACK)
-        quantise_w1(1, 0, 1)
-        quantise_w1(1, 1, 2)
-        quantise_w1(1, 2, PACK)
+        quantise_w1(lower[0][:], 0, 0)
+        round_w1(nc.vector.tensor_copy, lower[1][:], 1, 0)
+        round_w1(nc.scalar.copy, upper[:, 1, :], 1, 2)
+        quantise_w1(lower[1][:, 0:K_PASS], 1, 0)
+        quantise_w1(lower[1][:, K_PASS : 2 * K_PASS], 1, 1)
+        quantise_w1(upper[:].rearrange("p a c -> p (a c)"), 0, 2)
+        page.extend(load_page(i) for i in range(1, PACK))
 
         nc.vector.tensor_tensor(hid[0][:, 0:QUARTER], value_of(1, 0, 0, QUARTER), first[:, 0:QUARTER], MULT)
-        nc.scalar.copy(hid[0][:, QUARTER:BANK], value_of(2, 0, QUARTER, QUARTER))
-        nc.gpsimd.tensor_tensor(hid[0][:, QUARTER:BANK], hid[0][:, QUARTER:BANK], first[:, QUARTER:BANK], MULT)
+        nc.vector.tensor_tensor(hid[0][:, QUARTER:BANK], value_of(2, 0, QUARTER, QUARTER), first[:, QUARTER:BANK], MULT)
 
         def gated(s, gate, sums):
             i, j0 = STEPS[s]
@@ -264,8 +282,10 @@ def tile_list_forked_prefix_page_kernel(
         gates = placed([P, len(STEPS) - 1, BANK], F32, "gates", AT_GATES)
         for s in range(1, len(STEPS)):
             i, j0 = STEPS[s]
+            if (i, j0) == (0, BANK):
+                spread_wgs(1)
             gate = gates[:, s - 1, :]
-            gate_of(s, gate)
+            gate_of(LOGIT_BANKS[s], i, j0, gate, bias[:, ORDER[i] : ORDER[i] + 1])
             sums = value_of(VALUE_BANKS[s], i, j0, BANK)
             if s < len(STEPS) - 1:
                 gated(s, gate, sums)
@@ -298,9 +318,7 @@ def tile_list_forked_prefix_page_kernel(
                 if i < PACK - 1 or c >= STEPPED:
                     nc.scalar.copy(rounded(c, i), page[i][:, c0 : c0 + w])
 
-        scatter(0, 0, QUARTER)
-        scatter(0, QUARTER, QUARTER)
-        for s in range(1, len(STEPS)):
+        for s in range(len(STEPS)):
             i, j0 = STEPS[s]
             scatter(s, 0, BANK)
             if j0:

@@ -39,10 +39,7 @@ VALUE_BANKS = (1, 3, 2, 0, 3, 5, 7, 1)
 SPREAD_BANKS = ((1, 2, 3, 4), (4, 5, 6, 7))
 
 CHUNKS = [(0, 256), (256, 512), (768, 512), (1280, 512), (1792, 256)]
-SOLO_CHUNKS = 2
-WIDE = CHUNKS[SOLO_CHUNKS][0]
 STEPPED = 2
-PAIR = 2
 
 KIB = 1024
 LAP = 64
@@ -351,36 +348,31 @@ def tile_list_forked_prefix_page_kernel(
         def store_codes(c0, c1):
             nc.sync.dma_start(codes_out[:, c0:c1], page_w[:, c0:c1].bitcast(I32))
 
-        def multiply(turn, c, n, y, on_scalar):
-            c0, w = CHUNKS[c]
-            acc = bank(turn % BANKS)
-            nc.tensor.matmul_mx(
-                out=acc[:, 0:w],
-                lhsT=w8_w[:, block(n)].bitcast(FP8X4),
-                lhsT_scale=w8_z[:, block(n)],
-                rhs=page_w[:, c0 : c0 + w].bitcast(FP8X4),
-                rhs_scale=page_z[:, c0 : c0 + w],
-                start=True, stop=True,
-            )
-            if on_scalar:
-                nc.scalar.activation(y, acc[:, 0:w], ACT.Copy, scale=gains[:, n : n + 1])
-            else:
-                nc.vector.tensor_scalar(y, acc[:, 0:w], gains[:, n : n + 1], None, MULT)
+        y = placed([P, N_TILES, T2], F32, "y", AT_Y)
+        turns = list(range(N_TILES * len(CHUNKS)))
 
-        def solo_chunk(c, n0):
-            c0, w = CHUNKS[c]
-            y = placed([P, PAIR, w], F32, f"y{c}_{n0}", AT_Y + 4 * (N_TILES * c0 + n0 * w))
-            for n in range(n0, n0 + PAIR):
-                multiply(N_TILES * c + n, c, n, y[:, n - n0, :], True)
-            nc.sync.dma_start(y_rows[:, n0 : n0 + PAIR, c0 : c0 + w], y[:])
-
-        def last_chunks(n):
-            y = placed([P, T2 - WIDE], F32, f"y_wide{n}", AT_Y + 4 * (N_TILES * WIDE + n * (T2 - WIDE)))
-            for c in range(SOLO_CHUNKS, len(CHUNKS)):
+        def multiply(n, chunks, on_scalar):
+            for c in chunks:
                 c0, w = CHUNKS[c]
-                turn = SOLO_CHUNKS * N_TILES + (len(CHUNKS) - SOLO_CHUNKS) * n + c - SOLO_CHUNKS
-                multiply(turn, c, n, y[:, c0 - WIDE : c0 - WIDE + w], n % 2 == 0)
-            nc.sync.dma_start(y_rows[:, n, WIDE:T2], y[:])
+                acc = bank(turns.pop(0) % BANKS)
+                nc.tensor.matmul_mx(
+                    out=acc[:, 0:w],
+                    lhsT=w8_w[:, block(n)].bitcast(FP8X4),
+                    lhsT_scale=w8_z[:, block(n)],
+                    rhs=page_w[:, c0 : c0 + w].bitcast(FP8X4),
+                    rhs_scale=page_z[:, c0 : c0 + w],
+                    start=True, stop=True,
+                )
+                if on_scalar:
+                    nc.scalar.activation(y[:, n, c0 : c0 + w], acc[:, 0:w], ACT.Copy, scale=gains[:, n : n + 1])
+                else:
+                    nc.vector.tensor_scalar(y[:, n, c0 : c0 + w], acc[:, 0:w], gains[:, n : n + 1], None, MULT)
+
+        def store_rows(n0, n1, c0, c1):
+            nc.sync.dma_start(y_rows[:, n0:n1, c0:c1], y[:, n0:n1, c0:c1])
+
+        def store_chunk_codes(c):
+            store_codes(CHUNKS[c][0], sum(CHUNKS[c]))
 
         for c in range(len(CHUNKS)):
             if c < STEPPED:
@@ -388,17 +380,23 @@ def tile_list_forked_prefix_page_kernel(
             else:
                 weave(c)
             quantise(c)
-        store_codes(0, 256)
-        solo_chunk(0, 0)
-        store_codes(256, 768)
-        solo_chunk(0, 2)
-        solo_chunk(0, 4)
-        store_codes(768, 1280)
-        solo_chunk(1, 0)
-        solo_chunk(1, 2)
-        solo_chunk(1, 4)
-        store_codes(1280, T2)
+        last = len(CHUNKS)
+        store_chunk_codes(0)
+        for n in range(3):
+            multiply(n, [0], True)
+        store_rows(0, 3, 0, CHUNKS[1][0])
+        store_chunk_codes(1)
+        for n in (3, 4):
+            multiply(n, [0, 1], True)
+            store_rows(n, n + 1, 0, CHUNKS[2][0])
+        store_chunk_codes(2)
+        multiply(5, [0, 1, 2], True)
+        store_rows(5, 6, 0, CHUNKS[3][0])
+        for n in range(3):
+            multiply(n, [1], True)
+        store_codes(CHUNKS[3][0], T2)
         for r in range(Z_ROWS):
             nc.sync.dma_start(out_3[0, z_rows(r), :].bitcast(I32), page_z[z_partitions(r), :].bitcast(I32))
-        for n in range(N_TILES):
-            last_chunks(n)
+        for n, c, cut, on_scalar in ((5, 3, 3, True), (3, 2, 2, False), (0, 2, 1, True), (4, 2, 2, False), (1, 2, 1, True), (2, 2, 1, False)):
+            multiply(n, range(c, last), on_scalar)
+            store_rows(n, n + 1, CHUNKS[cut][0], T2)

@@ -384,19 +384,20 @@ def tile_list_forked_prefix_page_kernel(
         store_chunk_codes(0)
         for n in range(3):
             multiply(n, [0], True)
-        store_rows(0, 3, 0, CHUNKS[1][0])
+        store_rows(0, 1, 0, CHUNKS[1][0])
         store_chunk_codes(1)
+        store_rows(1, 3, 0, CHUNKS[1][0])
         for n in (3, 4):
             multiply(n, [0, 1], True)
             store_rows(n, n + 1, 0, CHUNKS[2][0])
         store_chunk_codes(2)
         multiply(5, [0, 1, 2], True)
         store_rows(5, 6, 0, CHUNKS[3][0])
-        for n in range(3):
-            multiply(n, [1], True)
+        multiply(0, [1, 2], True)
+        store_rows(0, 1, CHUNKS[1][0], CHUNKS[3][0])
         store_codes(CHUNKS[3][0], T2)
         for r in range(Z_ROWS):
             nc.sync.dma_start(out_3[0, z_rows(r), :].bitcast(I32), page_z[z_partitions(r), :].bitcast(I32))
-        for n, c, cut, on_scalar in ((5, 3, 3, True), (3, 2, 2, False), (0, 2, 1, True), (4, 2, 2, False), (1, 2, 1, True), (2, 2, 1, False)):
-            multiply(n, range(c, last), on_scalar)
+        for n, cut, on_scalar in ((5, 3, True), (3, 2, False), (0, 3, True), (4, 2, False), (1, 1, True), (2, 1, False)):
+            multiply(n, range(cut, last), on_scalar)
             store_rows(n, n + 1, CHUNKS[cut][0], T2)

@@ -38,7 +38,7 @@ LOGIT_BANKS = (0, 3, 0, 0, 3, 2, 4, 6)
 VALUE_BANKS = (1, 3, 2, 0, 3, 5, 7, 1)
 SPREAD_BANKS = ((1, 2, 3, 4), (4, 5, 6, 7))
 
-CHUNKS = [(0, 256), (256, 512), (768, 512), (1280, 512), (1792, 256)]
+CHUNKS = [(0, QUARTER), (QUARTER, QUARTER)] + [(c0, BANK) for c0 in range(BANK, T2, BANK)]
 STEPPED = 2
 
 KIB = 1024
@@ -205,8 +205,6 @@ def tile_list_forked_prefix_page_kernel(
 
         w1_w = held([P, PASSES * H], U32, "w1_w")
         w1_z = held([P, PASSES * H], U8, "w1_z")
-        bias_first = placed([P, 1], F32, "bias_first", AT_W1_BF16_UPPER)
-        nc.vector.tensor_copy(bias_first[:], bias[:, ORDER[0] : ORDER[0] + 1])
 
         def w1_block(a, t):
             return block(PACK * (t // 2) + 2 * a + t % 2)
@@ -250,7 +248,7 @@ def tile_list_forked_prefix_page_kernel(
             return product(b, j0, n, lambda a: w1_w[:, w1_block(a, t)], FP8X4, lambda a: w1_z[:, w1_block(a, t)])
 
         first = held([P, BANK], F32, "first")
-        gate_of(0, 0, 0, first[:, 0:QUARTER], bias_first[:])
+        gate_of(0, 0, 0, first[:, 0:QUARTER], bias[:, ORDER[0] : ORDER[0] + 1])
         gate_of(4, 0, QUARTER, first[:, QUARTER:BANK], bias[:, ORDER[0] : ORDER[0] + 1])
         lower = [placed([P, 2 * K_PASS], BF16, f"w1_lower{a}", AT_W1_BF16[a]) for a in range(PASSES)]
         upper = placed([P, PASSES, 2 * K_PASS], BF16, "w1_upper", AT_W1_BF16_UPPER)
@@ -380,24 +378,26 @@ def tile_list_forked_prefix_page_kernel(
             else:
                 weave(c)
             quantise(c)
-        last = len(CHUNKS)
         store_chunk_codes(0)
-        for n in range(3):
+        for n in range(2):
             multiply(n, [0], True)
-        store_rows(0, 1, 0, CHUNKS[1][0])
+        store_rows(0, 2, 0, QUARTER)
         store_chunk_codes(1)
-        store_rows(1, 3, 0, CHUNKS[1][0])
-        for n in (3, 4):
+        for n in range(2, N_TILES):
             multiply(n, [0, 1], True)
-            store_rows(n, n + 1, 0, CHUNKS[2][0])
+            store_rows(n, n + 1, 0, BANK)
         store_chunk_codes(2)
-        multiply(5, [0, 1, 2], True)
-        store_rows(5, 6, 0, CHUNKS[3][0])
-        multiply(0, [1, 2], True)
-        store_rows(0, 1, CHUNKS[1][0], CHUNKS[3][0])
-        store_codes(CHUNKS[3][0], T2)
+        for n in range(2):
+            multiply(n, [1, 2], True)
+            store_rows(n, n + 1, QUARTER, 2 * BANK)
+        store_codes(2 * BANK, T2)
+        for n0 in range(2, N_TILES, 2):
+            for n in (n0, n0 + 1):
+                multiply(n, [2], True)
+            store_rows(n0, n0 + 2, BANK, 2 * BANK)
         for r in range(Z_ROWS):
             nc.sync.dma_start(out_3[0, z_rows(r), :].bitcast(I32), page_z[z_partitions(r), :].bitcast(I32))
-        for n, cut, on_scalar in ((5, 3, True), (3, 2, False), (0, 3, True), (4, 2, False), (1, 1, True), (2, 1, False)):
-            multiply(n, range(cut, last), on_scalar)
-            store_rows(n, n + 1, CHUNKS[cut][0], T2)
+        for n0 in range(0, N_TILES, 2):
+            for n in (n0, n0 + 1):
+                multiply(n, [3, 4], n >= 4)
+            store_rows(n0, n0 + 2, 2 * BANK, T2)

@@ -30,6 +30,8 @@ QUADS = P // QUAD
 Z_ROWS = 4
 LIST_ROWS = 16
 N_TILES = N // P
+HALF_P = P // 2
+Z_EARLY = BANK + H
 
 ORDER = (0, 2, 3, 1)
 STEPS = [(0, 0), (1, 0), (2, 0), (0, BANK), (1, BANK), (3, 0), (2, BANK), (3, BANK)]
@@ -42,21 +44,29 @@ CHUNKS = [(0, QUARTER), (QUARTER, QUARTER)] + [(c0, BANK) for c0 in range(BANK, 
 STEPPED = 2
 
 KIB = 1024
-LAP = 64
-AT_TABLE0 = 8 * KIB - LAP
+ALIGN = 256
+AT_PAGE = (0, 56 * KIB, 48 * KIB, 24 * KIB)
+AT_TABLE = (8 * KIB - ALIGN, 56 * KIB - ALIGN)
 AT_WGS_LATE = 8 * KIB
-AT_GATES = 10 * KIB
-AT_W1_RAW = (24 * KIB, 10 * KIB)
-AT_PAGE = (0, 32 * KIB, 40 * KIB, 24 * KIB)
-AT_TABLE1 = 32 * KIB
-AT_V_Z_ROWS = 32 * KIB - LAP
-AT_WGS_TURNED = (48 * KIB, 56 * KIB)
-AT_W1_BF16 = (46 * KIB, 64 * KIB)
-AT_W1_BF16_UPPER = 68 * KIB
-AT_FACTOR = 68 * KIB
-AT_TAB_Z = 72 * KIB
-AT_W4_W = 72 * KIB
-AT_Y = 48 * KIB
+AT_ROWS_LATE = 10 * KIB
+AT_W1_RAW = (24 * KIB, 32 * KIB)
+AT_PICKED_Z = 32 * KIB - ALIGN
+AT_GATES = 32 * KIB
+AT_W4_Z_RAW = 72 * KIB - 2 * ALIGN
+AT_WGS_TURNED = (74 * KIB, 82 * KIB)
+AT_W1_LOWER = (70 * KIB - ALIGN, 90 * KIB)
+AT_W1_UPPER = (92 * KIB, 94 * KIB)
+AT_FACTOR = 94 * KIB
+AT_TAB_Z = 96 * KIB
+AT_W4_W = 96 * KIB
+AT_W1_W = 116 * KIB
+AT_WOVEN = (AT_W1_W + ALIGN, AT_W1_W + ALIGN + 2 * KIB)
+AT_PICKED_LATE = (121 * KIB, 123 * KIB)
+AT_HID_SHARED = 125 * KIB
+AT_W1_Z = 127 * KIB
+AT_HID_LAST = AT_HID_SHARED + ALIGN
+AT_ROUNDED = {2: AT_W1_W - 4 * KIB + ALIGN, 3: AT_PICKED_LATE[0], 4: AT_W1_Z + ALIGN}
+AT_Y = 64 * KIB
 
 
 def tile_list_forked_prefix_page_kernel(
@@ -70,10 +80,10 @@ def tile_list_forked_prefix_page_kernel(
         psum = ctx.enter_context(tc.psum_pool(name="psum", bufs=1))
 
         def held(shape, dtype, name, tag=None):
-            return keep.tile(shape, dtype, name=name, tag=tag or name, align_bytes=64)
+            return keep.tile(shape, dtype, name=name, tag=tag or name, align_bytes=ALIGN)
 
         def placed(shape, dtype, name, at):
-            return arena.tile(shape, dtype, name=name, align_bytes=64, offset=at)
+            return arena.tile(shape, dtype, name=name, align_bytes=ALIGN, offset=at)
 
         def bank(b):
             return psum.tile([P, BANK], F32, name=f"bank{b}")
@@ -81,8 +91,8 @@ def tile_list_forked_prefix_page_kernel(
         def z_partitions(r):
             return slice(r, P, QUAD)
 
-        def z_rows(r, a=0):
-            return slice(Z_ROWS * QUADS * a + r, Z_ROWS * QUADS * (a + 1), Z_ROWS)
+        def z_rows(r):
+            return slice(r, Z_ROWS * QUADS, Z_ROWS)
 
         def half(h):
             return slice(BANK * h, BANK * (h + 1))
@@ -93,41 +103,41 @@ def tile_list_forked_prefix_page_kernel(
         pick = keep.tile([P, S // LIST_ROWS], U16, name="pick")
         slot = keep.tile([P, S // LIST_ROWS], U16, name="slot")
         tab_z = placed([P, T], U8, "tab_z", AT_TAB_Z)
-        w4_z_raw = held([P, H], U8, "w4_z_raw")
-        z_rows_all = held([P, S + H], U8, "z_rows_all")
-        z_all = [held([P, S + H], U8, f"z_all{a}") for a in range(PASSES)]
-        w8_z = z_all[1][:, 0:N]
+        w4_z_raw = placed([P, H], U8, "w4_z_raw", AT_W4_Z_RAW)
+        z_early = held([P, PASSES * Z_EARLY], U8, "z_early")
+        z_late = held([P, PASSES * BANK], U8, "z_late")
+        w8_z = z_early[:, 0:N]
 
-        nc.vector.memset(tab_z[QUAD : 2 * QUAD, :].bitcast(I32), 0)
-        nc.vector.memset(tab_z[2 * QUAD : P, :].bitcast(I32), 0)
-        nc.vector.memset(w4_z_raw[QUAD : 2 * QUAD, :].bitcast(I32), 0)
-        nc.vector.memset(w4_z_raw[2 * QUAD : P, :].bitcast(I32), 0)
+        nc.gpsimd.memset(w4_z_raw[:].bitcast(I32), 0)
+        nc.gpsimd.memset(tab_z[:, 0 : T // 2].bitcast(I32), 0)
+        nc.vector.memset(tab_z[:, T // 2 : T].bitcast(I32), 0)
         identity = held([P, P], F32, "identity")
         make_identity(nc, identity[:])
-        for a in range(PASSES):
-            nc.gpsimd.memset(z_all[a][:].bitcast(I32), 0)
+        nc.gpsimd.memset(z_early[:].bitcast(I32), 0)
+        nc.gpsimd.memset(z_late[:].bitcast(I32), 0)
 
         def load_w1(a):
             raw = placed([P, PACK, H], F32, f"w1_raw{a}", AT_W1_RAW[a])
             nc.sync.dma_start(raw[:], w1[K_PASS * a : K_PASS * (a + 1), :].rearrange("(p j) c -> p j c", j=PACK))
             return raw
 
-        def load_table(a, c0, c1):
-            words = tab_words[a].rearrange("p t i -> p (t i)").bitcast(I32)
-            nc.sync.dma_start(tab_w[a][:, c0:c1].bitcast(I32), words[:, c0:c1])
+        def load_table(a):
+            words = placed([P, T], U32, f"tab_w{a}", AT_TABLE[a])
+            nc.sync.dma_start(words[:].bitcast(I32), tab_words[a].rearrange("p t i -> p (t i)").bitcast(I32))
+            return words
 
+        spread_rows = slice(0, P, PACK)
         nc.sync.dma_start(pick[:], offs)
-        nc.sync.dma_start(tab_z[0:QUAD, :].bitcast(I32), tab_scales.rearrange("a q t -> (a q) t").bitcast(I32))
-        nc.scalar.dma_start(w4_z_raw[0:QUAD, :].bitcast(I32), w4_scales.rearrange("a q c -> (a q) c").bitcast(I32))
         bias = held([P, PACK], F32, "bias")
         nc.scalar.dma_start(bias[:], bg.rearrange("(p t) -> p t", t=PACK))
-        w4_raw = held([P, PASSES, 2 * H], U8, "w4_raw")
         nc.sync.dma_start(slot[:], offs2)
         wgs_raw = [held([P, BANK], F32, "wgs_raw0")]
         nc.sync.dma_start(wgs_raw[0][:], wgs[:, half(0)])
-        tab_w = [placed([P, T], U32, "tab_w0", AT_TABLE0)]
-        load_table(0, 0, T)
+        nc.sync.dma_start(tab_z[spread_rows, :].bitcast(I32), tab_scales.rearrange("a q t -> (a q) t").bitcast(I32))
+        nc.scalar.dma_start(w4_z_raw[spread_rows, :].bitcast(I32), w4_scales.rearrange("a q c -> (a q) c").bitcast(I32))
+        w4_raw = held([P, PASSES, 2 * H], U8, "w4_raw")
         nc.sync.dma_start(w4_raw[:].bitcast(I32), w4_words.rearrange("a p c -> p a c").bitcast(I32))
+        tab_w = [load_table(0)]
 
         weights = held([P, PACK, S], F32, "weights")
 
@@ -151,22 +161,39 @@ def tile_list_forked_prefix_page_kernel(
 
         spread_wgs(0)
 
-        v_z_rows = placed([P, S], U8, "v_z_rows", AT_V_Z_ROWS)
-        nc.vector.tensor_copy(
-            z_rows_all[:, S : S + H].rearrange("p (t m) -> p t m", t=PACK),
-            w4_z_raw[:].rearrange("p (m t) -> p t m", t=PACK),
-        )
-        nc.vector.tensor_copy(v_z_rows[:], tab_z[:].indirect(pick[:]))
-        nc.vector.tensor_copy(z_rows_all[:, 0:S].bitcast(I32), v_z_rows[:].bitcast(I32))
+        def entries(lst, j0, n):
+            return lst[:, j0 // LIST_ROWS : (j0 + n) // LIST_ROWS]
 
-        def place_scales(a):
+        def join_passes(rows, c0, source):
+            for a in range(PASSES):
+                nc.vector.tensor_copy(
+                    rows[:, a, c0 : c0 + source.shape[1]].bitcast(I32), source[HALF_P * a : HALF_P * (a + 1), :].bitcast(I32)
+                )
+
+        def carry(plane, rows):
             for r in range(Z_ROWS):
-                nc.sync.dma_start(z_all[a][z_partitions(r), :].bitcast(I32), z_rows_all[z_rows(r, a), :].bitcast(I32))
+                nc.sync.dma_start(
+                    plane[z_partitions(r), :].bitcast(I32),
+                    rows[PACK * r : HALF_P : PACK * Z_ROWS].rearrange("p a c -> p (a c)").bitcast(I32),
+                )
 
-        tab_w.append(placed([P, T], U32, "tab_w1", AT_TABLE1))
-        for a in range(PASSES):
-            load_table(1, a * T // PASSES, (a + 1) * T // PASSES)
-            place_scales(a)
+        w4_z = held([P, H], U8, "w4_z")
+        nc.vector.tensor_copy(
+            w4_z[:].rearrange("p (t m) -> p t m", t=PACK), w4_z_raw[:].rearrange("p (m t) -> p t m", t=PACK)
+        )
+        tab_w.append(load_table(1))
+        rows_early = held([HALF_P, PASSES, Z_EARLY], U8, "rows_early")
+        join_passes(rows_early, BANK, w4_z)
+        picked_z = [placed([P, BANK], U8, "picked_z0", AT_PICKED_Z), held([P, BANK], U8, "picked_z1")]
+        nc.vector.tensor_copy(picked_z[0][:], tab_z[:].indirect(entries(pick, 0, BANK)))
+        join_passes(rows_early, 0, picked_z[0])
+        carry(z_early, rows_early)
+        nc.vector.tensor_copy(picked_z[1][:], tab_z[:].indirect(entries(pick, BANK, BANK)))
+
+        def picked_scales(a, j0, n):
+            if j0 < BANK:
+                return z_early[:, Z_EARLY * a + j0 : Z_EARLY * a + j0 + n]
+            return z_late[:, BANK * a + j0 - BANK : BANK * a + j0 - BANK + n]
 
         w4_w = placed([P, PASSES, 2 * H], U8, "w4_w", AT_W4_W)
         nc.vector.tensor_copy(
@@ -174,10 +201,10 @@ def tile_list_forked_prefix_page_kernel(
             w4_raw[:].bitcast(U16).rearrange("p a (m t) -> p a t m", t=PACK),
         )
 
-        v_w = [[held([P, BANK], U32, f"v_w{a}_{h}") for h in range(HALVES)] for a in range(PASSES)]
-
-        def entries(lst, j0, n):
-            return lst[:, j0 // LIST_ROWS : (j0 + n) // LIST_ROWS]
+        v_w = [
+            [held([P, BANK], U32, f"v_w{a}_0"), placed([P, BANK], U32, f"v_w{a}_1", AT_PICKED_LATE[a])]
+            for a in range(PASSES)
+        ]
 
         def picked_words(a, j0, n):
             return v_w[a][j0 // BANK][:, j0 % BANK : j0 % BANK + n]
@@ -199,12 +226,15 @@ def tile_list_forked_prefix_page_kernel(
         page = [load_page(0)]
         wgs_raw.append(placed([P, BANK], F32, "wgs_raw1", AT_WGS_LATE))
         nc.sync.dma_start(wgs_raw[1][:], wgs[:, half(1)])
+        rows_late = placed([HALF_P, PASSES, BANK], U8, "rows_late", AT_ROWS_LATE)
+        join_passes(rows_late, 0, picked_z[1])
+        carry(z_late, rows_late)
         gather_words(1, 0, QUARTER)
         gather_words(1, QUARTER, QUARTER)
         gather_words(1, BANK, BANK)
 
-        w1_w = held([P, PASSES * H], U32, "w1_w")
-        w1_z = held([P, PASSES * H], U8, "w1_z")
+        w1_w = placed([P, PASSES * H], U32, "w1_w", AT_W1_W)
+        w1_z = placed([P, PASSES * H], U8, "w1_z", AT_W1_Z)
 
         def w1_block(a, t):
             return block(PACK * (t // 2) + 2 * a + t % 2)
@@ -220,7 +250,11 @@ def tile_list_forked_prefix_page_kernel(
             columns = slice(c0, c0 + rounded_rows.shape[1] // PACK)
             nc.vector.quantize_mx(out=w1_w[:, columns].bitcast(FP8X4), scales=w1_z[:, columns], in_=rounded_rows)
 
-        hid = [held([P, BANK], F32, f"hid{s}") for s in range(len(STEPS) - 1)]
+        shared = STEPS.index((0, BANK))
+        hid = [
+            placed([P, BANK], F32, f"hid{s}", AT_HID_SHARED) if s == shared else held([P, BANK], F32, f"hid{s}")
+            for s in range(len(STEPS) - 1)
+        ]
 
         def product(b, j0, n, words, dtype, scales):
             acc = bank(b)
@@ -230,7 +264,7 @@ def tile_list_forked_prefix_page_kernel(
                     lhsT=words(a).bitcast(dtype),
                     lhsT_scale=scales(a),
                     rhs=picked_words(a, j0, n).bitcast(FP8X4),
-                    rhs_scale=z_all[a][:, j0 : j0 + n],
+                    rhs_scale=picked_scales(a, j0, n),
                     start=(a == 0), stop=(a == PASSES - 1),
                 )
             return acc[:, 0:n]
@@ -239,7 +273,7 @@ def tile_list_forked_prefix_page_kernel(
             t = ORDER[i]
             logit = product(
                 b, j0, gate.shape[1], lambda a: w4_w[:, a, 2 * P * t : 2 * P * (t + 1)], FP4X4,
-                lambda a: z_all[a][:, S + P * t : S + P * (t + 1)],
+                lambda a: z_early[:, Z_EARLY * a + BANK + P * t : Z_EARLY * a + BANK + P * (t + 1)],
             )
             nc.scalar.activation(gate, logit, ACT.Sigmoid, bias=row_bias)
 
@@ -250,17 +284,18 @@ def tile_list_forked_prefix_page_kernel(
         first = held([P, BANK], F32, "first")
         gate_of(0, 0, 0, first[:, 0:QUARTER], bias[:, ORDER[0] : ORDER[0] + 1])
         gate_of(4, 0, QUARTER, first[:, QUARTER:BANK], bias[:, ORDER[0] : ORDER[0] + 1])
-        lower = [placed([P, 2 * K_PASS], BF16, f"w1_lower{a}", AT_W1_BF16[a]) for a in range(PASSES)]
-        upper = placed([P, PASSES, 2 * K_PASS], BF16, "w1_upper", AT_W1_BF16_UPPER)
+        lower = [placed([P, 2 * K_PASS], BF16, f"w1_lower{a}", AT_W1_LOWER[a]) for a in range(PASSES)]
+        upper = [placed([P, 2 * K_PASS], BF16, f"w1_upper{a}", AT_W1_UPPER[a]) for a in range(PASSES)]
         round_w1(nc.vector.tensor_copy, lower[0][:], 0, 0)
-        round_w1(nc.scalar.copy, upper[:, 0, :], 0, 2)
+        round_w1(nc.scalar.copy, upper[0][:], 0, 2)
         nc.vector.tensor_tensor(first[:], first[:], weights[:, 0, 0:BANK], MULT)
         quantise_w1(lower[0][:], 0, 0)
+        quantise_w1(upper[0][:], 0, 2)
         round_w1(nc.vector.tensor_copy, lower[1][:], 1, 0)
-        round_w1(nc.scalar.copy, upper[:, 1, :], 1, 2)
+        round_w1(nc.scalar.copy, upper[1][:], 1, 2)
         quantise_w1(lower[1][:, 0:K_PASS], 1, 0)
         quantise_w1(lower[1][:, K_PASS : 2 * K_PASS], 1, 1)
-        quantise_w1(upper[:].rearrange("p a c -> p (a c)"), 0, 2)
+        quantise_w1(upper[1][:], 1, 2)
         page.extend(load_page(i) for i in range(1, PACK))
 
         nc.vector.tensor_tensor(hid[0][:, 0:QUARTER], value_of(1, 0, 0, QUARTER), first[:, 0:QUARTER], MULT)
@@ -288,8 +323,8 @@ def tile_list_forked_prefix_page_kernel(
         w8_w = held([P, N], U32, "w8_w", "v_w0_0")
         nc.sync.dma_start(w8_w[:].bitcast(I32), w8_words[0].rearrange("p c i -> p (c i)").bitcast(I32))
         for r in range(Z_ROWS):
-            nc.sync.dma_start(z_all[1][z_partitions(r), 0:N].bitcast(I32), w8_scales[0, z_rows(r), :].bitcast(I32))
-        gains = held([P, N_TILES], F32, "gains", "v_w0_1")
+            nc.sync.dma_start(z_early[z_partitions(r), 0:N].bitcast(I32), w8_scales[0, z_rows(r), :].bitcast(I32))
+        gains = held([P, N_TILES], F32, "gains", "v_w1_0")
         with nc.allow_non_contiguous_dma(reason="one gain value a partition and output tile"):
             nc.sync.dma_start(gains[:], gain.rearrange("(i p) -> p i", p=P))
 
@@ -297,9 +332,10 @@ def tile_list_forked_prefix_page_kernel(
             i, j0 = STEPS[s]
             nc.vector.tensor_copy(page[i][:].indirect(entries(slot, j0 + c0, n)), hid[s][:, c0 : c0 + n])
 
-        page_g = [held([P, PACK * w], BF16, f"page_g{c0}") for c0, w in CHUNKS]
+        page_g = [placed([P, PACK * w], BF16, f"page_g{c0}", at) for (c0, w), at in zip(CHUNKS, AT_WOVEN)]
+        page_g.extend(held([P, PACK * w], BF16, f"page_g{c0}") for c0, w in CHUNKS[STEPPED:])
         page_out = out_1.rearrange("(p t) c -> p t c", t=PACK)
-        page_b = {c: held([P, PACK, CHUNKS[c][1]], BF16, f"page_b{c}") for c in range(STEPPED, len(CHUNKS))}
+        page_b = {c: placed([P, PACK, CHUNKS[c][1]], BF16, f"page_b{c}", at) for c, at in AT_ROUNDED.items()}
 
         def woven(c, i):
             return page_g[c][:].rearrange("p (m t) -> p m t", t=PACK)[:, :, ORDER[i]]
@@ -319,7 +355,7 @@ def tile_list_forked_prefix_page_kernel(
             if j0:
                 finish(i)
             if j0 and i == 0:
-                hid.append(held([P, BANK], F32, "hid_last", f"hid{s}"))
+                hid.append(placed([P, BANK], F32, "hid_last", AT_HID_LAST))
                 gated(len(STEPS) - 1, gate, sums)
 
         page_w = held([P, T2], U32, "page_w")

@@ -385,28 +385,25 @@ def tile_list_forked_prefix_page_kernel(
         y = placed([P, N_TILES, T2], F32, "y", AT_Y)
         turns = list(range(N_TILES * len(CHUNKS)))
 
-        def multiply(n, chunks, on_scalar):
-            for c in chunks:
-                c0, w = CHUNKS[c]
-                acc = bank(turns.pop(0) % BANKS)
+        def multiply(n, c0, c1, on_scalar):
+            for b0 in range(c0 - c0 % BANK, c1, BANK):
+                cols = slice(max(b0, c0), min(b0 + BANK, c1))
+                acc = bank(turns.pop(0) % BANKS)[:, 0 : cols.stop - cols.start]
                 nc.tensor.matmul_mx(
-                    out=acc[:, 0:w],
+                    out=acc,
                     lhsT=w8_w[:, block(n)].bitcast(FP8X4),
                     lhsT_scale=w8_z[:, block(n)],
-                    rhs=page_w[:, c0 : c0 + w].bitcast(FP8X4),
-                    rhs_scale=page_z[:, c0 : c0 + w],
+                    rhs=page_w[:, cols].bitcast(FP8X4),
+                    rhs_scale=page_z[:, cols],
                     start=True, stop=True,
                 )
                 if on_scalar:
-                    nc.scalar.activation(y[:, n, c0 : c0 + w], acc[:, 0:w], ACT.Copy, scale=gains[:, n : n + 1])
+                    nc.scalar.activation(y[:, n, cols], acc, ACT.Copy, scale=gains[:, n : n + 1])
                 else:
-                    nc.vector.tensor_scalar(y[:, n, c0 : c0 + w], acc[:, 0:w], gains[:, n : n + 1], None, MULT)
+                    nc.vector.tensor_scalar(y[:, n, cols], acc, gains[:, n : n + 1], None, MULT)
 
         def store_rows(n0, n1, c0, c1):
             nc.sync.dma_start(y_rows[:, n0:n1, c0:c1], y[:, n0:n1, c0:c1])
-
-        def store_chunk_codes(c):
-            store_codes(CHUNKS[c][0], sum(CHUNKS[c]))
 
         for c in range(len(CHUNKS)):
             if c < STEPPED:
@@ -414,26 +411,18 @@ def tile_list_forked_prefix_page_kernel(
             else:
                 weave(c)
             quantise(c)
-        store_chunk_codes(0)
-        for n in range(2):
-            multiply(n, [0], True)
-        store_rows(0, 2, 0, QUARTER)
-        store_chunk_codes(1)
-        for n in range(2, N_TILES):
-            multiply(n, [0, 1], True)
-            store_rows(n, n + 1, 0, BANK)
-        store_chunk_codes(2)
-        for n in range(2):
-            multiply(n, [1, 2], True)
-            store_rows(n, n + 1, QUARTER, 2 * BANK)
-        store_codes(2 * BANK, T2)
-        for n0 in range(2, N_TILES, 2):
-            for n in (n0, n0 + 1):
-                multiply(n, [2], True)
-            store_rows(n0, n0 + 2, BANK, 2 * BANK)
+        cuts = (QUARTER, QUARTER, BANK, BANK, 2 * BANK, 2 * BANK)
+        store_codes(0, BANK)
+        for n in range(N_TILES):
+            multiply(n, 0, cuts[n], True)
+            if n:
+                store_rows(n if n > 1 else 0, n + 1, 0, cuts[n])
+            if n == 3:
+                store_codes(BANK, 2 * BANK)
+        store_codes(2 * BANK, 3 * BANK)
+        store_codes(3 * BANK, T2)
         for r in range(Z_ROWS):
             nc.sync.dma_start(out_3[0, z_rows(r), :].bitcast(I32), page_z[z_partitions(r), :].bitcast(I32))
-        for n0 in range(0, N_TILES, 2):
-            for n in (n0, n0 + 1):
-                multiply(n, [3, 4], n >= 4)
-            store_rows(n0, n0 + 2, 2 * BANK, T2)
+        for n in range(N_TILES):
+            multiply(n, cuts[n], T2, n % 2 == 0)
+            store_rows(n, n + 1, cuts[n], T2)

@@ -411,18 +411,25 @@ def tile_list_forked_prefix_page_kernel(
             else:
                 weave(c)
             quantise(c)
-        cuts = (QUARTER, QUARTER, BANK, BANK, 2 * BANK, 2 * BANK)
-        store_codes(0, BANK)
-        for n in range(N_TILES):
-            multiply(n, 0, cuts[n], True)
-            if n:
-                store_rows(n if n > 1 else 0, n + 1, 0, cuts[n])
-            if n == 3:
-                store_codes(BANK, 2 * BANK)
-        store_codes(2 * BANK, 3 * BANK)
-        store_codes(3 * BANK, T2)
+        store_codes(0, QUARTER)
+        for n in range(2):
+            multiply(n, 0, QUARTER, True)
+        store_rows(0, 2, 0, QUARTER)
+        store_codes(QUARTER, BANK)
+        for n in range(2, N_TILES):
+            multiply(n, 0, BANK, True)
+            store_rows(n, n + 1, 0, BANK)
+        store_codes(BANK, 2 * BANK)
+        for n in range(2):
+            multiply(n, QUARTER, 2 * BANK, True)
+            store_rows(n, n + 1, QUARTER, 2 * BANK)
+        store_codes(2 * BANK, T2)
         for r in range(Z_ROWS):
             nc.sync.dma_start(out_3[0, z_rows(r), :].bitcast(I32), page_z[z_partitions(r), :].bitcast(I32))
-        for n in range(N_TILES):
-            multiply(n, cuts[n], T2, n % 2 == 0)
-            store_rows(n, n + 1, cuts[n], T2)
+        for n in range(2, N_TILES):
+            multiply(n, BANK, 2 * BANK, True)
+            multiply(n, 2 * BANK, T2, False)
+            store_rows(n, n + 1, BANK, T2)
+        for n in range(2):
+            multiply(n, 2 * BANK, T2, True)
+        store_rows(0, 2, 2 * BANK, T2)

@@ -411,25 +411,29 @@ def tile_list_forked_prefix_page_kernel(
             else:
                 weave(c)
             quantise(c)
-        store_codes(0, QUARTER)
+        store_codes(0, BANK)
         for n in range(2):
             multiply(n, 0, QUARTER, True)
         store_rows(0, 2, 0, QUARTER)
-        store_codes(QUARTER, BANK)
         for n in range(2, N_TILES):
             multiply(n, 0, BANK, True)
             store_rows(n, n + 1, 0, BANK)
+        for n in range(2):
+            multiply(n, QUARTER, BANK, True)
+        store_rows(0, 2, QUARTER, BANK)
         store_codes(BANK, 2 * BANK)
         for n in range(2):
-            multiply(n, QUARTER, 2 * BANK, True)
-            store_rows(n, n + 1, QUARTER, 2 * BANK)
+            multiply(n, BANK, 2 * BANK, True)
+        store_rows(0, 2, BANK, 2 * BANK)
         store_codes(2 * BANK, T2)
+        for n0 in (2, 4):
+            for n in (n0, n0 + 1):
+                multiply(n, BANK, 2 * BANK, True)
+            store_rows(n0, n0 + 2, BANK, 2 * BANK)
         for r in range(Z_ROWS):
             nc.sync.dma_start(out_3[0, z_rows(r), :].bitcast(I32), page_z[z_partitions(r), :].bitcast(I32))
-        for n in range(2, N_TILES):
-            multiply(n, BANK, 2 * BANK, True)
-            multiply(n, 2 * BANK, T2, False)
-            store_rows(n, n + 1, BANK, T2)
-        for n in range(2):
-            multiply(n, 2 * BANK, T2, True)
-        store_rows(0, 2, 2 * BANK, T2)
+        for n in range(N_TILES):
+            multiply(n, 2 * BANK, T2, n >= 4)
+            if n == 1:
+                store_rows(0, 2, 2 * BANK, T2)
+        store_rows(2, N_TILES, 2 * BANK, T2)

@@ -127,16 +127,16 @@ def tile_list_forked_prefix_page_kernel(
             return words
 
         spread_rows = slice(0, P, PACK)
+        wgs_raw = [held([P, BANK], F32, "wgs_raw0")]
+        nc.sync.dma_start(wgs_raw[0][:], wgs[:, half(0)])
         nc.sync.dma_start(pick[:], offs)
         bias = held([P, PACK], F32, "bias")
         nc.scalar.dma_start(bias[:], bg.rearrange("(p t) -> p t", t=PACK))
-        nc.sync.dma_start(slot[:], offs2)
-        wgs_raw = [held([P, BANK], F32, "wgs_raw0")]
-        nc.sync.dma_start(wgs_raw[0][:], wgs[:, half(0)])
-        nc.sync.dma_start(tab_z[spread_rows, :].bitcast(I32), tab_scales.rearrange("a q t -> (a q) t").bitcast(I32))
-        nc.scalar.dma_start(w4_z_raw[spread_rows, :].bitcast(I32), w4_scales.rearrange("a q c -> (a q) c").bitcast(I32))
         w4_raw = held([P, PASSES, 2 * H], U8, "w4_raw")
         nc.sync.dma_start(w4_raw[:].bitcast(I32), w4_words.rearrange("a p c -> p a c").bitcast(I32))
+        nc.sync.dma_start(slot[:], offs2)
+        nc.sync.dma_start(tab_z[spread_rows, :].bitcast(I32), tab_scales.rearrange("a q t -> (a q) t").bitcast(I32))
+        nc.scalar.dma_start(w4_z_raw[spread_rows, :].bitcast(I32), w4_scales.rearrange("a q c -> (a q) c").bitcast(I32))
         tab_w = [load_table(0)]
 
         weights = held([P, PACK, S], F32, "weights")
@@ -411,29 +411,29 @@ def tile_list_forked_prefix_page_kernel(
             else:
                 weave(c)
             quantise(c)
-        store_codes(0, BANK)
+        store_codes(0, QUARTER)
         for n in range(2):
             multiply(n, 0, QUARTER, True)
         store_rows(0, 2, 0, QUARTER)
-        for n in range(2, N_TILES):
+        store_codes(QUARTER, BANK)
+        multiply(2, 0, QUARTER, True)
+        multiply(2, QUARTER, BANK, True)
+        store_rows(2, 3, 0, BANK)
+        for n in range(3, N_TILES):
             multiply(n, 0, BANK, True)
             store_rows(n, n + 1, 0, BANK)
-        for n in range(2):
-            multiply(n, QUARTER, BANK, True)
-        store_rows(0, 2, QUARTER, BANK)
         store_codes(BANK, 2 * BANK)
         for n in range(2):
-            multiply(n, BANK, 2 * BANK, True)
-        store_rows(0, 2, BANK, 2 * BANK)
+            multiply(n, QUARTER, 2 * BANK, True)
+            store_rows(n, n + 1, QUARTER, 2 * BANK)
         store_codes(2 * BANK, T2)
-        for n0 in (2, 4):
+        for n0 in range(2, N_TILES, 2):
             for n in (n0, n0 + 1):
                 multiply(n, BANK, 2 * BANK, True)
             store_rows(n0, n0 + 2, BANK, 2 * BANK)
         for r in range(Z_ROWS):
             nc.sync.dma_start(out_3[0, z_rows(r), :].bitcast(I32), page_z[z_partitions(r), :].bitcast(I32))
-        for n in range(N_TILES):
-            multiply(n, 2 * BANK, T2, n >= 4)
-            if n == 1:
-                store_rows(0, 2, 2 * BANK, T2)
-        store_rows(2, N_TILES, 2 * BANK, T2)
+        for n0 in range(0, N_TILES, 2):
+            for n in (n0, n0 + 1):
+                multiply(n, 2 * BANK, T2, n >= 4)
+            store_rows(n0, n0 + 2, 2 * BANK, T2)

from contextlib import ExitStack

import concourse.mybir as mybir
from concourse.masks import make_identity

K, H, N, T, S, T2 = 1024, 512, 768, 4096, 1024, 2048
FLOPS = 2 * (2 * K * H * S + H * N * T2)

F32 = mybir.dt.float32
BF16 = mybir.dt.bfloat16
I32 = mybir.dt.int32
U32 = mybir.dt.uint32
U16 = mybir.dt.uint16
U8 = mybir.dt.uint8
FP8X4 = mybir.dt.float8_e4m3fn_x4
FP4X4 = mybir.dt.float4_e2m1fn_x4
ACT = mybir.ActivationFunctionType
MULT = mybir.AluOpType.mult

P = 128
PACK = 4
K_PASS = P * PACK
PASSES = K // K_PASS
BANK = 512
BANKS = 8
HALVES = S // BANK
QUARTER = BANK // 2
QUAD = 32
QUADS = P // QUAD
Z_ROWS = 4
LIST_ROWS = 16
N_TILES = N // P
HALF_P = P // 2
Z_EARLY = BANK + H

ORDER = (0, 2, 3, 1)
STEPS = [(0, 0), (1, 0), (2, 0), (0, BANK), (1, BANK), (3, 0), (2, BANK), (3, BANK)]

LOGIT_BANKS = (0, 3, 0, 0, 3, 2, 4, 6)
VALUE_BANKS = (1, 3, 2, 0, 3, 5, 7, 1)
SPREAD_BANKS = ((1, 2, 3, 4), (4, 5, 6, 7))

CHUNKS = [(0, QUARTER), (QUARTER, QUARTER)] + [(c0, BANK) for c0 in range(BANK, T2, BANK)]
STEPPED = 2

KIB = 1024
ALIGN = 256
AT_PAGE = (0, 56 * KIB, 48 * KIB, 24 * KIB)
AT_TABLE = (8 * KIB - ALIGN, 56 * KIB - ALIGN)
AT_WGS_LATE = 8 * KIB
AT_ROWS_LATE = 10 * KIB
AT_W1_RAW = (24 * KIB, 32 * KIB)
AT_PICKED_Z = 32 * KIB - ALIGN
AT_GATES = 32 * KIB
AT_W4_Z_RAW = 72 * KIB - 2 * ALIGN
AT_WGS_TURNED = (74 * KIB, 82 * KIB)
AT_W1_LOWER = (70 * KIB - ALIGN, 90 * KIB)
AT_W1_UPPER = (92 * KIB, 94 * KIB)
AT_FACTOR = 94 * KIB
AT_TAB_Z = 96 * KIB
AT_W4_W = 96 * KIB
AT_W1_W = 116 * KIB
AT_WOVEN = (AT_W1_W + ALIGN, AT_W1_W + ALIGN + 2 * KIB)
AT_PICKED_LATE = (121 * KIB, 123 * KIB)
AT_HID_SHARED = 125 * KIB
AT_W1_Z = 127 * KIB
AT_HID_LAST = AT_HID_SHARED + ALIGN
AT_ROUNDED = {2: AT_W1_W - 4 * KIB + ALIGN, 3: AT_PICKED_LATE[0], 4: AT_W1_Z + ALIGN}
AT_Y = 64 * KIB


def tile_list_forked_prefix_page_kernel(
    tc, tab_words, tab_scales, offs, offs2, w1, w4_words, w4_scales, bg,
    page0, wgs, w8_words, w8_scales, gain, out_0, out_1, out_2, out_3,
):
    nc = tc.nc
    with ExitStack() as ctx:
        keep = ctx.enter_context(tc.tile_pool(name="keep", bufs=1))
        arena = ctx.enter_context(tc.tile_pool(name="arena", bufs=1))
        psum = ctx.enter_context(tc.psum_pool(name="psum", bufs=1))

        def held(shape, dtype, name, tag=None):
            return keep.tile(shape, dtype, name=name, tag=tag or name, align_bytes=ALIGN)

        def placed(shape, dtype, name, at):
            return arena.tile(shape, dtype, name=name, align_bytes=ALIGN, offset=at)

        def bank(b):
            return psum.tile([P, BANK], F32, name=f"bank{b}")

        def z_partitions(r):
            return slice(r, P, QUAD)

        def z_rows(r):
            return slice(r, Z_ROWS * QUADS, Z_ROWS)

        def half(h):
            return slice(BANK * h, BANK * (h + 1))

        def block(b):
            return slice(P * b, P * (b + 1))

        pick = keep.tile([P, S // LIST_ROWS], U16, name="pick")
        slot = keep.tile([P, S // LIST_ROWS], U16, name="slot")
        tab_z = placed([P, T], U8, "tab_z", AT_TAB_Z)
        w4_z_raw = placed([P, H], U8, "w4_z_raw", AT_W4_Z_RAW)
        z_early = held([P, PASSES * Z_EARLY], U8, "z_early")
        z_late = held([P, PASSES * BANK], U8, "z_late")
        w8_z = z_early[:, 0:N]

        nc.gpsimd.memset(w4_z_raw[:].bitcast(I32), 0)
        nc.gpsimd.memset(tab_z[:, 0 : T // 2].bitcast(I32), 0)
        nc.vector.memset(tab_z[:, T // 2 : T].bitcast(I32), 0)
        identity = held([P, P], F32, "identity")
        make_identity(nc, identity[:])
        nc.gpsimd.memset(z_early[:].bitcast(I32), 0)
        nc.gpsimd.memset(z_late[:].bitcast(I32), 0)

        def load_w1(a):
            raw = placed([P, PACK, H], F32, f"w1_raw{a}", AT_W1_RAW[a])
            nc.sync.dma_start(raw[:], w1[K_PASS * a : K_PASS * (a + 1), :].rearrange("(p j) c -> p j c", j=PACK))
            return raw

        def load_table(a):
            words = placed([P, T], U32, f"tab_w{a}", AT_TABLE[a])
            nc.sync.dma_start(words[:].bitcast(I32), tab_words[a].rearrange("p t i -> p (t i)").bitcast(I32))
            return words

        spread_rows = slice(0, P, PACK)
        wgs_raw = [held([P, BANK], F32, "wgs_raw0")]
        nc.sync.dma_start(wgs_raw[0][:], wgs[:, half(0)])
        nc.sync.dma_start(pick[:], offs)
        bias = held([P, PACK], F32, "bias")
        nc.scalar.dma_start(bias[:], bg.rearrange("(p t) -> p t", t=PACK))
        w4_raw = held([P, PASSES, 2 * H], U8, "w4_raw")
        nc.sync.dma_start(w4_raw[:].bitcast(I32), w4_words.rearrange("a p c -> p a c").bitcast(I32))
        nc.sync.dma_start(slot[:], offs2)
        nc.sync.dma_start(tab_z[spread_rows, :].bitcast(I32), tab_scales.rearrange("a q t -> (a q) t").bitcast(I32))
        nc.scalar.dma_start(w4_z_raw[spread_rows, :].bitcast(I32), w4_scales.rearrange("a q c -> (a q) c").bitcast(I32))
        tab_w = [load_table(0)]

        weights = held([P, PACK, S], F32, "weights")

        def spread_wgs(h):
            turned = bank(h)
            for b in range(PACK):
                nc.tensor.transpose(turned[:, block(b)], wgs_raw[h][:, block(b)], identity[:])
            spread = placed([P, PACK, PACK, QUADS, QUAD], F32, f"wgs_spread{h}", AT_WGS_TURNED[h])
            rows = turned[:].rearrange("j (b m t) -> j b m t", b=PACK, t=PACK)
            nc.scalar.copy(
                spread[:].rearrange("j b t q m -> j b q m t"),
                rows.unsqueeze(2).broadcast_to([P, PACK, QUADS, QUAD, PACK]),
            )
            for i in range(PACK):
                back = bank(SPREAD_BANKS[h][i])
                for b in range(PACK):
                    nc.tensor.transpose(
                        back[:, block(b)], spread[:, b, ORDER[i]].rearrange("j q m -> j (q m)"), identity[:]
                    )
                nc.scalar.copy(weights[:, i, half(h)], back[:])

        spread_wgs(0)

        def entries(lst, j0, n):
            return lst[:, j0 // LIST_ROWS : (j0 + n) // LIST_ROWS]

        def join_passes(rows, c0, source):
            for a in range(PASSES):
                nc.vector.tensor_copy(
                    rows[:, a, c0 : c0 + source.shape[1]].bitcast(I32), source[HALF_P * a : HALF_P * (a + 1), :].bitcast(I32)
                )

        def carry(plane, rows):
            for r in range(Z_ROWS):
                nc.sync.dma_start(
                    plane[z_partitions(r), :].bitcast(I32),
                    rows[PACK * r : HALF_P : PACK * Z_ROWS].rearrange("p a c -> p (a c)").bitcast(I32),
                )

        w4_z = held([P, H], U8, "w4_z")
        nc.vector.tensor_copy(
            w4_z[:].rearrange("p (t m) -> p t m", t=PACK), w4_z_raw[:].rearrange("p (m t) -> p t m", t=PACK)
        )
        tab_w.append(load_table(1))
        rows_early = held([HALF_P, PASSES, Z_EARLY], U8, "rows_early")
        join_passes(rows_early, BANK, w4_z)
        picked_z = [placed([P, BANK], U8, "picked_z0", AT_PICKED_Z), held([P, BANK], U8, "picked_z1")]
        nc.vector.tensor_copy(picked_z[0][:], tab_z[:].indirect(entries(pick, 0, BANK)))
        join_passes(rows_early, 0, picked_z[0])
        carry(z_early, rows_early)
        nc.vector.tensor_copy(picked_z[1][:], tab_z[:].indirect(entries(pick, BANK, BANK)))

        def picked_scales(a, j0, n):
            if j0 < BANK:
                return z_early[:, Z_EARLY * a + j0 : Z_EARLY * a + j0 + n]
            return z_late[:, BANK * a + j0 - BANK : BANK * a + j0 - BANK + n]

        w4_w = placed([P, PASSES, 2 * H], U8, "w4_w", AT_W4_W)
        nc.vector.tensor_copy(
            w4_w[:].bitcast(U16).rearrange("p a (t m) -> p a t m", t=PACK),
            w4_raw[:].bitcast(U16).rearrange("p a (m t) -> p a t m", t=PACK),
        )

        v_w = [
            [held([P, BANK], U32, f"v_w{a}_0"), placed([P, BANK], U32, f"v_w{a}_1", AT_PICKED_LATE[a])]
            for a in range(PASSES)
        ]

        def picked_words(a, j0, n):
            return v_w[a][j0 // BANK][:, j0 % BANK : j0 % BANK + n]

        def gather_words(a, j0, n):
            nc.vector.tensor_copy(picked_words(a, j0, n), tab_w[a][:].indirect(entries(pick, j0, n)))

        for h in range(HALVES):
            gather_words(0, BANK * h, BANK)

        page_rows = page0.rearrange("(p t) c -> p t c", t=PACK)

        def load_page(i):
            rows = placed([P, T2], F32, f"page{i}", AT_PAGE[i])
            nc.sync.dma_start(rows[:], page_rows[:, ORDER[i], :])
            return rows

        w1_raw = [load_w1(a) for a in range(PASSES)]
        page = [load_page(0)]
        wgs_raw.append(placed([P, BANK], F32, "wgs_raw1", AT_WGS_LATE))
        nc.sync.dma_start(wgs_raw[1][:], wgs[:, half(1)])
        rows_late = placed([HALF_P, PASSES, BANK], U8, "rows_late", AT_ROWS_LATE)
        join_passes(rows_late, 0, picked_z[1])
        carry(z_late, rows_late)
        gather_words(1, 0, QUARTER)
        gather_words(1, QUARTER, QUARTER)
        gather_words(1, BANK, BANK)

        w1_w = placed([P, PASSES * H], U32, "w1_w", AT_W1_W)
        w1_z = placed([P, PASSES * H], U8, "w1_z", AT_W1_Z)

        def w1_block(a, t):
            return block(PACK * (t // 2) + 2 * a + t % 2)

        def round_w1(copy, rounded_pair, a, t0):
            copy(
                rounded_pair.rearrange("p (t m j) -> p m j t", t=2, j=PACK),
                w1_raw[a][:].rearrange("p j (m t) -> p m j t", t=PACK)[:, :, :, t0 : t0 + 2],
            )

        def quantise_w1(rounded_rows, a, t0):
            c0 = w1_block(a, t0).start
            columns = slice(c0, c0 + rounded_rows.shape[1] // PACK)
            nc.vector.quantize_mx(out=w1_w[:, columns].bitcast(FP8X4), scales=w1_z[:, columns], in_=rounded_rows)

        shared = STEPS.index((0, BANK))
        hid = [
            placed([P, BANK], F32, f"hid{s}", AT_HID_SHARED) if s == shared else held([P, BANK], F32, f"hid{s}")
            for s in range(len(STEPS) - 1)
        ]

        def product(b, j0, n, words, dtype, scales):
            acc = bank(b)
            for a in range(PASSES):
                nc.tensor.matmul_mx(
                    out=acc[:, 0:n],
                    lhsT=words(a).bitcast(dtype),
                    lhsT_scale=scales(a),
                    rhs=picked_words(a, j0, n).bitcast(FP8X4),
                    rhs_scale=picked_scales(a, j0, n),
                    start=(a == 0), stop=(a == PASSES - 1),
                )
            return acc[:, 0:n]

        def gate_of(b, i, j0, gate, row_bias):
            t = ORDER[i]
            logit = product(
                b, j0, gate.shape[1], lambda a: w4_w[:, a, 2 * P * t : 2 * P * (t + 1)], FP4X4,
                lambda a: z_early[:, Z_EARLY * a + BANK + P * t : Z_EARLY * a + BANK + P * (t + 1)],
            )
            nc.scalar.activation(gate, logit, ACT.Sigmoid, bias=row_bias)

        def value_of(b, i, j0, n):
            t = ORDER[i]
            return product(b, j0, n, lambda a: w1_w[:, w1_block(a, t)], FP8X4, lambda a: w1_z[:, w1_block(a, t)])

        first = held([P, BANK], F32, "first")
        gate_of(0, 0, 0, first[:, 0:QUARTER], bias[:, ORDER[0] : ORDER[0] + 1])
        gate_of(4, 0, QUARTER, first[:, QUARTER:BANK], bias[:, ORDER[0] : ORDER[0] + 1])
        lower = [placed([P, 2 * K_PASS], BF16, f"w1_lower{a}", AT_W1_LOWER[a]) for a in range(PASSES)]
        upper = [placed([P, 2 * K_PASS], BF16, f"w1_upper{a}", AT_W1_UPPER[a]) for a in range(PASSES)]
        round_w1(nc.vector.tensor_copy, lower[0][:], 0, 0)
        round_w1(nc.scalar.copy, upper[0][:], 0, 2)
        nc.vector.tensor_tensor(first[:], first[:], weights[:, 0, 0:BANK], MULT)
        quantise_w1(lower[0][:], 0, 0)
        quantise_w1(upper[0][:], 0, 2)
        round_w1(nc.vector.tensor_copy, lower[1][:], 1, 0)
        round_w1(nc.scalar.copy, upper[1][:], 1, 2)
        quantise_w1(lower[1][:, 0:K_PASS], 1, 0)
        quantise_w1(lower[1][:, K_PASS : 2 * K_PASS], 1, 1)
        quantise_w1(upper[1][:], 1, 2)
        page.extend(load_page(i) for i in range(1, PACK))

        nc.vector.tensor_tensor(hid[0][:, 0:QUARTER], value_of(1, 0, 0, QUARTER), first[:, 0:QUARTER], MULT)
        nc.vector.tensor_tensor(hid[0][:, QUARTER:BANK], value_of(2, 0, QUARTER, QUARTER), first[:, QUARTER:BANK], MULT)

        def gated(s, gate, sums):
            i, j0 = STEPS[s]
            value = hid[s][:]
            factor = placed([P, BANK], F32, f"factor{s}", AT_FACTOR)
            nc.gpsimd.tensor_tensor(factor[:], gate, weights[:, i, j0 : j0 + BANK], MULT)
            nc.scalar.copy(value, sums)
            nc.gpsimd.tensor_tensor(value, value, factor[:], MULT)

        gates = placed([P, len(STEPS) - 1, BANK], F32, "gates", AT_GATES)
        for s in range(1, len(STEPS)):
            i, j0 = STEPS[s]
            if (i, j0) == (0, BANK):
                spread_wgs(1)
            gate = gates[:, s - 1, :]
            gate_of(LOGIT_BANKS[s], i, j0, gate, bias[:, ORDER[i] : ORDER[i] + 1])
            sums = value_of(VALUE_BANKS[s], i, j0, BANK)
            if s < len(STEPS) - 1:
                gated(s, gate, sums)

        w8_w = held([P, N], U32, "w8_w", "v_w0_0")
        nc.sync.dma_start(w8_w[:].bitcast(I32), w8_words[0].rearrange("p c i -> p (c i)").bitcast(I32))
        for r in range(Z_ROWS):
            nc.sync.dma_start(z_early[z_partitions(r), 0:N].bitcast(I32), w8_scales[0, z_rows(r), :].bitcast(I32))
        gains = held([P, N_TILES], F32, "gains", "v_w1_0")
        with nc.allow_non_contiguous_dma(reason="one gain value a partition and output tile"):
            nc.sync.dma_start(gains[:], gain.rearrange("(i p) -> p i", p=P))

        def scatter(s, c0, n):
            i, j0 = STEPS[s]
            nc.vector.tensor_copy(page[i][:].indirect(entries(slot, j0 + c0, n)), hid[s][:, c0 : c0 + n])

        page_g = [placed([P, PACK * w], BF16, f"page_g{c0}", at) for (c0, w), at in zip(CHUNKS, AT_WOVEN)]
        page_g.extend(held([P, PACK * w], BF16, f"page_g{c0}") for c0, w in CHUNKS[STEPPED:])
        page_out = out_1.rearrange("(p t) c -> p t c", t=PACK)
        page_b = {c: placed([P, PACK, CHUNKS[c][1]], BF16, f"page_b{c}", at) for c, at in AT_ROUNDED.items()}

        def woven(c, i):
            return page_g[c][:].rearrange("p (m t) -> p m t", t=PACK)[:, :, ORDER[i]]

        def rounded(c, i):
            return woven(c, i) if c < STEPPED else page_b[c][:, ORDER[i], :]

        def finish(i):
            nc.sync.dma_start(page_out[:, ORDER[i], :], page[i][:])
            for c, (c0, w) in enumerate(CHUNKS):
                if i < PACK - 1 or c >= STEPPED:
                    nc.scalar.copy(rounded(c, i), page[i][:, c0 : c0 + w])

        for s in range(len(STEPS)):
            i, j0 = STEPS[s]
            scatter(s, 0, BANK)
            if j0:
                finish(i)
            if j0 and i == 0:
                hid.append(placed([P, BANK], F32, "hid_last", AT_HID_LAST))
                gated(len(STEPS) - 1, gate, sums)

        page_w = held([P, T2], U32, "page_w")
        page_z = held([P, T2], U8, "page_z")
        y_rows = out_0.rearrange("(i p) c -> p i c", p=P)
        codes_out = out_2[0].rearrange("p m t -> p (m t)").bitcast(I32)

        def round_last(c):
            c0, w = CHUNKS[c]
            nc.vector.tensor_copy(rounded(c, PACK - 1), page[PACK - 1][:, c0 : c0 + w])

        def weave(c):
            nc.vector.tensor_copy(
                page_g[c][:].rearrange("p (c m t) -> p c t m", m=PACK, t=PACK),
                page_b[c][:].rearrange("p t (c m) -> p c t m", m=PACK),
            )

        def quantise(c):
            c0, w = CHUNKS[c]
            nc.vector.quantize_mx(
                out=page_w[:, c0 : c0 + w].bitcast(FP8X4), scales=page_z[:, c0 : c0 + w], in_=page_g[c][:]
            )

        def store_codes(c0, c1):
            nc.sync.dma_start(codes_out[:, c0:c1], page_w[:, c0:c1].bitcast(I32))

        y = placed([P, N_TILES, T2], F32, "y", AT_Y)
        turns = list(range(N_TILES * len(CHUNKS)))

        def multiply(n, c0, c1, on_scalar):
            for b0 in range(c0 - c0 % BANK, c1, BANK):
                cols = slice(max(b0, c0), min(b0 + BANK, c1))
                acc = bank(turns.pop(0) % BANKS)[:, 0 : cols.stop - cols.start]
                nc.tensor.matmul_mx(
                    out=acc,
                    lhsT=w8_w[:, block(n)].bitcast(FP8X4),
                    lhsT_scale=w8_z[:, block(n)],
                    rhs=page_w[:, cols].bitcast(FP8X4),
                    rhs_scale=page_z[:, cols],
                    start=True, stop=True,
                )
                if on_scalar:
                    nc.scalar.activation(y[:, n, cols], acc, ACT.Copy, scale=gains[:, n : n + 1])
                else:
                    nc.vector.tensor_scalar(y[:, n, cols], acc, gains[:, n : n + 1], None, MULT)

        def store_rows(n0, n1, c0, c1):
            nc.sync.dma_start(y_rows[:, n0:n1, c0:c1], y[:, n0:n1, c0:c1])

        for c in range(len(CHUNKS)):
            if c < STEPPED:
                round_last(c)
            else:
                weave(c)
            quantise(c)
        store_codes(0, QUARTER)
        for n in range(2):
            multiply(n, 0, QUARTER, True)
        store_rows(0, 2, 0, QUARTER)
        store_codes(QUARTER, BANK)
        multiply(2, 0, QUARTER, True)
        multiply(2, QUARTER, BANK, True)
        store_rows(2, 3, 0, BANK)
        for n in range(3, N_TILES):
            multiply(n, 0, BANK, True)
            store_rows(n, n + 1, 0, BANK)
        store_codes(BANK, 2 * BANK)
        for n in range(2):
            multiply(n, QUARTER, 2 * BANK, True)
            store_rows(n, n + 1, QUARTER, 2 * BANK)
        store_codes(2 * BANK, T2)
        for n0 in range(2, N_TILES, 2):
            for n in (n0, n0 + 1):
                multiply(n, BANK, 2 * BANK, True)
            store_rows(n0, n0 + 2, BANK, 2 * BANK)
        for r in range(Z_ROWS):
            nc.sync.dma_start(out_3[0, z_rows(r), :].bitcast(I32), page_z[z_partitions(r), :].bitcast(I32))
        for n0 in range(0, N_TILES, 2):
            for n in (n0, n0 + 1):
                multiply(n, 2 * BANK, T2, n >= 4)
            store_rows(n0, n0 + 2, 2 * BANK, T2)
